import numpy as np
import ml_dtypes


def mxq(x, axis, fmt="e4m3"):
    dtype, down = {"e4m3": (ml_dtypes.float8_e4m3fn, 7), "e5m2": (ml_dtypes.float8_e5m2, 14)}[fmt]
    v = np.moveaxis(np.asarray(x, np.float32).astype(ml_dtypes.bfloat16).astype(np.float64), axis, -1)
    blocks = v.reshape(v.shape[:-1] + (-1, 32))
    amax = np.abs(blocks).max(-1, keepdims=True)
    byte = np.maximum(np.where(amax > 0, np.frexp(amax)[1] - 1 + 127, 0) - down, 1)
    scale = np.exp2(byte - 127.0)
    codes = (blocks / scale).astype(np.float32).astype(dtype).astype(np.float64)
    return np.moveaxis((codes * scale).reshape(v.shape), -1, axis)


WIDE = False


def mx_kscale(k):
    if not WIDE:
        return np.ones(k)
    levels = np.array([18, -18])
    if k % 512:
        return np.exp2(np.random.permutation(np.resize(levels, k // 32))).repeat(32)
    a = np.empty((k // 512, 16))
    for p in range(k // 512):
        a[p, :8] = np.random.permutation(np.resize(levels, 8))
        for g in range(8):
            far = levels[np.abs(levels - a[p, g]) >= 10]
            a[p, g + 8] = far[np.random.randint(len(far))]
    return np.exp2(a.ravel()).repeat(32)


def f64(x):
    return np.asarray(x).astype(np.float64)


def striped(idx):
    return np.tile(np.asarray(idx).reshape(-1, 16).T, (8, 1)).astype(np.uint16)


def unstriped(offs):
    return offs[:16].T.reshape(-1).astype(np.int64)


def setup_inputs():
    n = np.random.standard_normal
    uni = np.random.uniform
    idx = np.random.permutation(2048)[:1024]
    bag = np.random.permutation(np.repeat(np.arange(512), 2))
    f_m = mx_kscale(512)
    return {
        "eT": (n((512, 2048)) / np.sqrt(512)).astype(np.float32),
        "W": (n((512, 512)) / np.sqrt(512) * f_m[:, None]).astype(np.float32),
        "dz": (n((512, 512)) / f_m[:, None]).astype(np.float32),
        "wc": np.tile(uni(0.75, 1.3, 1024), (128, 1)).astype(np.float32),
        "offs": striped(idx),
        "bagoffs": striped(bag),
    }


def reference(eT, W, dz, wc, offs, bagoffs):
    idx = unstriped(offs)
    bag = unstriped(bagoffs)
    eT_c = f64(eT)[:, idx]
    u = mxq(f64(W), 0, "e4m3").T @ mxq(f64(dz), 0, "e5m2")
    ub = u[:, bag]
    de = f64(wc)[:1] * ub
    out_0 = np.zeros((512, 2048))
    out_0[:, idx] = de
    ubt = ub.T
    et = eT_c.T
    dw = (ubt * et).sum(-1, keepdims=True)
    out_1 = dw.T
    return out_0, out_1

@@ -1,0 +1,169 @@
+from contextlib import ExitStack
+
+import concourse.mybir as mybir
+from concourse.masks import make_identity
+
+M, D, X, C, T = 512, 512, 512, 1024, 2048
+FLOPS = 2 * M * D * X
+
+F32 = mybir.dt.float32
+BF16 = mybir.dt.bfloat16
+U32 = mybir.dt.uint32
+U16 = mybir.dt.uint16
+U8 = mybir.dt.uint8
+E4M3 = mybir.dt.float8_e4m3fn_x4
+E5M2 = mybir.dt.float8_e5m2_x4
+MULT = mybir.AluOpType.mult
+ADD = mybir.AluOpType.add
+COPY = mybir.ActivationFunctionType.Copy
+
+P = 128
+PACK = 4
+D_TILES = D // P
+BLOCKS = C // P
+U_WINDOW = 1536
+HALF = X // 2
+DZ_VECTOR_SHARE = 168
+LAST_PIECES = (512, 256, 128, 128)
+
+
+def interleave_views(grouped, raw, lo, hi):
+    dst = grouped[:, lo:hi, :].rearrange("p (c i) t -> p c t i", i=PACK)
+    src = raw[:, :, lo:hi].rearrange("p t (c i) -> p c t i", i=PACK)
+    return dst, src
+
+
+def quantize(nc, grouped, codes, scales, fmt):
+    nc.vector.quantize_mx(out=codes.bitcast(fmt), scales=scales, in_=grouped[:].rearrange("p c t -> p (c t)"))
+
+
+def tile_attend_gebag_kernel(tc, eT, W, dz, wc, offs, bagoffs, out_0, out_1):
+    nc = tc.nc
+    with ExitStack() as ctx:
+        keep = ctx.enter_context(tc.tile_pool(name="keep", bufs=1))
+        psum = ctx.enter_context(tc.psum_pool(name="psum", bufs=8))
+
+        W_rows = W.rearrange("(p t) c -> p t c", t=PACK)
+        dz_rows = dz.rearrange("(p t) c -> p t c", t=PACK)
+
+        dz_raw = [keep.tile([P, PACK, HALF], F32, name="dz_raw%d" % h) for h in range(2)]
+        w_raw_first = keep.tile([P, PACK, P], F32)
+        w_raw_rest = keep.tile([P, PACK, D - P], F32)
+        bag_list = keep.tile([P, C // 16], U16)
+        idx_list = keep.tile([P, C // 16], U16)
+        wc_sb = keep.tile([P, C], F32)
+        table = [keep.tile([P, T], F32, name="table%d" % j) for j in range(D_TILES)]
+
+        nc.sync.dma_start(out=dz_raw[0][:], in_=dz_rows[:, :, :HALF])
+        nc.sync.dma_start(out=w_raw_first[:], in_=W_rows[:, :, :P])
+        nc.sync.dma_start(out=dz_raw[1][:], in_=dz_rows[:, :, HALF:])
+        nc.sync.dma_start(bag_list[:], bagoffs)
+        nc.sync.dma_start(out=w_raw_rest[:], in_=W_rows[:, :, P:])
+        nc.sync.dma_start(idx_list[:], offs)
+        nc.sync.dma_start(out=wc_sb[:], in_=wc)
+        for j in range(D_TILES):
+            nc.sync.dma_start(out=table[j][:], in_=eT[j * P : (j + 1) * P, :])
+
+        u_all = keep.tile([P, (D_TILES - 1) * X + U_WINDOW], F32)
+        windows = [keep.tile([P, T], F32, name="window%d" % k) for k in range(2)]
+        nc.vector.memset(u_all[:, D_TILES * X :], 0.0)
+        for window in windows:
+            nc.vector.memset(window[:], 0.0)
+        ident = keep.tile([P, P], F32)
+        make_identity(nc, ident[:])
+        dw_cols = keep.tile([P, P], F32)
+        nc.gpsimd.memset(dw_cols[:], 0.0)
+
+        dz_codes = keep.tile([P, X], U32, align_bytes=64)
+        dz_scales = keep.tile([P, X], U8, align_bytes=64)
+        dz_bf = [keep.tile([P, HALF, PACK], BF16, align_bytes=64, name="dz_bf%d" % h) for h in range(2)]
+        w_codes = [keep.tile([P, P], U32, align_bytes=64, name="w_codes%d" % j) for j in range(D_TILES)]
+        w_scales = [keep.tile([P, P], U8, align_bytes=64, name="w_scales%d" % j) for j in range(D_TILES)]
+        w_bf = [keep.tile([P, P, PACK], BF16, align_bytes=64, name="w_bf%d" % j) for j in range(D_TILES)]
+
+        dst, src = interleave_views(dz_bf[0], dz_raw[0], 0, HALF)
+        nc.vector.tensor_copy(out=dst, in_=src)
+        dst, src = interleave_views(w_bf[0], w_raw_first, 0, P)
+        nc.scalar.activation(out=dst, in_=src, func=COPY)
+        quantize(nc, dz_bf[0], dz_codes[:, :HALF], dz_scales[:, :HALF], E5M2)
+        quantize(nc, w_bf[0], w_codes[0][:], w_scales[0][:], E4M3)
+        dst, src = interleave_views(dz_bf[1], dz_raw[1], 0, DZ_VECTOR_SHARE)
+        nc.vector.tensor_copy(out=dst, in_=src)
+        dst, src = interleave_views(dz_bf[1], dz_raw[1], DZ_VECTOR_SHARE, HALF)
+        nc.scalar.activation(out=dst, in_=src, func=COPY)
+        quantize(nc, dz_bf[1], dz_codes[:, HALF:], dz_scales[:, HALF:], E5M2)
+
+        def u_start(j):
+            return (D_TILES - 1 - j) * X
+
+        def multiply(j):
+            acc = psum.tile([P, X], F32, tag="bank")
+            nc.tensor.matmul_mx(
+                out=acc[:],
+                lhsT=w_codes[j][:].bitcast(E4M3),
+                lhsT_scale=w_scales[j][:],
+                rhs=dz_codes[:].bitcast(E5M2),
+                rhs_scale=dz_scales[:],
+                start=True,
+                stop=True,
+            )
+            nc.scalar.copy(out=u_all[:, u_start(j) : u_start(j) + X], in_=acc[:])
+
+        multiply(0)
+        for j in range(1, D_TILES):
+            dst = w_bf[j][:].rearrange("p (c i) t -> p c t i", i=PACK)
+            src = w_raw_rest[:, :, (j - 1) * P : j * P].rearrange("p t (c i) -> p c t i", i=PACK)
+            nc.scalar.activation(out=dst, in_=src, func=COPY)
+
+        ub = [keep.tile([P, C], F32, name="ub%d" % j) for j in range(D_TILES)]
+        prod = [keep.tile([P, C], F32, name="prod%d" % j) for j in range(D_TILES)]
+        sums = []
+        spent = keep.tile([P, P], F32)
+
+        def gather_u(j):
+            window = u_all[:, u_start(j) : u_start(j) + U_WINDOW]
+            nc.vector.tensor_copy(ub[j][:], window.indirect(bag_list[:]))
+
+        def scatter(j):
+            window = windows[j % 2]
+            nc.vector.tensor_tensor(window[:].indirect(idx_list[:]), ub[j][:], wc_sb[:], MULT)
+            nc.sync.dma_start(out=out_0[j * P : (j + 1) * P, :], in_=window[:])
+
+        def gather_table(j, lo, hi):
+            nc.vector.tensor_tensor(prod[j][:, lo:hi], table[j][:].indirect(idx_list[:, lo // 16 : hi // 16]), ub[j][:, lo:hi], MULT)
+            for b in range(lo // P, hi // P):
+                nc.tensor.matmul(
+                    sums[b][:, :P],
+                    lhsT=prod[j][:, b * P : (b + 1) * P],
+                    rhs=ident[:],
+                    is_transpose=True,
+                    start=(j == 0),
+                    stop=(j == D_TILES - 1),
+                )
+                if j == D_TILES - 1:
+                    if b < BLOCKS - 1:
+                        nc.scalar.activation(out=spent[:], in_=sums[b][:, :P], func=COPY, accum_out=dw_cols[:, b : b + 1])
+                    else:
+                        nc.vector.tensor_reduce(out=dw_cols[:, b : b + 1], in_=sums[b][:, :P], axis=mybir.AxisListType.X, op=ADD)
+
+        gather_u(0)
+        for j in range(1, D_TILES):
+            quantize(nc, w_bf[j], w_codes[j][:], w_scales[j][:], E4M3)
+            multiply(j)
+        for b in range(BLOCKS):
+            sums.append(psum.tile([P, X], F32, tag="bank", name="sums%d" % b))
+        scatter(0)
+        for j in range(1, D_TILES):
+            gather_u(j)
+            gather_table(j - 1, 0, C)
+            scatter(j)
+        lo = 0
+        for width in LAST_PIECES:
+            gather_table(D_TILES - 1, lo, lo + width)
+            lo = lo + width
+
+        turned = psum.tile([P, X], F32, tag="bank")
+        nc.tensor.transpose(turned[:, :P], dw_cols[:], ident[:])
+        dw_rows = keep.tile([BLOCKS, P], F32)
+        nc.scalar.copy(out=dw_rows[:], in_=turned[:BLOCKS, :P])
+        nc.sync.dma_start(out=out_1.rearrange("o (b p) -> (o b) p", p=P), in_=dw_rows[:])

@@ -21,7 +21,7 @@ P = 128
 PACK = 4
 D_TILES = D // P
 BLOCKS = C // P
-U_WINDOW = 1536
+U_WINDOW = 1376
 HALF = X // 2
 DZ_VECTOR_SHARE = 168
 LAST_PIECES = (512, 256, 128, 128)
@@ -47,28 +47,30 @@ def tile_attend_gebag_kernel(tc, eT, W, dz, wc, offs, bagoffs, out_0, out_1):
         dz_rows = dz.rearrange("(p t) c -> p t c", t=PACK)
 
         dz_raw = [keep.tile([P, PACK, HALF], F32, name="dz_raw%d" % h) for h in range(2)]
-        w_raw_first = keep.tile([P, PACK, P], F32)
-        w_raw_rest = keep.tile([P, PACK, D - P], F32)
+        w_raw_0 = keep.tile([P, PACK, P], F32)
+        w_raw_1 = keep.tile([P, PACK, P], F32)
+        w_raw_23 = keep.tile([P, PACK, 2 * P], F32)
+        w_raw = [w_raw_0[:], w_raw_1[:], w_raw_23[:, :, :P], w_raw_23[:, :, P:]]
         bag_list = keep.tile([P, C // 16], U16)
         idx_list = keep.tile([P, C // 16], U16)
-        wc_sb = keep.tile([P, C], F32)
+        wc_sb = keep.tile([P, C], F32, tag="weights_then_product")
         table = [keep.tile([P, T], F32, name="table%d" % j) for j in range(D_TILES)]
 
         nc.sync.dma_start(out=dz_raw[0][:], in_=dz_rows[:, :, :HALF])
-        nc.sync.dma_start(out=w_raw_first[:], in_=W_rows[:, :, :P])
+        nc.sync.dma_start(out=w_raw_0[:], in_=W_rows[:, :, :P])
         nc.sync.dma_start(out=dz_raw[1][:], in_=dz_rows[:, :, HALF:])
+        nc.sync.dma_start(out=w_raw_1[:], in_=W_rows[:, :, P : 2 * P])
         nc.sync.dma_start(bag_list[:], bagoffs)
-        nc.sync.dma_start(out=w_raw_rest[:], in_=W_rows[:, :, P:])
+        nc.sync.dma_start(out=w_raw_23[:], in_=W_rows[:, :, 2 * P :])
         nc.sync.dma_start(idx_list[:], offs)
         nc.sync.dma_start(out=wc_sb[:], in_=wc)
         for j in range(D_TILES):
             nc.sync.dma_start(out=table[j][:], in_=eT[j * P : (j + 1) * P, :])
 
         u_all = keep.tile([P, (D_TILES - 1) * X + U_WINDOW], F32)
-        windows = [keep.tile([P, T], F32, name="window%d" % k) for k in range(2)]
+        window_even = keep.tile([P, T], F32)
         nc.vector.memset(u_all[:, D_TILES * X :], 0.0)
-        for window in windows:
-            nc.vector.memset(window[:], 0.0)
+        nc.vector.memset(window_even[:], 0.0)
         ident = keep.tile([P, P], F32)
         make_identity(nc, ident[:])
         dw_cols = keep.tile([P, P], F32)
@@ -79,11 +81,12 @@ def tile_attend_gebag_kernel(tc, eT, W, dz, wc, offs, bagoffs, out_0, out_1):
         dz_bf = [keep.tile([P, HALF, PACK], BF16, align_bytes=64, name="dz_bf%d" % h) for h in range(2)]
         w_codes = [keep.tile([P, P], U32, align_bytes=64, name="w_codes%d" % j) for j in range(D_TILES)]
         w_scales = [keep.tile([P, P], U8, align_bytes=64, name="w_scales%d" % j) for j in range(D_TILES)]
-        w_bf = [keep.tile([P, P, PACK], BF16, align_bytes=64, name="w_bf%d" % j) for j in range(D_TILES)]
+        w_bf = [keep.tile([P, P, PACK], BF16, align_bytes=64, name="w_bf%d" % j) for j in range(D_TILES - 1)]
+        w_bf.append(keep.tile([P, P, PACK], BF16, align_bytes=64, name="w_bf_last", tag="last_weights_then_window"))
 
         dst, src = interleave_views(dz_bf[0], dz_raw[0], 0, HALF)
         nc.vector.tensor_copy(out=dst, in_=src)
-        dst, src = interleave_views(w_bf[0], w_raw_first, 0, P)
+        dst, src = interleave_views(w_bf[0], w_raw[0], 0, P)
         nc.scalar.activation(out=dst, in_=src, func=COPY)
         quantize(nc, dz_bf[0], dz_codes[:, :HALF], dz_scales[:, :HALF], E5M2)
         quantize(nc, w_bf[0], w_codes[0][:], w_scales[0][:], E4M3)
@@ -107,16 +110,24 @@ def tile_attend_gebag_kernel(tc, eT, W, dz, wc, offs, bagoffs, out_0, out_1):
                 start=True,
                 stop=True,
             )
-            nc.scalar.copy(out=u_all[:, u_start(j) : u_start(j) + X], in_=acc[:])
+            if j == 0:
+                nc.vector.tensor_copy(out=u_all[:, u_start(j) : u_start(j) + X], in_=acc[:])
+            else:
+                nc.scalar.copy(out=u_all[:, u_start(j) : u_start(j) + X], in_=acc[:])
 
-        multiply(0)
-        for j in range(1, D_TILES):
-            dst = w_bf[j][:].rearrange("p (c i) t -> p c t i", i=PACK)
-            src = w_raw_rest[:, :, (j - 1) * P : j * P].rearrange("p t (c i) -> p c t i", i=PACK)
+        def cast_weights(j):
+            dst, src = interleave_views(w_bf[j], w_raw[j], 0, P)
             nc.scalar.activation(out=dst, in_=src, func=COPY)
 
+        cast_weights(1)
+        quantize(nc, w_bf[1], w_codes[1][:], w_scales[1][:], E4M3)
+        multiply(0)
+        multiply(1)
+        cast_weights(2)
+        cast_weights(3)
+
         ub = [keep.tile([P, C], F32, name="ub%d" % j) for j in range(D_TILES)]
-        prod = [keep.tile([P, C], F32, name="prod%d" % j) for j in range(D_TILES)]
+        prod = [keep.tile([P, C], F32, name="prod%d" % j) for j in range(D_TILES - 1)]
         sums = []
         spent = keep.tile([P, P], F32)
 
@@ -141,22 +152,28 @@ def tile_attend_gebag_kernel(tc, eT, W, dz, wc, offs, bagoffs, out_0, out_1):
                     stop=(j == D_TILES - 1),
                 )
                 if j == D_TILES - 1:
-                    if b < BLOCKS - 1:
+                    if b < BLOCKS - 2:
                         nc.scalar.activation(out=spent[:], in_=sums[b][:, :P], func=COPY, accum_out=dw_cols[:, b : b + 1])
                     else:
                         nc.vector.tensor_reduce(out=dw_cols[:, b : b + 1], in_=sums[b][:, :P], axis=mybir.AxisListType.X, op=ADD)
 
         gather_u(0)
-        for j in range(1, D_TILES):
+        for j in range(2, D_TILES):
             quantize(nc, w_bf[j], w_codes[j][:], w_scales[j][:], E4M3)
             multiply(j)
+        gather_u(1)
+        window_odd = keep.tile([P, T], F32, align_bytes=64, tag="last_weights_then_window")
+        nc.gpsimd.memset(window_odd[:], 0.0)
+        windows = [window_even, window_odd]
         for b in range(BLOCKS):
             sums.append(psum.tile([P, X], F32, tag="bank", name="sums%d" % b))
         scatter(0)
         for j in range(1, D_TILES):
-            gather_u(j)
+            if j + 1 < D_TILES:
+                gather_u(j + 1)
             gather_table(j - 1, 0, C)
             scatter(j)
+        prod.append(keep.tile([P, C], F32, name="prod_last", tag="weights_then_product"))
         lo = 0
         for width in LAST_PIECES:
             gather_table(D_TILES - 1, lo, lo + width)

@@ -53,7 +53,7 @@ def tile_attend_gebag_kernel(tc, eT, W, dz, wc, offs, bagoffs, out_0, out_1):
         w_raw = [w_raw_0[:], w_raw_1[:], w_raw_23[:, :, :P], w_raw_23[:, :, P:]]
         bag_list = keep.tile([P, C // 16], U16)
         idx_list = keep.tile([P, C // 16], U16)
-        wc_sb = keep.tile([P, C], F32, tag="weights_then_product")
+        wc_sb = keep.tile([P, C], F32)
         table = [keep.tile([P, T], F32, name="table%d" % j) for j in range(D_TILES)]
 
         nc.sync.dma_start(out=dz_raw[0][:], in_=dz_rows[:, :, :HALF])
@@ -128,20 +128,31 @@ def tile_attend_gebag_kernel(tc, eT, W, dz, wc, offs, bagoffs, out_0, out_1):
 
         ub = [keep.tile([P, C], F32, name="ub%d" % j) for j in range(D_TILES)]
         prod = [keep.tile([P, C], F32, name="prod%d" % j) for j in range(D_TILES - 1)]
+        picked = [keep.tile([P, C], F32, name="picked%d" % j) for j in range(D_TILES - 1)]
+        de = [keep.tile([P, C], F32, name="de%d" % j) for j in range(D_TILES - 1)]
+        de.append(keep.tile([P, C], F32, name="de_last", tag="weighted_then_product"))
         sums = []
         spent = keep.tile([P, P], F32)
 
         def gather_u(j):
             window = u_all[:, u_start(j) : u_start(j) + U_WINDOW]
             nc.vector.tensor_copy(ub[j][:], window.indirect(bag_list[:]))
+            weigh(j)
+
+        def weigh(j):
+            nc.gpsimd.tensor_tensor(de[j][:], ub[j][:], wc_sb[:], MULT)
 
         def scatter(j):
             window = windows[j % 2]
-            nc.vector.tensor_tensor(window[:].indirect(idx_list[:]), ub[j][:], wc_sb[:], MULT)
+            nc.vector.tensor_copy(window[:].indirect(idx_list[:]), de[j][:])
             nc.sync.dma_start(out=out_0[j * P : (j + 1) * P, :], in_=window[:])
 
         def gather_table(j, lo, hi):
-            nc.vector.tensor_tensor(prod[j][:, lo:hi], table[j][:].indirect(idx_list[:, lo // 16 : hi // 16]), ub[j][:, lo:hi], MULT)
+            if j < D_TILES - 1:
+                nc.vector.tensor_copy(picked[j][:], table[j][:].indirect(idx_list[:]))
+                nc.gpsimd.tensor_tensor(prod[j][:], picked[j][:], ub[j][:], MULT)
+            else:
+                nc.vector.tensor_tensor(prod[j][:, lo:hi], table[j][:].indirect(idx_list[:, lo // 16 : hi // 16]), ub[j][:, lo:hi], MULT)
             for b in range(lo // P, hi // P):
                 nc.tensor.matmul(
                     sums[b][:, :P],
@@ -173,7 +184,7 @@ def tile_attend_gebag_kernel(tc, eT, W, dz, wc, offs, bagoffs, out_0, out_1):
                 gather_u(j + 1)
             gather_table(j - 1, 0, C)
             scatter(j)
-        prod.append(keep.tile([P, C], F32, name="prod_last", tag="weights_then_product"))
+        prod.append(keep.tile([P, C], F32, name="prod_last", tag="weighted_then_product"))
         lo = 0
         for width in LAST_PIECES:
             gather_table(D_TILES - 1, lo, lo + width)

@@ -19,12 +19,14 @@ COPY = mybir.ActivationFunctionType.Copy
 
 P = 128
 PACK = 4
+SQUARE = 32
 D_TILES = D // P
 BLOCKS = C // P
 U_WINDOW = 1376
-HALF = X // 2
-DZ_VECTOR_SHARE = 168
-LAST_PIECES = (512, 256, 128, 128)
+DZ_VECTOR_SHARE = 336
+EARLY = C // 2
+LAST = C - P
+VECTOR_SUMS = 2
 
 
 def interleave_views(grouped, raw, lo, hi):
@@ -41,60 +43,57 @@ def tile_attend_gebag_kernel(tc, eT, W, dz, wc, offs, bagoffs, out_0, out_1):
     nc = tc.nc
     with ExitStack() as ctx:
         keep = ctx.enter_context(tc.tile_pool(name="keep", bufs=1))
+        placed = ctx.enter_context(tc.tile_pool(name="placed", bufs=1))
         psum = ctx.enter_context(tc.psum_pool(name="psum", bufs=8))
 
         W_rows = W.rearrange("(p t) c -> p t c", t=PACK)
         dz_rows = dz.rearrange("(p t) c -> p t c", t=PACK)
 
-        dz_raw = [keep.tile([P, PACK, HALF], F32, name="dz_raw%d" % h) for h in range(2)]
+        dz_raw = keep.tile([P, PACK, X], F32)
         w_raw_0 = keep.tile([P, PACK, P], F32)
         w_raw_1 = keep.tile([P, PACK, P], F32)
         w_raw_23 = keep.tile([P, PACK, 2 * P], F32)
-        w_raw = [w_raw_0[:], w_raw_1[:], w_raw_23[:, :, :P], w_raw_23[:, :, P:]]
         bag_list = keep.tile([P, C // 16], U16)
         idx_list = keep.tile([P, C // 16], U16)
         wc_sb = keep.tile([P, C], F32)
         table = [keep.tile([P, T], F32, name="table%d" % j) for j in range(D_TILES)]
 
-        nc.sync.dma_start(out=dz_raw[0][:], in_=dz_rows[:, :, :HALF])
+        nc.sync.dma_start(out=dz_raw[:], in_=dz_rows)
         nc.sync.dma_start(out=w_raw_0[:], in_=W_rows[:, :, :P])
-        nc.sync.dma_start(out=dz_raw[1][:], in_=dz_rows[:, :, HALF:])
-        nc.sync.dma_start(out=w_raw_1[:], in_=W_rows[:, :, P : 2 * P])
-        nc.sync.dma_start(bag_list[:], bagoffs)
-        nc.sync.dma_start(out=w_raw_23[:], in_=W_rows[:, :, 2 * P :])
         nc.sync.dma_start(idx_list[:], offs)
+        nc.sync.dma_start(out=table[0][:], in_=eT[:P, :])
+        nc.sync.dma_start(bag_list[:], bagoffs)
+        nc.sync.dma_start(out=w_raw_1[:], in_=W_rows[:, :, P : 2 * P])
+        nc.sync.dma_start(out=w_raw_23[:], in_=W_rows[:, :, 2 * P :])
         nc.sync.dma_start(out=wc_sb[:], in_=wc)
-        for j in range(D_TILES):
+        for j in range(1, D_TILES):
             nc.sync.dma_start(out=table[j][:], in_=eT[j * P : (j + 1) * P, :])
 
         u_all = keep.tile([P, (D_TILES - 1) * X + U_WINDOW], F32)
-        window_even = keep.tile([P, T], F32)
-        nc.vector.memset(u_all[:, D_TILES * X :], 0.0)
-        nc.vector.memset(window_even[:], 0.0)
+        windows = [keep.tile([P, T], F32, name="window%d" % h) for h in range(2)]
+        for window in windows:
+            nc.vector.memset(window[:], 0.0)
+        nc.gpsimd.memset(u_all[:, D_TILES * X :], 0.0)
         ident = keep.tile([P, P], F32)
         make_identity(nc, ident[:])
-        dw_cols = keep.tile([P, P], F32)
+        dw_cols = keep.tile([P, BLOCKS * SQUARE], F32, align_bytes=64)
         nc.gpsimd.memset(dw_cols[:], 0.0)
 
         dz_codes = keep.tile([P, X], U32, align_bytes=64)
         dz_scales = keep.tile([P, X], U8, align_bytes=64)
-        dz_bf = [keep.tile([P, HALF, PACK], BF16, align_bytes=64, name="dz_bf%d" % h) for h in range(2)]
-        w_codes = [keep.tile([P, P], U32, align_bytes=64, name="w_codes%d" % j) for j in range(D_TILES)]
-        w_scales = [keep.tile([P, P], U8, align_bytes=64, name="w_scales%d" % j) for j in range(D_TILES)]
-        w_bf = [keep.tile([P, P, PACK], BF16, align_bytes=64, name="w_bf%d" % j) for j in range(D_TILES - 1)]
-        w_bf.append(keep.tile([P, P, PACK], BF16, align_bytes=64, name="w_bf_last", tag="last_weights_then_window"))
+        dz_bf = keep.tile([P, X, PACK], BF16, align_bytes=64)
+        w_codes = keep.tile([P, D], U32, align_bytes=64)
+        w_scales = keep.tile([P, D], U8, align_bytes=64)
+        w_bf_0 = keep.tile([P, P, PACK], BF16, align_bytes=64)
+        w_bf_1 = keep.tile([P, P, PACK], BF16, align_bytes=64, tag="weights_1_then_ub_0")
+        w_bf_23 = placed.tile([P, 2 * P, PACK], BF16, align_bytes=64, offset=3072)
 
-        dst, src = interleave_views(dz_bf[0], dz_raw[0], 0, HALF)
-        nc.vector.tensor_copy(out=dst, in_=src)
-        dst, src = interleave_views(w_bf[0], w_raw[0], 0, P)
-        nc.scalar.activation(out=dst, in_=src, func=COPY)
-        quantize(nc, dz_bf[0], dz_codes[:, :HALF], dz_scales[:, :HALF], E5M2)
-        quantize(nc, w_bf[0], w_codes[0][:], w_scales[0][:], E4M3)
-        dst, src = interleave_views(dz_bf[1], dz_raw[1], 0, DZ_VECTOR_SHARE)
-        nc.vector.tensor_copy(out=dst, in_=src)
-        dst, src = interleave_views(dz_bf[1], dz_raw[1], DZ_VECTOR_SHARE, HALF)
-        nc.scalar.activation(out=dst, in_=src, func=COPY)
-        quantize(nc, dz_bf[1], dz_codes[:, HALF:], dz_scales[:, HALF:], E5M2)
+        def cast(engine_copy, grouped, raw, lo, hi):
+            dst, src = interleave_views(grouped, raw, lo, hi)
+            engine_copy(out=dst, in_=src)
+
+        def scalar_cast(out, in_):
+            nc.scalar.activation(out=out, in_=in_, func=COPY)
 
         def u_start(j):
             return (D_TILES - 1 - j) * X
@@ -103,43 +102,35 @@ def tile_attend_gebag_kernel(tc, eT, W, dz, wc, offs, bagoffs, out_0, out_1):
             acc = psum.tile([P, X], F32, tag="bank")
             nc.tensor.matmul_mx(
                 out=acc[:],
-                lhsT=w_codes[j][:].bitcast(E4M3),
-                lhsT_scale=w_scales[j][:],
+                lhsT=w_codes[:, j * P : (j + 1) * P].bitcast(E4M3),
+                lhsT_scale=w_scales[:, j * P : (j + 1) * P],
                 rhs=dz_codes[:].bitcast(E5M2),
                 rhs_scale=dz_scales[:],
                 start=True,
                 stop=True,
             )
-            if j == 0:
-                nc.vector.tensor_copy(out=u_all[:, u_start(j) : u_start(j) + X], in_=acc[:])
-            else:
-                nc.scalar.copy(out=u_all[:, u_start(j) : u_start(j) + X], in_=acc[:])
+            nc.scalar.copy(out=u_all[:, u_start(j) : u_start(j) + X], in_=acc[:])
 
-        def cast_weights(j):
-            dst, src = interleave_views(w_bf[j], w_raw[j], 0, P)
-            nc.scalar.activation(out=dst, in_=src, func=COPY)
-
-        cast_weights(1)
-        quantize(nc, w_bf[1], w_codes[1][:], w_scales[1][:], E4M3)
+        cast(nc.vector.tensor_copy, dz_bf, dz_raw, 0, DZ_VECTOR_SHARE)
+        cast(scalar_cast, dz_bf, dz_raw, DZ_VECTOR_SHARE, X)
+        cast(scalar_cast, w_bf_0, w_raw_0, 0, P)
+        quantize(nc, dz_bf, dz_codes[:], dz_scales[:], E5M2)
+        quantize(nc, w_bf_0, w_codes[:, :P], w_scales[:, :P], E4M3)
         multiply(0)
-        multiply(1)
-        cast_weights(2)
-        cast_weights(3)
 
-        ub = [keep.tile([P, C], F32, name="ub%d" % j) for j in range(D_TILES)]
-        prod = [keep.tile([P, C], F32, name="prod%d" % j) for j in range(D_TILES - 1)]
         picked = [keep.tile([P, C], F32, name="picked%d" % j) for j in range(D_TILES - 1)]
-        de = [keep.tile([P, C], F32, name="de%d" % j) for j in range(D_TILES - 1)]
-        de.append(keep.tile([P, C], F32, name="de_last", tag="weighted_then_product"))
+        prod = [keep.tile([P, C], F32, name="prod%d" % j) for j in range(D_TILES - 1)]
+        ub = []
+        de = []
         sums = []
         spent = keep.tile([P, P], F32)
+
+        def gather_table(j):
+            nc.vector.tensor_copy(picked[j][:], table[j][:].indirect(idx_list[:]))
 
         def gather_u(j):
             window = u_all[:, u_start(j) : u_start(j) + U_WINDOW]
             nc.vector.tensor_copy(ub[j][:], window.indirect(bag_list[:]))
-            weigh(j)
-
-        def weigh(j):
             nc.gpsimd.tensor_tensor(de[j][:], ub[j][:], wc_sb[:], MULT)
 
         def scatter(j):
@@ -147,51 +138,69 @@ def tile_attend_gebag_kernel(tc, eT, W, dz, wc, offs, bagoffs, out_0, out_1):
             nc.vector.tensor_copy(window[:].indirect(idx_list[:]), de[j][:])
             nc.sync.dma_start(out=out_0[j * P : (j + 1) * P, :], in_=window[:])
 
-        def gather_table(j, lo, hi):
-            if j < D_TILES - 1:
-                nc.vector.tensor_copy(picked[j][:], table[j][:].indirect(idx_list[:]))
-                nc.gpsimd.tensor_tensor(prod[j][:], picked[j][:], ub[j][:], MULT)
-            else:
-                nc.vector.tensor_tensor(prod[j][:, lo:hi], table[j][:].indirect(idx_list[:, lo // 16 : hi // 16]), ub[j][:, lo:hi], MULT)
+        def turn_and_add(j, values, lo, hi):
             for b in range(lo // P, hi // P):
                 nc.tensor.matmul(
                     sums[b][:, :P],
-                    lhsT=prod[j][:, b * P : (b + 1) * P],
+                    lhsT=values[:, b * P - lo : (b + 1) * P - lo],
                     rhs=ident[:],
                     is_transpose=True,
                     start=(j == 0),
                     stop=(j == D_TILES - 1),
                 )
-                if j == D_TILES - 1:
-                    if b < BLOCKS - 2:
-                        nc.scalar.activation(out=spent[:], in_=sums[b][:, :P], func=COPY, accum_out=dw_cols[:, b : b + 1])
-                    else:
-                        nc.vector.tensor_reduce(out=dw_cols[:, b : b + 1], in_=sums[b][:, :P], axis=mybir.AxisListType.X, op=ADD)
 
-        gather_u(0)
-        for j in range(2, D_TILES):
-            quantize(nc, w_bf[j], w_codes[j][:], w_scales[j][:], E4M3)
-            multiply(j)
-        gather_u(1)
-        window_odd = keep.tile([P, T], F32, align_bytes=64, tag="last_weights_then_window")
-        nc.gpsimd.memset(window_odd[:], 0.0)
-        windows = [window_even, window_odd]
+        def product(j):
+            nc.gpsimd.tensor_tensor(prod[j][:], picked[j][:], ub[j][:], MULT)
+            turn_and_add(j, prod[j], 0, C)
+
+        def last_product(values, lo, hi):
+            j = D_TILES - 1
+            nc.vector.tensor_tensor(values, table[j][:].indirect(idx_list[:, lo // 16 : hi // 16]), ub[j][:, lo:hi], MULT)
+            turn_and_add(j, values, lo, hi)
+
+        def dw_column(b):
+            return dw_cols[:, b * SQUARE : b * SQUARE + 1]
+
+        gather_table(0)
+        cast(scalar_cast, w_bf_1, w_raw_1, 0, P)
+        quantize(nc, w_bf_1, w_codes[:, P : 2 * P], w_scales[:, P : 2 * P], E4M3)
+        multiply(1)
+        cast(scalar_cast, w_bf_23, w_raw_23, 0, 2 * P)
+        quantize(nc, w_bf_23, w_codes[:, 2 * P :], w_scales[:, 2 * P :], E4M3)
+        multiply(2)
+        multiply(3)
+
+        ub.append(keep.tile([P, C], F32, align_bytes=64, name="ub0", tag="weights_1_then_ub_0"))
+        ub.append(placed.tile([P, C], F32, align_bytes=64, name="ub1", offset=0))
+        ub.extend(keep.tile([P, C], F32, name="ub%d" % j) for j in range(2, D_TILES))
+        de.append(placed.tile([P, C], F32, align_bytes=64, name="de0", offset=4096))
+        de.extend(keep.tile([P, C], F32, name="de%d" % j) for j in range(1, D_TILES - 1))
+        de.append(keep.tile([P, C], F32, name="de_last", tag="de_then_product"))
         for b in range(BLOCKS):
             sums.append(psum.tile([P, X], F32, tag="bank", name="sums%d" % b))
-        scatter(0)
-        for j in range(1, D_TILES):
-            if j + 1 < D_TILES:
-                gather_u(j + 1)
-            gather_table(j - 1, 0, C)
-            scatter(j)
-        prod.append(keep.tile([P, C], F32, name="prod_last", tag="weighted_then_product"))
-        lo = 0
-        for width in LAST_PIECES:
-            gather_table(D_TILES - 1, lo, lo + width)
-            lo = lo + width
 
-        turned = psum.tile([P, X], F32, tag="bank")
-        nc.tensor.transpose(turned[:, :P], dw_cols[:], ident[:])
-        dw_rows = keep.tile([BLOCKS, P], F32)
-        nc.scalar.copy(out=dw_rows[:], in_=turned[:BLOCKS, :P])
-        nc.sync.dma_start(out=out_1.rearrange("o (b p) -> (o b) p", p=P), in_=dw_rows[:])
+        gather_u(0)
+        for j in range(D_TILES - 1):
+            gather_u(j + 1)
+            product(j)
+            scatter(j)
+            if j + 1 < D_TILES - 1:
+                gather_table(j + 1)
+
+        prod_early = keep.tile([P, EARLY], F32)
+        last_product(prod_early[:], 0, EARLY)
+        scatter(D_TILES - 1)
+        prod_late = keep.tile([P, C - EARLY], F32, tag="de_then_product")
+        last_product(prod_late[:, : LAST - EARLY], EARLY, LAST)
+        last_product(prod_late[:, LAST - EARLY :], LAST, C)
+        for b in range(BLOCKS - VECTOR_SUMS):
+            nc.scalar.activation(out=spent[:], in_=sums[b][:, :P], func=COPY, accum_out=dw_column(b))
+        for b in range(BLOCKS - VECTOR_SUMS, BLOCKS):
+            nc.vector.tensor_reduce(out=dw_column(b), in_=sums[b][:, :P], axis=mybir.AxisListType.X, op=ADD)
+
+        dw_rows = keep.tile([P, BLOCKS * SQUARE], F32, align_bytes=64)
+        nc.vector.transpose(dw_rows[:], dw_cols[:])
+        nc.sync.dma_start(
+            out=out_1.rearrange("o (b q i) -> (o q) b i", q=P // SQUARE, i=SQUARE),
+            in_=dw_rows[0:P:SQUARE, :].rearrange("q (b i) -> q b i", i=SQUARE),
+        )

@@ -26,7 +26,6 @@ U_WINDOW = 1376
 DZ_VECTOR_SHARE = 336
 EARLY = C // 2
 LAST = C - P
-VECTOR_SUMS = 2
 
 
 def interleave_views(grouped, raw, lo, hi):
@@ -36,7 +35,7 @@ def interleave_views(grouped, raw, lo, hi):
 
 
 def quantize(nc, grouped, codes, scales, fmt):
-    nc.vector.quantize_mx(out=codes.bitcast(fmt), scales=scales, in_=grouped[:].rearrange("p c t -> p (c t)"))
+    nc.vector.quantize_mx(out=codes.bitcast(fmt), scales=scales, in_=grouped.rearrange("p c t -> p (c t)"))
 
 
 def tile_attend_gebag_kernel(tc, eT, W, dz, wc, offs, bagoffs, out_0, out_1):
@@ -51,8 +50,7 @@ def tile_attend_gebag_kernel(tc, eT, W, dz, wc, offs, bagoffs, out_0, out_1):
 
         dz_raw = keep.tile([P, PACK, X], F32)
         w_raw_0 = keep.tile([P, PACK, P], F32)
-        w_raw_1 = keep.tile([P, PACK, P], F32)
-        w_raw_23 = keep.tile([P, PACK, 2 * P], F32)
+        w_raw_rest = keep.tile([P, PACK, D - P], F32)
         bag_list = keep.tile([P, C // 16], U16)
         idx_list = keep.tile([P, C // 16], U16)
         wc_sb = keep.tile([P, C], F32)
@@ -63,10 +61,10 @@ def tile_attend_gebag_kernel(tc, eT, W, dz, wc, offs, bagoffs, out_0, out_1):
         nc.sync.dma_start(idx_list[:], offs)
         nc.sync.dma_start(out=table[0][:], in_=eT[:P, :])
         nc.sync.dma_start(bag_list[:], bagoffs)
-        nc.sync.dma_start(out=w_raw_1[:], in_=W_rows[:, :, P : 2 * P])
-        nc.sync.dma_start(out=w_raw_23[:], in_=W_rows[:, :, 2 * P :])
+        nc.sync.dma_start(out=w_raw_rest[:], in_=W_rows[:, :, P:])
+        nc.sync.dma_start(out=table[1][:], in_=eT[P : 2 * P, :])
         nc.sync.dma_start(out=wc_sb[:], in_=wc)
-        for j in range(1, D_TILES):
+        for j in range(2, D_TILES):
             nc.sync.dma_start(out=table[j][:], in_=eT[j * P : (j + 1) * P, :])
 
         u_all = keep.tile([P, (D_TILES - 1) * X + U_WINDOW], F32)
@@ -76,8 +74,10 @@ def tile_attend_gebag_kernel(tc, eT, W, dz, wc, offs, bagoffs, out_0, out_1):
         nc.gpsimd.memset(u_all[:, D_TILES * X :], 0.0)
         ident = keep.tile([P, P], F32)
         make_identity(nc, ident[:])
-        dw_cols = keep.tile([P, BLOCKS * SQUARE], F32, align_bytes=64)
-        nc.gpsimd.memset(dw_cols[:], 0.0)
+        dw_cols_early = keep.tile([P, P], F32)
+        dw_cols_late = keep.tile([P, P], F32, align_bytes=64)
+        nc.gpsimd.memset(dw_cols_early[:], 0.0)
+        nc.gpsimd.memset(dw_cols_late[:], 0.0)
 
         dz_codes = keep.tile([P, X], U32, align_bytes=64)
         dz_scales = keep.tile([P, X], U8, align_bytes=64)
@@ -85,8 +85,7 @@ def tile_attend_gebag_kernel(tc, eT, W, dz, wc, offs, bagoffs, out_0, out_1):
         w_codes = keep.tile([P, D], U32, align_bytes=64)
         w_scales = keep.tile([P, D], U8, align_bytes=64)
         w_bf_0 = keep.tile([P, P, PACK], BF16, align_bytes=64)
-        w_bf_1 = keep.tile([P, P, PACK], BF16, align_bytes=64, tag="weights_1_then_ub_0")
-        w_bf_23 = placed.tile([P, 2 * P, PACK], BF16, align_bytes=64, offset=3072)
+        w_bf_rest = placed.tile([P, D - P, PACK], BF16, align_bytes=64, offset=3072)
 
         def cast(engine_copy, grouped, raw, lo, hi):
             dst, src = interleave_views(grouped, raw, lo, hi)
@@ -114,13 +113,13 @@ def tile_attend_gebag_kernel(tc, eT, W, dz, wc, offs, bagoffs, out_0, out_1):
         cast(nc.vector.tensor_copy, dz_bf, dz_raw, 0, DZ_VECTOR_SHARE)
         cast(scalar_cast, dz_bf, dz_raw, DZ_VECTOR_SHARE, X)
         cast(scalar_cast, w_bf_0, w_raw_0, 0, P)
-        quantize(nc, dz_bf, dz_codes[:], dz_scales[:], E5M2)
-        quantize(nc, w_bf_0, w_codes[:, :P], w_scales[:, :P], E4M3)
+        quantize(nc, dz_bf[:], dz_codes[:], dz_scales[:], E5M2)
+        quantize(nc, w_bf_0[:], w_codes[:, :P], w_scales[:, :P], E4M3)
         multiply(0)
 
-        picked = [keep.tile([P, C], F32, name="picked%d" % j) for j in range(D_TILES - 1)]
-        prod = [keep.tile([P, C], F32, name="prod%d" % j) for j in range(D_TILES - 1)]
-        ub = []
+        ub = [keep.tile([P, C], F32, name="ub%d" % j) for j in range(D_TILES)]
+        picked = [keep.tile([P, C], F32, name="picked0")]
+        prod = []
         de = []
         sums = []
         spent = keep.tile([P, P], F32)
@@ -131,11 +130,11 @@ def tile_attend_gebag_kernel(tc, eT, W, dz, wc, offs, bagoffs, out_0, out_1):
         def gather_u(j):
             window = u_all[:, u_start(j) : u_start(j) + U_WINDOW]
             nc.vector.tensor_copy(ub[j][:], window.indirect(bag_list[:]))
-            nc.gpsimd.tensor_tensor(de[j][:], ub[j][:], wc_sb[:], MULT)
+            nc.gpsimd.tensor_tensor(de[j], ub[j][:], wc_sb[:], MULT)
 
         def scatter(j):
             window = windows[j % 2]
-            nc.vector.tensor_copy(window[:].indirect(idx_list[:]), de[j][:])
+            nc.vector.tensor_copy(window[:].indirect(idx_list[:]), de[j])
             nc.sync.dma_start(out=out_0[j * P : (j + 1) * P, :], in_=window[:])
 
         def turn_and_add(j, values, lo, hi):
@@ -150,7 +149,7 @@ def tile_attend_gebag_kernel(tc, eT, W, dz, wc, offs, bagoffs, out_0, out_1):
                 )
 
         def product(j):
-            nc.gpsimd.tensor_tensor(prod[j][:], picked[j][:], ub[j][:], MULT)
+            nc.gpsimd.tensor_tensor(prod[j], picked[j][:], ub[j][:], MULT)
             turn_and_add(j, prod[j], 0, C)
 
         def last_product(values, lo, hi):
@@ -158,49 +157,61 @@ def tile_attend_gebag_kernel(tc, eT, W, dz, wc, offs, bagoffs, out_0, out_1):
             nc.vector.tensor_tensor(values, table[j][:].indirect(idx_list[:, lo // 16 : hi // 16]), ub[j][:, lo:hi], MULT)
             turn_and_add(j, values, lo, hi)
 
-        def dw_column(b):
-            return dw_cols[:, b * SQUARE : b * SQUARE + 1]
+        def sum_on_scalar(b, column):
+            nc.scalar.activation(out=spent[:], in_=sums[b][:, :P], func=COPY, accum_out=column)
+
+        def sum_on_vector(b, column):
+            nc.vector.tensor_reduce(out=column, in_=sums[b][:, :P], axis=mybir.AxisListType.X, op=ADD)
 
         gather_table(0)
-        cast(scalar_cast, w_bf_1, w_raw_1, 0, P)
-        quantize(nc, w_bf_1, w_codes[:, P : 2 * P], w_scales[:, P : 2 * P], E4M3)
-        multiply(1)
-        cast(scalar_cast, w_bf_23, w_raw_23, 0, 2 * P)
-        quantize(nc, w_bf_23, w_codes[:, 2 * P :], w_scales[:, 2 * P :], E4M3)
-        multiply(2)
-        multiply(3)
+        cast(scalar_cast, w_bf_rest, w_raw_rest, 0, D - P)
+        quantize(nc, w_bf_rest[:, :P, :], w_codes[:, P : 2 * P], w_scales[:, P : 2 * P], E4M3)
+        quantize(nc, w_bf_rest[:, P:, :], w_codes[:, 2 * P :], w_scales[:, 2 * P :], E4M3)
+        for j in range(1, D_TILES):
+            multiply(j)
 
-        ub.append(keep.tile([P, C], F32, align_bytes=64, name="ub0", tag="weights_1_then_ub_0"))
-        ub.append(placed.tile([P, C], F32, align_bytes=64, name="ub1", offset=0))
-        ub.extend(keep.tile([P, C], F32, name="ub%d" % j) for j in range(2, D_TILES))
-        de.append(placed.tile([P, C], F32, align_bytes=64, name="de0", offset=4096))
-        de.extend(keep.tile([P, C], F32, name="de%d" % j) for j in range(1, D_TILES - 1))
-        de.append(keep.tile([P, C], F32, name="de_last", tag="de_then_product"))
+        picked.append(placed.tile([P, C], F32, align_bytes=64, name="picked1", offset=0))
+        picked.append(keep.tile([P, C], F32, name="picked2"))
+        first_products = placed.tile([P, 2 * C], F32, align_bytes=64, offset=4096)
+        prod.append(first_products[:, C:])
+        prod.extend(keep.tile([P, C], F32, name="prod%d" % j)[:] for j in range(1, D_TILES - 1))
+        de.append(first_products[:, :C])
+        de.extend(keep.tile([P, C], F32, name="de%d" % j)[:] for j in range(1, D_TILES - 1))
+        de.append(keep.tile([P, C], F32, name="de_last", tag="de_then_product")[:])
         for b in range(BLOCKS):
             sums.append(psum.tile([P, X], F32, tag="bank", name="sums%d" % b))
 
         gather_u(0)
         for j in range(D_TILES - 1):
+            if j + 1 < D_TILES - 1:
+                gather_table(j + 1)
             gather_u(j + 1)
             product(j)
             scatter(j)
-            if j + 1 < D_TILES - 1:
-                gather_table(j + 1)
 
         prod_early = keep.tile([P, EARLY], F32)
         last_product(prod_early[:], 0, EARLY)
+        early_blocks = EARLY // P
+        for b in range(early_blocks):
+            sum_on_scalar(b, dw_cols_early[:, b : b + 1])
+        turned = psum.tile([P, X], F32, tag="bank")
+        nc.tensor.transpose(turned[:, :P], dw_cols_early[:], ident[:])
+        dw_rows_early = keep.tile([early_blocks, P], F32)
+        nc.scalar.copy(out=dw_rows_early[:], in_=turned[:early_blocks, :P])
+        nc.sync.dma_start(out=out_1[:, :EARLY].rearrange("o (b p) -> (o b) p", p=P), in_=dw_rows_early[:])
+
         scatter(D_TILES - 1)
         prod_late = keep.tile([P, C - EARLY], F32, tag="de_then_product")
         last_product(prod_late[:, : LAST - EARLY], EARLY, LAST)
         last_product(prod_late[:, LAST - EARLY :], LAST, C)
-        for b in range(BLOCKS - VECTOR_SUMS):
-            nc.scalar.activation(out=spent[:], in_=sums[b][:, :P], func=COPY, accum_out=dw_column(b))
-        for b in range(BLOCKS - VECTOR_SUMS, BLOCKS):
-            nc.vector.tensor_reduce(out=dw_column(b), in_=sums[b][:, :P], axis=mybir.AxisListType.X, op=ADD)
+        for b in range(early_blocks, BLOCKS):
+            at = (b - early_blocks) * SQUARE
+            add_up = sum_on_scalar if b in (early_blocks, BLOCKS - 1) else sum_on_vector
+            add_up(b, dw_cols_late[:, at : at + 1])
 
-        dw_rows = keep.tile([P, BLOCKS * SQUARE], F32, align_bytes=64)
-        nc.vector.transpose(dw_rows[:], dw_cols[:])
+        dw_rows_late = keep.tile([P, P], F32, align_bytes=64)
+        nc.vector.transpose(dw_rows_late[:], dw_cols_late[:])
         nc.sync.dma_start(
-            out=out_1.rearrange("o (b q i) -> (o q) b i", q=P // SQUARE, i=SQUARE),
-            in_=dw_rows[0:P:SQUARE, :].rearrange("q (b i) -> q b i", i=SQUARE),
+            out=out_1[:, EARLY:].rearrange("o (b q i) -> (o q) b i", q=P // SQUARE, i=SQUARE),
+            in_=dw_rows_late[0:P:SQUARE, :].rearrange("q (b i) -> q b i", i=SQUARE),
         )

@@ -26,6 +26,7 @@ U_WINDOW = 1376
 DZ_VECTOR_SHARE = 336
 EARLY = C // 2
 LAST = C - P
+COPIED_TILES = 2
 
 
 def interleave_views(grouped, raw, lo, hi):
@@ -42,7 +43,6 @@ def tile_attend_gebag_kernel(tc, eT, W, dz, wc, offs, bagoffs, out_0, out_1):
     nc = tc.nc
     with ExitStack() as ctx:
         keep = ctx.enter_context(tc.tile_pool(name="keep", bufs=1))
-        placed = ctx.enter_context(tc.tile_pool(name="placed", bufs=1))
         psum = ctx.enter_context(tc.psum_pool(name="psum", bufs=8))
 
         W_rows = W.rearrange("(p t) c -> p t c", t=PACK)
@@ -53,7 +53,7 @@ def tile_attend_gebag_kernel(tc, eT, W, dz, wc, offs, bagoffs, out_0, out_1):
         w_raw_rest = keep.tile([P, PACK, D - P], F32)
         bag_list = keep.tile([P, C // 16], U16)
         idx_list = keep.tile([P, C // 16], U16)
-        wc_sb = keep.tile([P, C], F32)
+        wc_sb = keep.tile([P, C], F32, tag="wc_then_product")
         table = [keep.tile([P, T], F32, name="table%d" % j) for j in range(D_TILES)]
 
         nc.sync.dma_start(out=dz_raw[:], in_=dz_rows)
@@ -68,7 +68,7 @@ def tile_attend_gebag_kernel(tc, eT, W, dz, wc, offs, bagoffs, out_0, out_1):
             nc.sync.dma_start(out=table[j][:], in_=eT[j * P : (j + 1) * P, :])
 
         u_all = keep.tile([P, (D_TILES - 1) * X + U_WINDOW], F32)
-        windows = [keep.tile([P, T], F32, name="window%d" % h) for h in range(2)]
+        windows = [keep.tile([P, T], F32, name="window%d" % h, tag="window%d" % h) for h in range(2)]
         for window in windows:
             nc.vector.memset(window[:], 0.0)
         nc.gpsimd.memset(u_all[:, D_TILES * X :], 0.0)
@@ -85,7 +85,7 @@ def tile_attend_gebag_kernel(tc, eT, W, dz, wc, offs, bagoffs, out_0, out_1):
         w_codes = keep.tile([P, D], U32, align_bytes=64)
         w_scales = keep.tile([P, D], U8, align_bytes=64)
         w_bf_0 = keep.tile([P, P, PACK], BF16, align_bytes=64)
-        w_bf_rest = placed.tile([P, D - P, PACK], BF16, align_bytes=64, offset=3072)
+        w_bf_rest = keep.tile([P, D - P, PACK], BF16, align_bytes=64, tag="weights_then_products")
 
         def cast(engine_copy, grouped, raw, lo, hi):
             dst, src = interleave_views(grouped, raw, lo, hi)
@@ -118,7 +118,7 @@ def tile_attend_gebag_kernel(tc, eT, W, dz, wc, offs, bagoffs, out_0, out_1):
         multiply(0)
 
         ub = [keep.tile([P, C], F32, name="ub%d" % j) for j in range(D_TILES)]
-        picked = [keep.tile([P, C], F32, name="picked0")]
+        picked = [keep.tile([P, C], F32, name="picked%d" % j) for j in range(COPIED_TILES)]
         prod = []
         de = []
         sums = []
@@ -152,8 +152,7 @@ def tile_attend_gebag_kernel(tc, eT, W, dz, wc, offs, bagoffs, out_0, out_1):
             nc.gpsimd.tensor_tensor(prod[j], picked[j][:], ub[j][:], MULT)
             turn_and_add(j, prod[j], 0, C)
 
-        def last_product(values, lo, hi):
-            j = D_TILES - 1
+        def fused_product(j, values, lo, hi):
             nc.vector.tensor_tensor(values, table[j][:].indirect(idx_list[:, lo // 16 : hi // 16]), ub[j][:, lo:hi], MULT)
             turn_and_add(j, values, lo, hi)
 
@@ -170,27 +169,26 @@ def tile_attend_gebag_kernel(tc, eT, W, dz, wc, offs, bagoffs, out_0, out_1):
         for j in range(1, D_TILES):
             multiply(j)
 
-        picked.append(placed.tile([P, C], F32, align_bytes=64, name="picked1", offset=0))
-        picked.append(keep.tile([P, C], F32, name="picked2"))
-        first_products = placed.tile([P, 2 * C], F32, align_bytes=64, offset=4096)
+        first_products = keep.tile([P, 2 * C], F32, align_bytes=64, tag="weights_then_products")
         prod.append(first_products[:, C:])
-        prod.extend(keep.tile([P, C], F32, name="prod%d" % j)[:] for j in range(1, D_TILES - 1))
+        prod.append(keep.tile([P, C], F32, name="prod1")[:])
         de.append(first_products[:, :C])
-        de.extend(keep.tile([P, C], F32, name="de%d" % j)[:] for j in range(1, D_TILES - 1))
-        de.append(keep.tile([P, C], F32, name="de_last", tag="de_then_product")[:])
+        de.extend(keep.tile([P, C], F32, name="de%d" % j)[:] for j in range(1, D_TILES))
         for b in range(BLOCKS):
             sums.append(psum.tile([P, X], F32, tag="bank", name="sums%d" % b))
 
         gather_u(0)
+        gather_table(1)
         for j in range(D_TILES - 1):
-            if j + 1 < D_TILES - 1:
-                gather_table(j + 1)
             gather_u(j + 1)
-            product(j)
+            if j < COPIED_TILES:
+                product(j)
             scatter(j)
 
-        prod_early = keep.tile([P, EARLY], F32)
-        last_product(prod_early[:], 0, EARLY)
+        prod_early = keep.tile([P, C], F32, tag="wc_then_product")
+        for j in range(COPIED_TILES, D_TILES):
+            at = (j - COPIED_TILES) * EARLY
+            fused_product(j, prod_early[:, at : at + EARLY], 0, EARLY)
         early_blocks = EARLY // P
         for b in range(early_blocks):
             sum_on_scalar(b, dw_cols_early[:, b : b + 1])
@@ -201,9 +199,10 @@ def tile_attend_gebag_kernel(tc, eT, W, dz, wc, offs, bagoffs, out_0, out_1):
         nc.sync.dma_start(out=out_1[:, :EARLY].rearrange("o (b p) -> (o b) p", p=P), in_=dw_rows_early[:])
 
         scatter(D_TILES - 1)
-        prod_late = keep.tile([P, C - EARLY], F32, tag="de_then_product")
-        last_product(prod_late[:, : LAST - EARLY], EARLY, LAST)
-        last_product(prod_late[:, LAST - EARLY :], LAST, C)
+        prod_late = keep.tile([P, C], F32, tag="window0")
+        fused_product(D_TILES - 2, prod_late[:, :EARLY], EARLY, C)
+        fused_product(D_TILES - 1, prod_late[:, EARLY:LAST], EARLY, LAST)
+        fused_product(D_TILES - 1, prod_late[:, LAST:], LAST, C)
         for b in range(early_blocks, BLOCKS):
             at = (b - early_blocks) * SQUARE
             add_up = sum_on_scalar if b in (early_blocks, BLOCKS - 1) else sum_on_vector

@@ -57,7 +57,7 @@ def tile_attend_gebag_kernel(tc, eT, W, dz, wc, offs, bagoffs, out_0, out_1):
         table = [keep.tile([P, T], F32, name="table%d" % j) for j in range(D_TILES)]
 
         nc.sync.dma_start(out=dz_raw[:], in_=dz_rows)
-        nc.sync.dma_start(out=w_raw_0[:], in_=W_rows[:, :, :P])
+        nc.scalar.dma_start(out=w_raw_0[:], in_=W_rows[:, :, :P])
         nc.sync.dma_start(idx_list[:], offs)
         nc.sync.dma_start(out=table[0][:], in_=eT[:P, :])
         nc.sync.dma_start(bag_list[:], bagoffs)
@@ -67,11 +67,9 @@ def tile_attend_gebag_kernel(tc, eT, W, dz, wc, offs, bagoffs, out_0, out_1):
         for j in range(2, D_TILES):
             nc.sync.dma_start(out=table[j][:], in_=eT[j * P : (j + 1) * P, :])
 
-        u_all = keep.tile([P, (D_TILES - 1) * X + U_WINDOW], F32)
         windows = [keep.tile([P, T], F32, name="window%d" % h, tag="window%d" % h) for h in range(2)]
         for window in windows:
             nc.vector.memset(window[:], 0.0)
-        nc.gpsimd.memset(u_all[:, D_TILES * X :], 0.0)
         ident = keep.tile([P, P], F32)
         make_identity(nc, ident[:])
         dw_cols_early = keep.tile([P, P], F32)
@@ -84,7 +82,7 @@ def tile_attend_gebag_kernel(tc, eT, W, dz, wc, offs, bagoffs, out_0, out_1):
         dz_bf = keep.tile([P, X, PACK], BF16, align_bytes=64)
         w_codes = keep.tile([P, D], U32, align_bytes=64)
         w_scales = keep.tile([P, D], U8, align_bytes=64)
-        w_bf_0 = keep.tile([P, P, PACK], BF16, align_bytes=64)
+        w_bf_0 = keep.tile([P, P, PACK], BF16, align_bytes=64, tag="weights_then_u")
         w_bf_rest = keep.tile([P, D - P, PACK], BF16, align_bytes=64, tag="weights_then_products")
 
         def cast(engine_copy, grouped, raw, lo, hi):
@@ -115,6 +113,8 @@ def tile_attend_gebag_kernel(tc, eT, W, dz, wc, offs, bagoffs, out_0, out_1):
         cast(scalar_cast, w_bf_0, w_raw_0, 0, P)
         quantize(nc, dz_bf[:], dz_codes[:], dz_scales[:], E5M2)
         quantize(nc, w_bf_0[:], w_codes[:, :P], w_scales[:, :P], E4M3)
+        u_all = keep.tile([P, (D_TILES - 1) * X + U_WINDOW], F32, align_bytes=64, tag="weights_then_u")
+        nc.gpsimd.memset(u_all[:, D_TILES * X :], 0.0)
         multiply(0)
 
         ub = [keep.tile([P, C], F32, name="ub%d" % j) for j in range(D_TILES)]

@@ -53,7 +53,7 @@ def tile_attend_gebag_kernel(tc, eT, W, dz, wc, offs, bagoffs, out_0, out_1):
         w_raw_rest = keep.tile([P, PACK, D - P], F32)
         bag_list = keep.tile([P, C // 16], U16)
         idx_list = keep.tile([P, C // 16], U16)
-        wc_sb = keep.tile([P, C], F32, tag="wc_then_product")
+        wc_sb = keep.tile([P, C], F32)
         table = [keep.tile([P, T], F32, name="table%d" % j) for j in range(D_TILES)]
 
         nc.sync.dma_start(out=dz_raw[:], in_=dz_rows)
@@ -91,6 +91,9 @@ def tile_attend_gebag_kernel(tc, eT, W, dz, wc, offs, bagoffs, out_0, out_1):
 
         def scalar_cast(out, in_):
             nc.scalar.activation(out=out, in_=in_, func=COPY)
+
+        def gpsimd_cast(out, in_):
+            nc.gpsimd.tensor_scalar(out=out, in0=in_, scalar1=1.0, scalar2=0.0, op0=MULT, op1=ADD)
 
         def u_start(j):
             return (D_TILES - 1 - j) * X
@@ -163,7 +166,8 @@ def tile_attend_gebag_kernel(tc, eT, W, dz, wc, offs, bagoffs, out_0, out_1):
             nc.vector.tensor_reduce(out=column, in_=sums[b][:, :P], axis=mybir.AxisListType.X, op=ADD)
 
         gather_table(0)
-        cast(scalar_cast, w_bf_rest, w_raw_rest, 0, D - P)
+        cast(scalar_cast, w_bf_rest, w_raw_rest, 0, D - 2 * P)
+        cast(gpsimd_cast, w_bf_rest, w_raw_rest, D - 2 * P, D - P)
         quantize(nc, w_bf_rest[:, :P, :], w_codes[:, P : 2 * P], w_scales[:, P : 2 * P], E4M3)
         quantize(nc, w_bf_rest[:, P:, :], w_codes[:, 2 * P :], w_scales[:, 2 * P :], E4M3)
         for j in range(1, D_TILES):
@@ -185,10 +189,12 @@ def tile_attend_gebag_kernel(tc, eT, W, dz, wc, offs, bagoffs, out_0, out_1):
                 product(j)
             scatter(j)
 
-        prod_early = keep.tile([P, C], F32, tag="wc_then_product")
         for j in range(COPIED_TILES, D_TILES):
-            at = (j - COPIED_TILES) * EARLY
-            fused_product(j, prod_early[:, at : at + EARLY], 0, EARLY)
+            picked_early = keep.tile([P, EARLY], F32, name="picked_early%d" % j)
+            prod_early = keep.tile([P, EARLY], F32, name="prod_early%d" % j)
+            nc.vector.tensor_copy(picked_early[:], table[j][:].indirect(idx_list[:, : EARLY // 16]))
+            nc.gpsimd.tensor_tensor(prod_early[:], picked_early[:], ub[j][:, :EARLY], MULT)
+            turn_and_add(j, prod_early, 0, EARLY)
         early_blocks = EARLY // P
         for b in range(early_blocks):
             sum_on_scalar(b, dw_cols_early[:, b : b + 1])

@@ -56,8 +56,8 @@ def tile_attend_gebag_kernel(tc, eT, W, dz, wc, offs, bagoffs, out_0, out_1):
         wc_sb = keep.tile([P, C], F32)
         table = [keep.tile([P, T], F32, name="table%d" % j) for j in range(D_TILES)]
 
-        nc.sync.dma_start(out=dz_raw[:], in_=dz_rows)
         nc.scalar.dma_start(out=w_raw_0[:], in_=W_rows[:, :, :P])
+        nc.sync.dma_start(out=dz_raw[:], in_=dz_rows)
         nc.sync.dma_start(idx_list[:], offs)
         nc.sync.dma_start(out=table[0][:], in_=eT[:P, :])
         nc.sync.dma_start(bag_list[:], bagoffs)
@@ -79,10 +79,9 @@ def tile_attend_gebag_kernel(tc, eT, W, dz, wc, offs, bagoffs, out_0, out_1):
 
         dz_codes = keep.tile([P, X], U32, align_bytes=64)
         dz_scales = keep.tile([P, X], U8, align_bytes=64)
-        dz_bf = keep.tile([P, X, PACK], BF16, align_bytes=64)
         w_codes = keep.tile([P, D], U32, align_bytes=64)
         w_scales = keep.tile([P, D], U8, align_bytes=64)
-        w_bf_0 = keep.tile([P, P, PACK], BF16, align_bytes=64, tag="weights_then_u")
+        w_bf_0 = keep.tile([P, P, PACK], BF16, align_bytes=64, tag="dz_then_u")
         w_bf_rest = keep.tile([P, D - P, PACK], BF16, align_bytes=64, tag="weights_then_products")
 
         def cast(engine_copy, grouped, raw, lo, hi):
@@ -111,12 +110,13 @@ def tile_attend_gebag_kernel(tc, eT, W, dz, wc, offs, bagoffs, out_0, out_1):
             )
             nc.scalar.copy(out=u_all[:, u_start(j) : u_start(j) + X], in_=acc[:])
 
+        cast(scalar_cast, w_bf_0, w_raw_0, 0, P)
+        quantize(nc, w_bf_0[:], w_codes[:, :P], w_scales[:, :P], E4M3)
+        dz_bf = keep.tile([P, X, PACK], BF16, align_bytes=64, tag="dz_then_u")
         cast(nc.vector.tensor_copy, dz_bf, dz_raw, 0, DZ_VECTOR_SHARE)
         cast(scalar_cast, dz_bf, dz_raw, DZ_VECTOR_SHARE, X)
-        cast(scalar_cast, w_bf_0, w_raw_0, 0, P)
         quantize(nc, dz_bf[:], dz_codes[:], dz_scales[:], E5M2)
-        quantize(nc, w_bf_0[:], w_codes[:, :P], w_scales[:, :P], E4M3)
-        u_all = keep.tile([P, (D_TILES - 1) * X + U_WINDOW], F32, align_bytes=64, tag="weights_then_u")
+        u_all = keep.tile([P, (D_TILES - 1) * X + U_WINDOW], F32, align_bytes=64, tag="dz_then_u")
         nc.gpsimd.memset(u_all[:, D_TILES * X :], 0.0)
         multiply(0)
 

@@ -56,7 +56,7 @@ def tile_attend_gebag_kernel(tc, eT, W, dz, wc, offs, bagoffs, out_0, out_1):
         wc_sb = keep.tile([P, C], F32)
         table = [keep.tile([P, T], F32, name="table%d" % j) for j in range(D_TILES)]
 
-        nc.scalar.dma_start(out=w_raw_0[:], in_=W_rows[:, :, :P])
+        nc.sync.dma_start(out=w_raw_0[:], in_=W_rows[:, :, :P])
         nc.sync.dma_start(out=dz_raw[:], in_=dz_rows)
         nc.sync.dma_start(idx_list[:], offs)
         nc.sync.dma_start(out=table[0][:], in_=eT[:P, :])

@@ -25,6 +25,7 @@ BLOCKS = C // P
 U_WINDOW = 1376
 DZ_VECTOR_SHARE = 336
 EARLY = C // 2
+MIDDLE = C - 2 * P
 LAST = C - P
 COPIED_TILES = 2
 
@@ -125,7 +126,7 @@ def tile_attend_gebag_kernel(tc, eT, W, dz, wc, offs, bagoffs, out_0, out_1):
         prod = []
         de = []
         sums = []
-        spent = keep.tile([P, P], F32)
+        spent = keep.tile([P, BLOCKS, P], F32)
 
         def gather_table(j):
             nc.vector.tensor_copy(picked[j][:], table[j][:].indirect(idx_list[:]))
@@ -160,7 +161,7 @@ def tile_attend_gebag_kernel(tc, eT, W, dz, wc, offs, bagoffs, out_0, out_1):
             turn_and_add(j, values, lo, hi)
 
         def sum_on_scalar(b, column):
-            nc.scalar.activation(out=spent[:], in_=sums[b][:, :P], func=COPY, accum_out=column)
+            nc.scalar.activation(out=spent[:, b, :], in_=sums[b][:, :P], func=COPY, accum_out=column)
 
         def sum_on_vector(b, column):
             nc.vector.tensor_reduce(out=column, in_=sums[b][:, :P], axis=mybir.AxisListType.X, op=ADD)
@@ -206,12 +207,15 @@ def tile_attend_gebag_kernel(tc, eT, W, dz, wc, offs, bagoffs, out_0, out_1):
 
         scatter(D_TILES - 1)
         prod_late = keep.tile([P, C], F32, tag="window0")
-        fused_product(D_TILES - 2, prod_late[:, :EARLY], EARLY, C)
-        fused_product(D_TILES - 1, prod_late[:, EARLY:LAST], EARLY, LAST)
-        fused_product(D_TILES - 1, prod_late[:, LAST:], LAST, C)
+        pieces = [(D_TILES - 2, EARLY, MIDDLE), (D_TILES - 1, EARLY, MIDDLE), (D_TILES - 2, MIDDLE, C)]
+        pieces += [(D_TILES - 1, MIDDLE, LAST), (D_TILES - 1, LAST, C)]
+        filled = 0
+        for j, lo, hi in pieces:
+            fused_product(j, prod_late[:, filled : filled + hi - lo], lo, hi)
+            filled += hi - lo
         for b in range(early_blocks, BLOCKS):
             at = (b - early_blocks) * SQUARE
-            add_up = sum_on_scalar if b in (early_blocks, BLOCKS - 1) else sum_on_vector
+            add_up = sum_on_vector if b == BLOCKS - 2 else sum_on_scalar
             add_up(b, dw_cols_late[:, at : at + 1])
 
         dw_rows_late = keep.tile([P, P], F32, align_bytes=64)

@@ -27,6 +27,7 @@ DZ_VECTOR_SHARE = 336
 EARLY = C // 2
 MIDDLE = C - 2 * P
 LAST = C - P
+PIECE = 2 * P
 COPIED_TILES = 2
 
 
@@ -121,9 +122,8 @@ def tile_attend_gebag_kernel(tc, eT, W, dz, wc, offs, bagoffs, out_0, out_1):
         nc.gpsimd.memset(u_all[:, D_TILES * X :], 0.0)
         multiply(0)
 
-        ub = [keep.tile([P, C], F32, name="ub%d" % j) for j in range(D_TILES)]
-        picked = [keep.tile([P, C], F32, name="picked%d" % j) for j in range(COPIED_TILES)]
-        prod = []
+        ub = [keep.tile([P, C], F32, name="ub%d" % j)[:] for j in range(COPIED_TILES)]
+        picked = [keep.tile([P, C], F32, name="picked%d" % j, tag="picked%d" % j) for j in range(COPIED_TILES)]
         de = []
         sums = []
         spent = keep.tile([P, BLOCKS, P], F32)
@@ -133,8 +133,8 @@ def tile_attend_gebag_kernel(tc, eT, W, dz, wc, offs, bagoffs, out_0, out_1):
 
         def gather_u(j):
             window = u_all[:, u_start(j) : u_start(j) + U_WINDOW]
-            nc.vector.tensor_copy(ub[j][:], window.indirect(bag_list[:]))
-            nc.gpsimd.tensor_tensor(de[j], ub[j][:], wc_sb[:], MULT)
+            nc.vector.tensor_copy(ub[j], window.indirect(bag_list[:]))
+            nc.gpsimd.tensor_tensor(de[j], ub[j], wc_sb[:], MULT)
 
         def scatter(j):
             window = windows[j % 2]
@@ -153,8 +153,8 @@ def tile_attend_gebag_kernel(tc, eT, W, dz, wc, offs, bagoffs, out_0, out_1):
                 )
 
         def product(j):
-            nc.gpsimd.tensor_tensor(prod[j], picked[j][:], ub[j][:], MULT)
-            turn_and_add(j, prod[j], 0, C)
+            nc.gpsimd.tensor_tensor(ub[j], ub[j], picked[j][:], MULT)
+            turn_and_add(j, ub[j], 0, C)
 
         def fused_product(j, values, lo, hi):
             nc.vector.tensor_tensor(values, table[j][:].indirect(idx_list[:, lo // 16 : hi // 16]), ub[j][:, lo:hi], MULT)
@@ -174,28 +174,38 @@ def tile_attend_gebag_kernel(tc, eT, W, dz, wc, offs, bagoffs, out_0, out_1):
         for j in range(1, D_TILES):
             multiply(j)
 
-        first_products = keep.tile([P, 2 * C], F32, align_bytes=64, tag="weights_then_products")
-        prod.append(first_products[:, C:])
-        prod.append(keep.tile([P, C], F32, name="prod1")[:])
-        de.append(first_products[:, :C])
-        de.extend(keep.tile([P, C], F32, name="de%d" % j)[:] for j in range(1, D_TILES))
+        de.append(keep.tile([P, C], F32, name="de0", align_bytes=64, tag="weights_then_products")[:])
         for b in range(BLOCKS):
             sums.append(psum.tile([P, X], F32, tag="bank", name="sums%d" % b))
 
+        def gather_piece(j, values, lo, hi):
+            nc.vector.tensor_copy(values, table[j][:].indirect(idx_list[:, lo // 16 : hi // 16]))
+            early.append((j, values, lo, hi))
+
+        early = []
         gather_u(0)
         gather_table(1)
-        for j in range(D_TILES - 1):
-            gather_u(j + 1)
-            if j < COPIED_TILES:
-                product(j)
+        product(0)
+        held = [keep.tile([P, 2 * C + PIECE], F32, name="held0", tag="picked0")]
+        de.append(held[0][:, C + PIECE :])
+        de.append(keep.tile([P, C], F32, name="de2", tag="de2_then_picked")[:])
+        de.append(keep.tile([P, C], F32, name="de3")[:])
+        gather_u(1)
+        product(1)
+        held.append(keep.tile([P, C + PIECE], F32, name="held1", tag="picked1"))
+        for j in range(COPIED_TILES):
             scatter(j)
-
-        for j in range(COPIED_TILES, D_TILES):
-            picked_early = keep.tile([P, EARLY], F32, name="picked_early%d" % j)
-            prod_early = keep.tile([P, EARLY], F32, name="prod_early%d" % j)
-            nc.vector.tensor_copy(picked_early[:], table[j][:].indirect(idx_list[:, : EARLY // 16]))
-            nc.gpsimd.tensor_tensor(prod_early[:], picked_early[:], ub[j][:, :EARLY], MULT)
-            turn_and_add(j, prod_early, 0, EARLY)
+            ub.append(held[j][:, :C])
+            gather_u(j + 2)
+            gather_piece(D_TILES - 2, held[j][:, C : C + PIECE], j * PIECE, (j + 1) * PIECE)
+        scatter(D_TILES - 2)
+        last_pieces = keep.tile([P, C], F32, tag="de2_then_picked")
+        gather_piece(D_TILES - 2, last_pieces[:, :PIECE], EARLY, MIDDLE)
+        gather_piece(D_TILES - 1, last_pieces[:, PIECE:], 0, MIDDLE)
+        for j, values, lo, hi in early:
+            prod_early = keep.tile([P, hi - lo], F32, name="prod_early%d_%d" % (j, lo))
+            nc.gpsimd.tensor_tensor(prod_early[:], values, ub[j][:, lo:hi], MULT)
+            turn_and_add(j, prod_early, lo, hi)
         early_blocks = EARLY // P
         for b in range(early_blocks):
             sum_on_scalar(b, dw_cols_early[:, b : b + 1])
@@ -207,8 +217,7 @@ def tile_attend_gebag_kernel(tc, eT, W, dz, wc, offs, bagoffs, out_0, out_1):
 
         scatter(D_TILES - 1)
         prod_late = keep.tile([P, C], F32, tag="window0")
-        pieces = [(D_TILES - 2, EARLY, MIDDLE), (D_TILES - 1, EARLY, MIDDLE), (D_TILES - 2, MIDDLE, C)]
-        pieces += [(D_TILES - 1, MIDDLE, LAST), (D_TILES - 1, LAST, C)]
+        pieces = [(D_TILES - 2, MIDDLE, C), (D_TILES - 1, MIDDLE, LAST), (D_TILES - 1, LAST, C)]
         filled = 0
         for j, lo, hi in pieces:
             fused_product(j, prod_late[:, filled : filled + hi - lo], lo, hi)

@@ -24,11 +24,9 @@ D_TILES = D // P
 BLOCKS = C // P
 U_WINDOW = 1376
 DZ_VECTOR_SHARE = 336
-EARLY = C // 2
-MIDDLE = C - 2 * P
+EARLY = C - 2 * P
 LAST = C - P
-PIECE = 2 * P
-COPIED_TILES = 2
+ROUNDED_AT = 4 * T - 64
 
 
 def interleave_views(grouped, raw, lo, hi):
@@ -45,6 +43,7 @@ def tile_attend_gebag_kernel(tc, eT, W, dz, wc, offs, bagoffs, out_0, out_1):
     nc = tc.nc
     with ExitStack() as ctx:
         keep = ctx.enter_context(tc.tile_pool(name="keep", bufs=1))
+        reused = ctx.enter_context(tc.tile_pool(name="reused", bufs=1))
         psum = ctx.enter_context(tc.psum_pool(name="psum", bufs=8))
 
         W_rows = W.rearrange("(p t) c -> p t c", t=PACK)
@@ -83,7 +82,7 @@ def tile_attend_gebag_kernel(tc, eT, W, dz, wc, offs, bagoffs, out_0, out_1):
         dz_scales = keep.tile([P, X], U8, align_bytes=64)
         w_codes = keep.tile([P, D], U32, align_bytes=64)
         w_scales = keep.tile([P, D], U8, align_bytes=64)
-        w_bf_0 = keep.tile([P, P, PACK], BF16, align_bytes=64, tag="dz_then_u")
+        w_bf_0 = reused.tile([P, P, PACK], BF16, align_bytes=64, offset=ROUNDED_AT)
         w_bf_rest = keep.tile([P, D - P, PACK], BF16, align_bytes=64, tag="weights_then_products")
 
         def cast(engine_copy, grouped, raw, lo, hi):
@@ -114,30 +113,34 @@ def tile_attend_gebag_kernel(tc, eT, W, dz, wc, offs, bagoffs, out_0, out_1):
 
         cast(scalar_cast, w_bf_0, w_raw_0, 0, P)
         quantize(nc, w_bf_0[:], w_codes[:, :P], w_scales[:, :P], E4M3)
-        dz_bf = keep.tile([P, X, PACK], BF16, align_bytes=64, tag="dz_then_u")
+        dz_bf = reused.tile([P, X, PACK], BF16, align_bytes=64, offset=ROUNDED_AT)
         cast(nc.vector.tensor_copy, dz_bf, dz_raw, 0, DZ_VECTOR_SHARE)
         cast(scalar_cast, dz_bf, dz_raw, DZ_VECTOR_SHARE, X)
         quantize(nc, dz_bf[:], dz_codes[:], dz_scales[:], E5M2)
-        u_all = keep.tile([P, (D_TILES - 1) * X + U_WINDOW], F32, align_bytes=64, tag="dz_then_u")
+        u_all = reused.tile([P, (D_TILES - 1) * X + U_WINDOW], F32, align_bytes=64, offset=4 * T)
         nc.gpsimd.memset(u_all[:, D_TILES * X :], 0.0)
+        windows.append(reused.tile([P, T], F32, name="window2", align_bytes=64, offset=0))
+        nc.gpsimd.memset(windows[2][:], 0.0)
         multiply(0)
 
-        ub = [keep.tile([P, C], F32, name="ub%d" % j)[:] for j in range(COPIED_TILES)]
-        picked = [keep.tile([P, C], F32, name="picked%d" % j, tag="picked%d" % j) for j in range(COPIED_TILES)]
+        ub = [keep.tile([P, C], F32, name="ub0", tag="ub0_then_window")[:], keep.tile([P, C], F32, name="ub1", tag="ub1_then_pieces")[:]]
+        picked = [keep.tile([P, C], F32, name="picked%d" % j, tag="picked%d" % j) for j in range(2)]
         de = []
         sums = []
         spent = keep.tile([P, BLOCKS, P], F32)
 
-        def gather_table(j):
-            nc.vector.tensor_copy(picked[j][:], table[j][:].indirect(idx_list[:]))
+        def gather_table(j, values, lo, hi):
+            nc.vector.tensor_copy(values, table[j][:].indirect(idx_list[:, lo // 16 : hi // 16]))
 
         def gather_u(j):
             window = u_all[:, u_start(j) : u_start(j) + U_WINDOW]
             nc.vector.tensor_copy(ub[j], window.indirect(bag_list[:]))
+
+        def weigh(j):
             nc.gpsimd.tensor_tensor(de[j], ub[j], wc_sb[:], MULT)
 
         def scatter(j):
-            window = windows[j % 2]
+            window = windows[j]
             nc.vector.tensor_copy(window[:].indirect(idx_list[:]), de[j])
             nc.sync.dma_start(out=out_0[j * P : (j + 1) * P, :], in_=window[:])
 
@@ -152,9 +155,9 @@ def tile_attend_gebag_kernel(tc, eT, W, dz, wc, offs, bagoffs, out_0, out_1):
                     stop=(j == D_TILES - 1),
                 )
 
-        def product(j):
-            nc.gpsimd.tensor_tensor(ub[j], ub[j], picked[j][:], MULT)
-            turn_and_add(j, ub[j], 0, C)
+        def product(j, values, columns, hi):
+            nc.gpsimd.tensor_tensor(values, ub[j][:, :hi], columns, MULT)
+            turn_and_add(j, values, 0, hi)
 
         def fused_product(j, values, lo, hi):
             nc.vector.tensor_tensor(values, table[j][:].indirect(idx_list[:, lo // 16 : hi // 16]), ub[j][:, lo:hi], MULT)
@@ -166,7 +169,7 @@ def tile_attend_gebag_kernel(tc, eT, W, dz, wc, offs, bagoffs, out_0, out_1):
         def sum_on_vector(b, column):
             nc.vector.tensor_reduce(out=column, in_=sums[b][:, :P], axis=mybir.AxisListType.X, op=ADD)
 
-        gather_table(0)
+        gather_table(0, picked[0][:], 0, C)
         cast(scalar_cast, w_bf_rest, w_raw_rest, 0, D - 2 * P)
         cast(gpsimd_cast, w_bf_rest, w_raw_rest, D - 2 * P, D - P)
         quantize(nc, w_bf_rest[:, :P, :], w_codes[:, P : 2 * P], w_scales[:, P : 2 * P], E4M3)
@@ -178,34 +181,41 @@ def tile_attend_gebag_kernel(tc, eT, W, dz, wc, offs, bagoffs, out_0, out_1):
         for b in range(BLOCKS):
             sums.append(psum.tile([P, X], F32, tag="bank", name="sums%d" % b))
 
-        def gather_piece(j, values, lo, hi):
-            nc.vector.tensor_copy(values, table[j][:].indirect(idx_list[:, lo // 16 : hi // 16]))
-            early.append((j, values, lo, hi))
-
-        early = []
         gather_u(0)
-        gather_table(1)
-        product(0)
-        held = [keep.tile([P, 2 * C + PIECE], F32, name="held0", tag="picked0")]
-        de.append(held[0][:, C + PIECE :])
-        de.append(keep.tile([P, C], F32, name="de2", tag="de2_then_picked")[:])
-        de.append(keep.tile([P, C], F32, name="de3")[:])
+        weigh(0)
+        gather_table(1, picked[1][:], 0, C)
+        product(0, ub[0], picked[0][:], C)
         gather_u(1)
-        product(1)
-        held.append(keep.tile([P, C + PIECE], F32, name="held1", tag="picked1"))
-        for j in range(COPIED_TILES):
-            scatter(j)
-            ub.append(held[j][:, :C])
-            gather_u(j + 2)
-            gather_piece(D_TILES - 2, held[j][:, C : C + PIECE], j * PIECE, (j + 1) * PIECE)
-        scatter(D_TILES - 2)
-        last_pieces = keep.tile([P, C], F32, tag="de2_then_picked")
-        gather_piece(D_TILES - 2, last_pieces[:, :PIECE], EARLY, MIDDLE)
-        gather_piece(D_TILES - 1, last_pieces[:, PIECE:], 0, MIDDLE)
-        for j, values, lo, hi in early:
-            prod_early = keep.tile([P, hi - lo], F32, name="prod_early%d_%d" % (j, lo))
-            nc.gpsimd.tensor_tensor(prod_early[:], values, ub[j][:, lo:hi], MULT)
-            turn_and_add(j, prod_early, lo, hi)
+        scatter(0)
+        windows.append(keep.tile([P, T], F32, name="window3", tag="ub0_then_window"))
+
+        after_0 = keep.tile([P, 2 * C], F32, tag="picked0")
+        de.append(after_0[:, :C])
+        ub.append(after_0[:, C:])
+        weigh(1)
+        product(1, ub[1], picked[1][:], C)
+        gather_u(2)
+        scatter(1)
+        nc.gpsimd.memset(windows[3][:], 0.0)
+
+        after_1 = keep.tile([P, 2 * C], F32, tag="picked1")
+        de.append(after_1[:, :C])
+        ub.append(after_1[:, C:])
+        weigh(2)
+        gather_u(3)
+        picked_2 = keep.tile([P, EARLY], F32, tag="ub1_then_pieces")
+        gather_table(2, picked_2[:], 0, EARLY)
+        scatter(2)
+        product(2, ub[2][:, :EARLY], picked_2[:], EARLY)
+
+        after_2 = keep.tile([P, C + EARLY], F32, tag="ub1_then_pieces")
+        de.append(after_2[:, :C])
+        weigh(3)
+        gather_table(3, after_2[:, C:], 0, EARLY)
+        scatter(3)
+        prod_3 = keep.tile([P, EARLY], F32, tag="last_products")
+        product(3, prod_3[:], after_2[:, C:], EARLY)
+
         early_blocks = EARLY // P
         for b in range(early_blocks):
             sum_on_scalar(b, dw_cols_early[:, b : b + 1])
@@ -215,9 +225,8 @@ def tile_attend_gebag_kernel(tc, eT, W, dz, wc, offs, bagoffs, out_0, out_1):
         nc.scalar.copy(out=dw_rows_early[:], in_=turned[:early_blocks, :P])
         nc.sync.dma_start(out=out_1[:, :EARLY].rearrange("o (b p) -> (o b) p", p=P), in_=dw_rows_early[:])
 
-        scatter(D_TILES - 1)
-        prod_late = keep.tile([P, C], F32, tag="window0")
-        pieces = [(D_TILES - 2, MIDDLE, C), (D_TILES - 1, MIDDLE, LAST), (D_TILES - 1, LAST, C)]
+        prod_late = keep.tile([P, 2 * (C - EARLY)], F32, tag="last_products")
+        pieces = [(D_TILES - 2, EARLY, C), (D_TILES - 1, EARLY, LAST), (D_TILES - 1, LAST, C)]
         filled = 0
         for j, lo, hi in pieces:
             fused_product(j, prod_late[:, filled : filled + hi - lo], lo, hi)
@@ -227,9 +236,10 @@ def tile_attend_gebag_kernel(tc, eT, W, dz, wc, offs, bagoffs, out_0, out_1):
             add_up = sum_on_vector if b == BLOCKS - 2 else sum_on_scalar
             add_up(b, dw_cols_late[:, at : at + 1])
 
+        late_blocks = BLOCKS - early_blocks
         dw_rows_late = keep.tile([P, P], F32, align_bytes=64)
         nc.vector.transpose(dw_rows_late[:], dw_cols_late[:])
         nc.sync.dma_start(
             out=out_1[:, EARLY:].rearrange("o (b q i) -> (o q) b i", q=P // SQUARE, i=SQUARE),
-            in_=dw_rows_late[0:P:SQUARE, :].rearrange("q (b i) -> q b i", i=SQUARE),
+            in_=dw_rows_late[0:P:SQUARE, : late_blocks * SQUARE].rearrange("q (b i) -> q b i", i=SQUARE),
         )

@@ -26,6 +26,8 @@ U_WINDOW = 1376
 DZ_VECTOR_SHARE = 336
 EARLY = C - 2 * P
 LAST = C - P
+HALF = C // 2
+SLOT = 4 * HALF
 ROUNDED_AT = 4 * T - 64
 
 
@@ -44,6 +46,7 @@ def tile_attend_gebag_kernel(tc, eT, W, dz, wc, offs, bagoffs, out_0, out_1):
     with ExitStack() as ctx:
         keep = ctx.enter_context(tc.tile_pool(name="keep", bufs=1))
         reused = ctx.enter_context(tc.tile_pool(name="reused", bufs=1))
+        links = ctx.enter_context(tc.tile_pool(name="links", bufs=1))
         psum = ctx.enter_context(tc.psum_pool(name="psum", bufs=8))
 
         W_rows = W.rearrange("(p t) c -> p t c", t=PACK)
@@ -123,27 +126,6 @@ def tile_attend_gebag_kernel(tc, eT, W, dz, wc, offs, bagoffs, out_0, out_1):
         nc.gpsimd.memset(windows[2][:], 0.0)
         multiply(0)
 
-        ub = [keep.tile([P, C], F32, name="ub0", tag="ub0_then_window")[:], keep.tile([P, C], F32, name="ub1", tag="ub1_then_pieces")[:]]
-        picked = [keep.tile([P, C], F32, name="picked%d" % j, tag="picked%d" % j) for j in range(2)]
-        de = []
-        sums = []
-        spent = keep.tile([P, BLOCKS, P], F32)
-
-        def gather_table(j, values, lo, hi):
-            nc.vector.tensor_copy(values, table[j][:].indirect(idx_list[:, lo // 16 : hi // 16]))
-
-        def gather_u(j):
-            window = u_all[:, u_start(j) : u_start(j) + U_WINDOW]
-            nc.vector.tensor_copy(ub[j], window.indirect(bag_list[:]))
-
-        def weigh(j):
-            nc.gpsimd.tensor_tensor(de[j], ub[j], wc_sb[:], MULT)
-
-        def scatter(j):
-            window = windows[j]
-            nc.vector.tensor_copy(window[:].indirect(idx_list[:]), de[j])
-            nc.sync.dma_start(out=out_0[j * P : (j + 1) * P, :], in_=window[:])
-
         def turn_and_add(j, values, lo, hi):
             for b in range(lo // P, hi // P):
                 nc.tensor.matmul(
@@ -155,66 +137,86 @@ def tile_attend_gebag_kernel(tc, eT, W, dz, wc, offs, bagoffs, out_0, out_1):
                     stop=(j == D_TILES - 1),
                 )
 
-        def product(j, values, columns, hi):
-            nc.gpsimd.tensor_tensor(values, ub[j][:, :hi], columns, MULT)
-            turn_and_add(j, values, 0, hi)
-
-        def fused_product(j, values, lo, hi):
-            nc.vector.tensor_tensor(values, table[j][:].indirect(idx_list[:, lo // 16 : hi // 16]), ub[j][:, lo:hi], MULT)
-            turn_and_add(j, values, lo, hi)
-
         def sum_on_scalar(b, column):
             nc.scalar.activation(out=spent[:, b, :], in_=sums[b][:, :P], func=COPY, accum_out=column)
 
         def sum_on_vector(b, column):
             nc.vector.tensor_reduce(out=column, in_=sums[b][:, :P], axis=mybir.AxisListType.X, op=ADD)
 
-        gather_table(0, picked[0][:], 0, C)
+        sums = []
+        spent = keep.tile([P, BLOCKS, P], F32)
+        link_at = [3 * SLOT * k for k in range(4)] + [3 * SLOT * 3 + 2 * SLOT * k for k in range(1, 5)]
+        picked, ub, de = {}, {}, {}
+
+        def slots(k):
+            j, h = divmod(k, 2)
+            return j, h * HALF, (EARLY if k in (5, 7) else (h + 1) * HALF)
+
+        def gather_table(k):
+            j, lo, hi = slots(k)
+            picked[k] = links.tile([P, 3 * HALF], F32, name="picked%d" % k, offset=link_at[k])
+            nc.vector.tensor_copy(picked[k][:, : hi - lo], table[j][:].indirect(idx_list[:, lo // 16 : hi // 16]))
+
+        def gather_u(k, values):
+            j, h = divmod(k, 2)
+            ub[k] = values
+            window = u_all[:, u_start(j) : u_start(j) + U_WINDOW]
+            nc.vector.tensor_copy(values[:], window.indirect(bag_list[:, h * HALF // 16 : (h + 1) * HALF // 16]))
+
+        def gather_u_behind(k, link):
+            gather_u(k, links.tile([P, HALF], F32, name="ub%d" % k, offset=link_at[link] + SLOT))
+
+        def weigh_and_scatter(k, values):
+            j, h = divmod(k, 2)
+            lo, hi = h * HALF, (h + 1) * HALF
+            nc.gpsimd.tensor_tensor(values[:], ub[k][:], wc_sb[:, lo:hi], MULT)
+            nc.vector.tensor_copy(windows[j][:].indirect(idx_list[:, lo // 16 : hi // 16]), values[:])
+            if h == 1:
+                nc.sync.dma_start(out=out_0[j * P : (j + 1) * P, :], in_=windows[j][:])
+
+        def product(k):
+            j, lo, hi = slots(k)
+            nc.gpsimd.tensor_tensor(ub[k][:, : hi - lo], ub[k][:, : hi - lo], picked[k][:, : hi - lo], MULT)
+            turn_and_add(j, ub[k], lo, hi)
+
+        def fused_product(j, values, lo, hi):
+            listed = table[j][:].indirect(idx_list[:, lo // 16 : hi // 16])
+            nc.vector.tensor_tensor(values, listed, ub[2 * j + 1][:, lo - HALF : hi - HALF], MULT)
+            turn_and_add(j, values, lo, hi)
+
+        gather_table(0)
+        gather_table(1)
         cast(scalar_cast, w_bf_rest, w_raw_rest, 0, D - 2 * P)
         cast(gpsimd_cast, w_bf_rest, w_raw_rest, D - 2 * P, D - P)
+        gather_u(0, keep.tile([P, HALF], F32, name="ub0", tag="ub0_then_window"))
+        gather_u(1, keep.tile([P, HALF], F32, name="ub1"))
         quantize(nc, w_bf_rest[:, :P, :], w_codes[:, P : 2 * P], w_scales[:, P : 2 * P], E4M3)
         quantize(nc, w_bf_rest[:, P:, :], w_codes[:, 2 * P :], w_scales[:, 2 * P :], E4M3)
         for j in range(1, D_TILES):
             multiply(j)
-
-        de.append(keep.tile([P, C], F32, name="de0", align_bytes=64, tag="weights_then_products")[:])
         for b in range(BLOCKS):
             sums.append(psum.tile([P, X], F32, tag="bank", name="sums%d" % b))
+        gather_table(2)
+        gather_table(3)
+        gather_u(2, keep.tile([P, HALF], F32, name="ub2"))
+        gather_u(3, keep.tile([P, HALF], F32, name="ub3"))
 
-        gather_u(0)
-        weigh(0)
-        gather_table(1, picked[1][:], 0, C)
-        product(0, ub[0], picked[0][:], C)
-        gather_u(1)
-        scatter(0)
-        windows.append(keep.tile([P, T], F32, name="window3", tag="ub0_then_window"))
-
-        after_0 = keep.tile([P, 2 * C], F32, tag="picked0")
-        de.append(after_0[:, :C])
-        ub.append(after_0[:, C:])
-        weigh(1)
-        product(1, ub[1], picked[1][:], C)
-        gather_u(2)
-        scatter(1)
-        nc.gpsimd.memset(windows[3][:], 0.0)
-
-        after_1 = keep.tile([P, 2 * C], F32, tag="picked1")
-        de.append(after_1[:, :C])
-        ub.append(after_1[:, C:])
-        weigh(2)
-        gather_u(3)
-        picked_2 = keep.tile([P, EARLY], F32, tag="ub1_then_pieces")
-        gather_table(2, picked_2[:], 0, EARLY)
-        scatter(2)
-        product(2, ub[2][:, :EARLY], picked_2[:], EARLY)
-
-        after_2 = keep.tile([P, C + EARLY], F32, tag="ub1_then_pieces")
-        de.append(after_2[:, :C])
-        weigh(3)
-        gather_table(3, after_2[:, C:], 0, EARLY)
-        scatter(3)
-        prod_3 = keep.tile([P, EARLY], F32, tag="last_products")
-        product(3, prod_3[:], after_2[:, C:], EARLY)
+        u_behind = {0: 4, 1: 5, 2: 6, 4: 7}
+        table_behind = {3: 4, 4: 5, 5: 6, 6: 7}
+        for k in range(2 * D_TILES):
+            if k == 0:
+                values = keep.tile([P, HALF], F32, name="de0", align_bytes=64, tag="weights_then_products")
+            else:
+                values = links.tile([P, HALF], F32, name="de%d" % k, offset=link_at[k - 1])
+            weigh_and_scatter(k, values)
+            product(k)
+            if k in u_behind:
+                gather_u_behind(u_behind[k], k)
+            if k in table_behind:
+                gather_table(table_behind[k])
+            if k == 1:
+                windows.append(keep.tile([P, T], F32, name="window3", tag="ub0_then_window"))
+                nc.gpsimd.memset(windows[3][:], 0.0)
 
         early_blocks = EARLY // P
         for b in range(early_blocks):
@@ -223,9 +225,9 @@ def tile_attend_gebag_kernel(tc, eT, W, dz, wc, offs, bagoffs, out_0, out_1):
         nc.tensor.transpose(turned[:, :P], dw_cols_early[:], ident[:])
         dw_rows_early = keep.tile([early_blocks, P], F32)
         nc.scalar.copy(out=dw_rows_early[:], in_=turned[:early_blocks, :P])
-        nc.sync.dma_start(out=out_1[:, :EARLY].rearrange("o (b p) -> (o b) p", p=P), in_=dw_rows_early[:])
+        nc.scalar.dma_start(out=out_1[:, :EARLY].rearrange("o (b p) -> (o b) p", p=P), in_=dw_rows_early[:])
 
-        prod_late = keep.tile([P, 2 * (C - EARLY)], F32, tag="last_products")
+        prod_late = links.tile([P, 2 * (C - EARLY)], F32, offset=link_at[7])
         pieces = [(D_TILES - 2, EARLY, C), (D_TILES - 1, EARLY, LAST), (D_TILES - 1, LAST, C)]
         filled = 0
         for j, lo, hi in pieces:

@@ -163,6 +163,10 @@ def tile_attend_gebag_kernel(tc, eT, W, dz, wc, offs, bagoffs, out_0, out_1):
             window = u_all[:, u_start(j) : u_start(j) + U_WINDOW]
             nc.vector.tensor_copy(values[:], window.indirect(bag_list[:, h * HALF // 16 : (h + 1) * HALF // 16]))
 
+        def gather_u_whole(j, values):
+            ub[2 * j], ub[2 * j + 1] = values[:, :HALF], values[:, HALF:]
+            nc.vector.tensor_copy(values[:], u_all[:, u_start(j) : u_start(j) + U_WINDOW].indirect(bag_list[:]))
+
         def gather_u_behind(k, link):
             gather_u(k, links.tile([P, HALF], F32, name="ub%d" % k, offset=link_at[link] + SLOT))
 
@@ -188,8 +192,7 @@ def tile_attend_gebag_kernel(tc, eT, W, dz, wc, offs, bagoffs, out_0, out_1):
         gather_table(1)
         cast(scalar_cast, w_bf_rest, w_raw_rest, 0, D - 2 * P)
         cast(gpsimd_cast, w_bf_rest, w_raw_rest, D - 2 * P, D - P)
-        gather_u(0, keep.tile([P, HALF], F32, name="ub0", tag="ub0_then_window"))
-        gather_u(1, keep.tile([P, HALF], F32, name="ub1"))
+        gather_u_whole(0, keep.tile([P, C], F32, name="ub_0", tag="ub0_then_window"))
         quantize(nc, w_bf_rest[:, :P, :], w_codes[:, P : 2 * P], w_scales[:, P : 2 * P], E4M3)
         quantize(nc, w_bf_rest[:, P:, :], w_codes[:, 2 * P :], w_scales[:, 2 * P :], E4M3)
         for j in range(1, D_TILES):
@@ -198,8 +201,7 @@ def tile_attend_gebag_kernel(tc, eT, W, dz, wc, offs, bagoffs, out_0, out_1):
             sums.append(psum.tile([P, X], F32, tag="bank", name="sums%d" % b))
         gather_table(2)
         gather_table(3)
-        gather_u(2, keep.tile([P, HALF], F32, name="ub2"))
-        gather_u(3, keep.tile([P, HALF], F32, name="ub3"))
+        gather_u_whole(1, keep.tile([P, C], F32, name="ub_1"))
 
         u_behind = {0: 4, 1: 5, 2: 6, 4: 7}
         table_behind = {3: 4, 4: 5, 5: 6, 6: 7}
@@ -214,18 +216,18 @@ def tile_attend_gebag_kernel(tc, eT, W, dz, wc, offs, bagoffs, out_0, out_1):
                 gather_u_behind(u_behind[k], k)
             if k in table_behind:
                 gather_table(table_behind[k])
-            if k == 1:
+            if k == 2:
                 windows.append(keep.tile([P, T], F32, name="window3", tag="ub0_then_window"))
                 nc.gpsimd.memset(windows[3][:], 0.0)
 
-        early_blocks = EARLY // P
+        early_blocks = HALF // P
         for b in range(early_blocks):
             sum_on_scalar(b, dw_cols_early[:, b : b + 1])
         turned = psum.tile([P, X], F32, tag="bank")
         nc.tensor.transpose(turned[:, :P], dw_cols_early[:], ident[:])
         dw_rows_early = keep.tile([early_blocks, P], F32)
         nc.scalar.copy(out=dw_rows_early[:], in_=turned[:early_blocks, :P])
-        nc.scalar.dma_start(out=out_1[:, :EARLY].rearrange("o (b p) -> (o b) p", p=P), in_=dw_rows_early[:])
+        nc.scalar.dma_start(out=out_1[:, :HALF].rearrange("o (b p) -> (o b) p", p=P), in_=dw_rows_early[:])
 
         prod_late = links.tile([P, 2 * (C - EARLY)], F32, offset=link_at[7])
         pieces = [(D_TILES - 2, EARLY, C), (D_TILES - 1, EARLY, LAST), (D_TILES - 1, LAST, C)]
@@ -242,6 +244,6 @@ def tile_attend_gebag_kernel(tc, eT, W, dz, wc, offs, bagoffs, out_0, out_1):
         dw_rows_late = keep.tile([P, P], F32, align_bytes=64)
         nc.vector.transpose(dw_rows_late[:], dw_cols_late[:])
         nc.sync.dma_start(
-            out=out_1[:, EARLY:].rearrange("o (b q i) -> (o q) b i", q=P // SQUARE, i=SQUARE),
+            out=out_1[:, HALF:].rearrange("o (b q i) -> (o q) b i", q=P // SQUARE, i=SQUARE),
             in_=dw_rows_late[0:P:SQUARE, : late_blocks * SQUARE].rearrange("q (b i) -> q b i", i=SQUARE),
         )

@@ -27,7 +27,11 @@ DZ_VECTOR_SHARE = 336
 EARLY = C - 2 * P
 LAST = C - P
 HALF = C // 2
-SLOT = 4 * HALF
+CUTS = 4
+PIECE = C // CUTS
+PIECES = D_TILES * CUTS
+SLOT = 4 * PIECE
+LANE = 7
 ROUNDED_AT = 4 * T - 64
 
 
@@ -57,7 +61,7 @@ def tile_attend_gebag_kernel(tc, eT, W, dz, wc, offs, bagoffs, out_0, out_1):
         w_raw_rest = keep.tile([P, PACK, D - P], F32)
         bag_list = keep.tile([P, C // 16], U16)
         idx_list = keep.tile([P, C // 16], U16)
-        wc_sb = keep.tile([P, C], F32)
+        wc_sb = [keep.tile([P, PIECE], F32, name="wc%d" % h, tag="wc%d" % h) for h in range(CUTS)]
         table = [keep.tile([P, T], F32, name="table%d" % j) for j in range(D_TILES)]
 
         nc.sync.dma_start(out=w_raw_0[:], in_=W_rows[:, :, :P])
@@ -67,9 +71,10 @@ def tile_attend_gebag_kernel(tc, eT, W, dz, wc, offs, bagoffs, out_0, out_1):
         nc.sync.dma_start(bag_list[:], bagoffs)
         nc.sync.dma_start(out=w_raw_rest[:], in_=W_rows[:, :, P:])
         nc.sync.dma_start(out=table[1][:], in_=eT[P : 2 * P, :])
-        nc.sync.dma_start(out=wc_sb[:], in_=wc)
-        for j in range(2, D_TILES):
-            nc.sync.dma_start(out=table[j][:], in_=eT[j * P : (j + 1) * P, :])
+        nc.sync.dma_start(out=table[2][:], in_=eT[2 * P : 3 * P, :])
+        for h in range(CUTS):
+            nc.sync.dma_start(out=wc_sb[h][:], in_=wc[:, h * PIECE : (h + 1) * PIECE])
+        nc.sync.dma_start(out=table[3][:], in_=eT[3 * P :, :])
 
         windows = [keep.tile([P, T], F32, name="window%d" % h, tag="window%d" % h) for h in range(2)]
         for window in windows:
@@ -86,7 +91,7 @@ def tile_attend_gebag_kernel(tc, eT, W, dz, wc, offs, bagoffs, out_0, out_1):
         w_codes = keep.tile([P, D], U32, align_bytes=64)
         w_scales = keep.tile([P, D], U8, align_bytes=64)
         w_bf_0 = reused.tile([P, P, PACK], BF16, align_bytes=64, offset=ROUNDED_AT)
-        w_bf_rest = keep.tile([P, D - P, PACK], BF16, align_bytes=64, tag="weights_then_products")
+        w_bf_rest = links.tile([P, D - P, PACK], BF16, align_bytes=64, offset=0)
 
         def cast(engine_copy, grouped, raw, lo, hi):
             dst, src = interleave_views(grouped, raw, lo, hi)
@@ -145,51 +150,38 @@ def tile_attend_gebag_kernel(tc, eT, W, dz, wc, offs, bagoffs, out_0, out_1):
 
         sums = []
         spent = keep.tile([P, BLOCKS, P], F32)
-        link_at = [3 * SLOT * k for k in range(4)] + [3 * SLOT * 3 + 2 * SLOT * k for k in range(1, 5)]
-        picked, ub, de = {}, {}, {}
+        picked, picked_at, ub = {}, {}, {}
 
-        def slots(k):
-            j, h = divmod(k, 2)
-            return j, h * HALF, (EARLY if k in (5, 7) else (h + 1) * HALF)
+        def span(k):
+            j, h = divmod(k, CUTS)
+            return j, h * PIECE, (h + 1) * PIECE
 
-        def gather_table(k):
-            j, lo, hi = slots(k)
-            picked[k] = links.tile([P, 3 * HALF], F32, name="picked%d" % k, offset=link_at[k])
-            nc.vector.tensor_copy(picked[k][:, : hi - lo], table[j][:].indirect(idx_list[:, lo // 16 : hi // 16]))
+        def listed(j, lo, hi):
+            return table[j][:].indirect(idx_list[:, lo // 16 : hi // 16])
 
-        def gather_u(k, values):
-            j, h = divmod(k, 2)
-            ub[k] = values
-            window = u_all[:, u_start(j) : u_start(j) + U_WINDOW]
-            nc.vector.tensor_copy(values[:], window.indirect(bag_list[:, h * HALF // 16 : (h + 1) * HALF // 16]))
+        def bagged(j, lo, hi):
+            return u_all[:, u_start(j) : u_start(j) + U_WINDOW].indirect(bag_list[:, lo // 16 : hi // 16])
+
+        def placed(name, slot, columns):
+            return links.tile([P, columns], F32, name=name, offset=slot * SLOT)
+
+        def gather_table(k, slot):
+            picked_at[k] = slot
+            picked[k] = placed("picked%d" % k, slot, 3 * PIECE)[:, :PIECE]
+            nc.vector.tensor_copy(picked[k], listed(*span(k)))
 
         def gather_u_whole(j, values):
-            ub[2 * j], ub[2 * j + 1] = values[:, :HALF], values[:, HALF:]
-            nc.vector.tensor_copy(values[:], u_all[:, u_start(j) : u_start(j) + U_WINDOW].indirect(bag_list[:]))
+            for h in range(CUTS):
+                ub[j * CUTS + h] = values[:, h * PIECE : (h + 1) * PIECE]
+            nc.vector.tensor_copy(values[:], bagged(j, 0, C))
 
-        def gather_u_behind(k, link):
-            gather_u(k, links.tile([P, HALF], F32, name="ub%d" % k, offset=link_at[link] + SLOT))
-
-        def weigh_and_scatter(k, values):
-            j, h = divmod(k, 2)
-            lo, hi = h * HALF, (h + 1) * HALF
-            nc.gpsimd.tensor_tensor(values[:], ub[k][:], wc_sb[:, lo:hi], MULT)
-            nc.vector.tensor_copy(windows[j][:].indirect(idx_list[:, lo // 16 : hi // 16]), values[:])
-            if h == 1:
-                nc.sync.dma_start(out=out_0[j * P : (j + 1) * P, :], in_=windows[j][:])
-
-        def product(k):
-            j, lo, hi = slots(k)
-            nc.gpsimd.tensor_tensor(ub[k][:, : hi - lo], ub[k][:, : hi - lo], picked[k][:, : hi - lo], MULT)
-            turn_and_add(j, ub[k], lo, hi)
-
-        def fused_product(j, values, lo, hi):
-            listed = table[j][:].indirect(idx_list[:, lo // 16 : hi // 16])
-            nc.vector.tensor_tensor(values, listed, ub[2 * j + 1][:, lo - HALF : hi - HALF], MULT)
+        def product(k, values):
+            j, lo, hi = span(k)
+            nc.gpsimd.tensor_tensor(values[:], ub[k], picked[k], MULT)
             turn_and_add(j, values, lo, hi)
 
-        gather_table(0)
-        gather_table(1)
+        for k in range(CUTS):
+            gather_table(k, LANE * (k + 1))
         cast(scalar_cast, w_bf_rest, w_raw_rest, 0, D - 2 * P)
         cast(gpsimd_cast, w_bf_rest, w_raw_rest, D - 2 * P, D - P)
         gather_u_whole(0, keep.tile([P, C], F32, name="ub_0", tag="ub0_then_window"))
@@ -199,26 +191,54 @@ def tile_attend_gebag_kernel(tc, eT, W, dz, wc, offs, bagoffs, out_0, out_1):
             multiply(j)
         for b in range(BLOCKS):
             sums.append(psum.tile([P, X], F32, tag="bank", name="sums%d" % b))
-        gather_table(2)
-        gather_table(3)
+        for k in range(CUTS, 2 * CUTS - 1):
+            gather_table(k, LANE * (k + 1))
         gather_u_whole(1, keep.tile([P, C], F32, name="ub_1"))
 
-        u_behind = {0: 4, 1: 5, 2: 6, 4: 7}
-        table_behind = {3: 4, 4: 5, 5: 6, 6: 7}
-        for k in range(2 * D_TILES):
-            if k == 0:
-                values = keep.tile([P, HALF], F32, name="de0", align_bytes=64, tag="weights_then_products")
+        late = (3 * CUTS - 1, PIECES - 1)
+        products = [k for k in range(PIECES) if k not in late]
+        to_gather = [(listed, 2 * CUTS - 1)]
+        for k in range(2 * CUTS, PIECES):
+            to_gather.append((bagged, k))
+            if k not in late:
+                to_gather.append((listed, k))
+        to_gather.append(to_gather.pop(-2))
+
+        free = 0
+        for k in range(PIECES):
+            j, lo, hi = span(k)
+            chained = k < len(products) - 1
+            if k < len(products):
+                de = placed("de%d" % k, free, PIECE)
             else:
-                values = links.tile([P, HALF], F32, name="de%d" % k, offset=link_at[k - 1])
-            weigh_and_scatter(k, values)
-            product(k)
-            if k in u_behind:
-                gather_u_behind(u_behind[k], k)
-            if k in table_behind:
-                gather_table(table_behind[k])
-            if k == 2:
+                de = keep.tile([P, PIECE], F32, name="de%d" % k)
+            nc.gpsimd.tensor_tensor(de[:], ub[k], wc_sb[k % CUTS][:], MULT)
+            nc.vector.tensor_copy(windows[j][:].indirect(idx_list[:, lo // 16 : hi // 16]), de[:])
+            if hi == C:
+                nc.sync.dma_start(out=out_0[j * P : (j + 1) * P, :], in_=windows[j][:])
+            if chained:
+                product(products[k], placed("prod%d" % k, free + 1, PIECE))
+                free = picked_at[products[k]]
+            if k < len(to_gather):
+                source, later = to_gather[k]
+                if chained and source is listed:
+                    gather_table(later, free + 2)
+                else:
+                    if chained:
+                        values = placed("ub%d" % later, free + 2, PIECE)
+                    else:
+                        values = keep.tile([P, PIECE], F32, name="gathered%d" % k, tag="wc%d" % (k % CUTS))
+                    (ub if source is bagged else picked)[later] = values[:]
+                    nc.vector.tensor_copy(values[:], source(*span(later)))
+            if k == CUTS:
                 windows.append(keep.tile([P, T], F32, name="window3", tag="ub0_then_window"))
                 nc.gpsimd.memset(windows[3][:], 0.0)
+        product(products[-1], keep.tile([P, PIECE], F32, name="prod_last"))
+
+        def fused_product(j, values, lo, hi):
+            at = (CUTS - 1) * PIECE
+            nc.vector.tensor_tensor(values, listed(j, lo, hi), ub[(j + 1) * CUTS - 1][:, lo - at : hi - at], MULT)
+            turn_and_add(j, values, lo, hi)
 
         early_blocks = HALF // P
         for b in range(early_blocks):
@@ -229,7 +249,7 @@ def tile_attend_gebag_kernel(tc, eT, W, dz, wc, offs, bagoffs, out_0, out_1):
         nc.scalar.copy(out=dw_rows_early[:], in_=turned[:early_blocks, :P])
         nc.scalar.dma_start(out=out_1[:, :HALF].rearrange("o (b p) -> (o b) p", p=P), in_=dw_rows_early[:])
 
-        prod_late = links.tile([P, 2 * (C - EARLY)], F32, offset=link_at[7])
+        prod_late = keep.tile([P, 2 * (C - EARLY)], F32, tag="wc%d" % (CUTS - 1))
         pieces = [(D_TILES - 2, EARLY, C), (D_TILES - 1, EARLY, LAST), (D_TILES - 1, LAST, C)]
         filled = 0
         for j, lo, hi in pieces:

@@ -177,7 +177,7 @@ def tile_attend_gebag_kernel(tc, eT, W, dz, wc, offs, bagoffs, out_0, out_1):
 
         def product(k, values):
             j, lo, hi = span(k)
-            nc.gpsimd.tensor_tensor(values[:], ub[k], picked[k], MULT)
+            nc.gpsimd.tensor_tensor(values, ub[k], picked[k], MULT)
             turn_and_add(j, values, lo, hi)
 
         for k in range(CUTS):
@@ -217,7 +217,7 @@ def tile_attend_gebag_kernel(tc, eT, W, dz, wc, offs, bagoffs, out_0, out_1):
             if hi == C:
                 nc.sync.dma_start(out=out_0[j * P : (j + 1) * P, :], in_=windows[j][:])
             if chained:
-                product(products[k], placed("prod%d" % k, free + 1, PIECE))
+                product(products[k], ub[k] if products[k] == k else placed("prod%d" % k, free + 1, PIECE)[:])
                 free = picked_at[products[k]]
             if k < len(to_gather):
                 source, later = to_gather[k]
@@ -233,7 +233,7 @@ def tile_attend_gebag_kernel(tc, eT, W, dz, wc, offs, bagoffs, out_0, out_1):
             if k == CUTS:
                 windows.append(keep.tile([P, T], F32, name="window3", tag="ub0_then_window"))
                 nc.gpsimd.memset(windows[3][:], 0.0)
-        product(products[-1], keep.tile([P, PIECE], F32, name="prod_last"))
+        product(products[-1], keep.tile([P, PIECE], F32, name="prod_last")[:])
 
         def fused_product(j, values, lo, hi):
             at = (CUTS - 1) * PIECE

@@ -31,7 +31,8 @@ CUTS = 4
 PIECE = C // CUTS
 PIECES = D_TILES * CUTS
 SLOT = 4 * PIECE
-LANE = 7
+LANE = 8
+WEIGHTS_AT = LANE * (2 * CUTS + 1)
 ROUNDED_AT = 4 * T - 64
 
 
@@ -61,7 +62,8 @@ def tile_attend_gebag_kernel(tc, eT, W, dz, wc, offs, bagoffs, out_0, out_1):
         w_raw_rest = keep.tile([P, PACK, D - P], F32)
         bag_list = keep.tile([P, C // 16], U16)
         idx_list = keep.tile([P, C // 16], U16)
-        wc_sb = [keep.tile([P, PIECE], F32, name="wc%d" % h, tag="wc%d" % h) for h in range(CUTS)]
+        wc_again = links.tile([P, PIECE], F32, offset=4 * T + WEIGHTS_AT * SLOT)
+        wc_sb = keep.tile([P, C], F32)
         table = [keep.tile([P, T], F32, name="table%d" % j) for j in range(D_TILES)]
 
         nc.sync.dma_start(out=w_raw_0[:], in_=W_rows[:, :, :P])
@@ -72,9 +74,9 @@ def tile_attend_gebag_kernel(tc, eT, W, dz, wc, offs, bagoffs, out_0, out_1):
         nc.sync.dma_start(out=w_raw_rest[:], in_=W_rows[:, :, P:])
         nc.sync.dma_start(out=table[1][:], in_=eT[P : 2 * P, :])
         nc.sync.dma_start(out=table[2][:], in_=eT[2 * P : 3 * P, :])
-        for h in range(CUTS):
-            nc.sync.dma_start(out=wc_sb[h][:], in_=wc[:, h * PIECE : (h + 1) * PIECE])
+        nc.sync.dma_start(out=wc_sb[:], in_=wc)
         nc.sync.dma_start(out=table[3][:], in_=eT[3 * P :, :])
+        nc.sync.dma_start(out=wc_again[:], in_=wc[:, :PIECE])
 
         windows = [keep.tile([P, T], F32, name="window%d" % h, tag="window%d" % h) for h in range(2)]
         for window in windows:
@@ -91,7 +93,7 @@ def tile_attend_gebag_kernel(tc, eT, W, dz, wc, offs, bagoffs, out_0, out_1):
         w_codes = keep.tile([P, D], U32, align_bytes=64)
         w_scales = keep.tile([P, D], U8, align_bytes=64)
         w_bf_0 = reused.tile([P, P, PACK], BF16, align_bytes=64, offset=ROUNDED_AT)
-        w_bf_rest = links.tile([P, D - P, PACK], BF16, align_bytes=64, offset=0)
+        w_bf_rest = links.tile([P, D - P, PACK], BF16, align_bytes=64, offset=ROUNDED_AT)
 
         def cast(engine_copy, grouped, raw, lo, hi):
             dst, src = interleave_views(grouped, raw, lo, hi)
@@ -163,11 +165,11 @@ def tile_attend_gebag_kernel(tc, eT, W, dz, wc, offs, bagoffs, out_0, out_1):
             return u_all[:, u_start(j) : u_start(j) + U_WINDOW].indirect(bag_list[:, lo // 16 : hi // 16])
 
         def placed(name, slot, columns):
-            return links.tile([P, columns], F32, name=name, offset=slot * SLOT)
+            return links.tile([P, columns], F32, name=name, offset=4 * T + slot * SLOT)
 
         def gather_table(k, slot):
             picked_at[k] = slot
-            picked[k] = placed("picked%d" % k, slot, 3 * PIECE)[:, :PIECE]
+            picked[k] = placed("picked%d" % k, slot, (4 if k == 0 else 3) * PIECE)[:, :PIECE]
             nc.vector.tensor_copy(picked[k], listed(*span(k)))
 
         def gather_u_whole(j, values):
@@ -184,56 +186,58 @@ def tile_attend_gebag_kernel(tc, eT, W, dz, wc, offs, bagoffs, out_0, out_1):
             gather_table(k, LANE * (k + 1))
         cast(scalar_cast, w_bf_rest, w_raw_rest, 0, D - 2 * P)
         cast(gpsimd_cast, w_bf_rest, w_raw_rest, D - 2 * P, D - P)
-        gather_u_whole(0, keep.tile([P, C], F32, name="ub_0", tag="ub0_then_window"))
+        ub_0 = keep.tile([P, C], F32)
+        gather_u_whole(0, ub_0)
         quantize(nc, w_bf_rest[:, :P, :], w_codes[:, P : 2 * P], w_scales[:, P : 2 * P], E4M3)
         quantize(nc, w_bf_rest[:, P:, :], w_codes[:, 2 * P :], w_scales[:, 2 * P :], E4M3)
         for j in range(1, D_TILES):
             multiply(j)
         for b in range(BLOCKS):
             sums.append(psum.tile([P, X], F32, tag="bank", name="sums%d" % b))
-        for k in range(CUTS, 2 * CUTS - 1):
+        for k in range(CUTS, 2 * CUTS):
             gather_table(k, LANE * (k + 1))
         gather_u_whole(1, keep.tile([P, C], F32, name="ub_1"))
 
         late = (3 * CUTS - 1, PIECES - 1)
-        products = [k for k in range(PIECES) if k not in late]
-        to_gather = [(listed, 2 * CUTS - 1)]
-        for k in range(2 * CUTS, PIECES):
-            to_gather.append((bagged, k))
-            if k not in late:
-                to_gather.append((listed, k))
-        to_gather.append(to_gather.pop(-2))
+        to_gather = [(2 * k - 3, bagged, k) for k in range(2 * CUTS, PIECES)]
+        to_gather += [(2 * k, listed, k) for k in range(2 * CUTS, PIECES) if k not in late]
+        to_gather.sort(key=lambda entry: entry[0])
+        windows.append(links.tile([P, T], F32, name="window3", offset=0))
+        nc.gpsimd.memset(windows[3][:], 0.0)
 
-        free = 0
-        for k in range(PIECES):
+        def weigh(k, values):
             j, lo, hi = span(k)
-            chained = k < len(products) - 1
-            if k < len(products):
-                de = placed("de%d" % k, free, PIECE)
-            else:
-                de = keep.tile([P, PIECE], F32, name="de%d" % k)
-            nc.gpsimd.tensor_tensor(de[:], ub[k], wc_sb[k % CUTS][:], MULT)
-            nc.vector.tensor_copy(windows[j][:].indirect(idx_list[:, lo // 16 : hi // 16]), de[:])
+            weights = wc_again[:] if k - 1 == late[0] else wc_sb[:, lo:hi]
+            nc.gpsimd.tensor_tensor(values, ub[k], weights, MULT)
+
+        def scatter(j, lo, hi, values):
+            nc.vector.tensor_copy(windows[j][:].indirect(idx_list[:, lo // 16 : hi // 16]), values)
             if hi == C:
                 nc.sync.dma_start(out=out_0[j * P : (j + 1) * P, :], in_=windows[j][:])
-            if chained:
-                product(products[k], ub[k] if products[k] == k else placed("prod%d" % k, free + 1, PIECE)[:])
-                free = picked_at[products[k]]
-            if k < len(to_gather):
-                source, later = to_gather[k]
-                if chained and source is listed:
-                    gather_table(later, free + 2)
+
+        first_two = placed("first_two", 0, 2 * PIECE)
+        nc.gpsimd.tensor_tensor(first_two[:], ub_0[:, : 2 * PIECE], wc_sb[:, : 2 * PIECE], MULT)
+        scatter(0, 0, 2 * PIECE, first_two[:])
+        for k in range(1, PIECES):
+            if k >= 2:
+                if k == 2 or k == PIECES - 1:
+                    de = placed("de%d" % k, picked_at[k - 2] + 1, PIECE)
+                elif k - 3 in late:
+                    de = placed("de%d" % k, picked_at[k - 4] + 1, PIECE)
                 else:
-                    if chained:
-                        values = placed("ub%d" % later, free + 2, PIECE)
-                    else:
-                        values = keep.tile([P, PIECE], F32, name="gathered%d" % k, tag="wc%d" % (k % CUTS))
-                    (ub if source is bagged else picked)[later] = values[:]
-                    nc.vector.tensor_copy(values[:], source(*span(later)))
-            if k == CUTS:
-                windows.append(keep.tile([P, T], F32, name="window3", tag="ub0_then_window"))
-                nc.gpsimd.memset(windows[3][:], 0.0)
-        product(products[-1], keep.tile([P, PIECE], F32, name="prod_last")[:])
+                    de = placed("de%d" % k, picked_at[k - 3], PIECE)
+                weigh(k, de[:])
+                scatter(*span(k), de[:])
+            if k - 1 in picked:
+                product(k - 1, placed("prod1", picked_at[0] + 3, PIECE)[:] if k == 2 else ub[k - 1])
+            if k - 1 < len(to_gather):
+                source, later = to_gather[k - 1][1:]
+                slot = picked_at[k - 1] + 2 if k - 1 in picked else WEIGHTS_AT
+                if source is listed:
+                    gather_table(later, slot)
+                else:
+                    ub[later] = placed("ub%d" % later, slot, PIECE)[:]
+                    nc.vector.tensor_copy(ub[later], bagged(*span(later)))
 
         def fused_product(j, values, lo, hi):
             at = (CUTS - 1) * PIECE
@@ -249,7 +253,7 @@ def tile_attend_gebag_kernel(tc, eT, W, dz, wc, offs, bagoffs, out_0, out_1):
         nc.scalar.copy(out=dw_rows_early[:], in_=turned[:early_blocks, :P])
         nc.scalar.dma_start(out=out_1[:, :HALF].rearrange("o (b p) -> (o b) p", p=P), in_=dw_rows_early[:])
 
-        prod_late = keep.tile([P, 2 * (C - EARLY)], F32, tag="wc%d" % (CUTS - 1))
+        prod_late = placed("prod_late", picked_at[PIECES - 2], 2 * (C - EARLY))
         pieces = [(D_TILES - 2, EARLY, C), (D_TILES - 1, EARLY, LAST), (D_TILES - 1, LAST, C)]
         filled = 0
         for j, lo, hi in pieces:

@@ -76,7 +76,7 @@ def tile_attend_gebag_kernel(tc, eT, W, dz, wc, offs, bagoffs, out_0, out_1):
         nc.sync.dma_start(out=table[2][:], in_=eT[2 * P : 3 * P, :])
         nc.sync.dma_start(out=wc_sb[:], in_=wc)
         nc.sync.dma_start(out=table[3][:], in_=eT[3 * P :, :])
-        nc.sync.dma_start(out=wc_again[:], in_=wc[:, :PIECE])
+        nc.sync.dma_start(out=wc_again[:], in_=wc[:, HALF:EARLY])
 
         windows = [keep.tile([P, T], F32, name="window%d" % h, tag="window%d" % h) for h in range(2)]
         for window in windows:
@@ -199,15 +199,16 @@ def tile_attend_gebag_kernel(tc, eT, W, dz, wc, offs, bagoffs, out_0, out_1):
         gather_u_whole(1, keep.tile([P, C], F32, name="ub_1"))
 
         late = (3 * CUTS - 1, PIECES - 1)
-        to_gather = [(2 * k - 3, bagged, k) for k in range(2 * CUTS, PIECES)]
-        to_gather += [(2 * k, listed, k) for k in range(2 * CUTS, PIECES) if k not in late]
+        order = [0, 1, 4, 2, 5, 3, 6, 8, 7, 9, 12, 10, 13, 11, 14, 15]
+        to_gather = [(2 * order.index(k) - 3, bagged, k) for k in range(2 * CUTS, PIECES)]
+        to_gather += [(2 * order.index(k), listed, k) for k in range(2 * CUTS, PIECES) if k not in late]
         to_gather.sort(key=lambda entry: entry[0])
         windows.append(links.tile([P, T], F32, name="window3", offset=0))
         nc.gpsimd.memset(windows[3][:], 0.0)
 
         def weigh(k, values):
             j, lo, hi = span(k)
-            weights = wc_again[:] if k - 1 == late[0] else wc_sb[:, lo:hi]
+            weights = wc_again[:] if k == PIECES - 2 else wc_sb[:, lo:hi]
             nc.gpsimd.tensor_tensor(values, ub[k], weights, MULT)
 
         def scatter(j, lo, hi, values):
@@ -218,21 +219,17 @@ def tile_attend_gebag_kernel(tc, eT, W, dz, wc, offs, bagoffs, out_0, out_1):
         first_two = placed("first_two", 0, 2 * PIECE)
         nc.gpsimd.tensor_tensor(first_two[:], ub_0[:, : 2 * PIECE], wc_sb[:, : 2 * PIECE], MULT)
         scatter(0, 0, 2 * PIECE, first_two[:])
-        for k in range(1, PIECES):
-            if k >= 2:
-                if k == 2 or k == PIECES - 1:
-                    de = placed("de%d" % k, picked_at[k - 2] + 1, PIECE)
-                elif k - 3 in late:
-                    de = placed("de%d" % k, picked_at[k - 4] + 1, PIECE)
-                else:
-                    de = placed("de%d" % k, picked_at[k - 3], PIECE)
+        for at in range(1, PIECES):
+            k, before = order[at], order[at - 1]
+            if at >= 2:
+                de = placed("de%d" % k, picked_at[0] + 1 if at == 2 else picked_at[order[at - 3]], PIECE)
                 weigh(k, de[:])
                 scatter(*span(k), de[:])
-            if k - 1 in picked:
-                product(k - 1, placed("prod1", picked_at[0] + 3, PIECE)[:] if k == 2 else ub[k - 1])
-            if k - 1 < len(to_gather):
-                source, later = to_gather[k - 1][1:]
-                slot = picked_at[k - 1] + 2 if k - 1 in picked else WEIGHTS_AT
+            if before in picked:
+                product(before, placed("prod1", picked_at[0] + 3, PIECE)[:] if at == 2 else ub[before])
+            if at - 1 < len(to_gather):
+                source, later = to_gather[at - 1][1:]
+                slot = picked_at[before] + 2 if before in picked else WEIGHTS_AT
                 if source is listed:
                     gather_table(later, slot)
                 else:

@@ -22,18 +22,9 @@ PACK = 4
 SQUARE = 32
 D_TILES = D // P
 BLOCKS = C // P
-U_WINDOW = 1376
-DZ_VECTOR_SHARE = 336
-EARLY = C - 2 * P
-LAST = C - P
 HALF = C // 2
-CUTS = 4
-PIECE = C // CUTS
-PIECES = D_TILES * CUTS
-SLOT = 4 * PIECE
-LANE = 8
-WEIGHTS_AT = LANE * (2 * CUTS + 1)
-ROUNDED_AT = 4 * T - 64
+PIECE = C // 4
+DZ_VECTOR_SHARE = 160
 
 
 def interleave_views(grouped, raw, lo, hi):
@@ -51,49 +42,53 @@ def tile_attend_gebag_kernel(tc, eT, W, dz, wc, offs, bagoffs, out_0, out_1):
     with ExitStack() as ctx:
         keep = ctx.enter_context(tc.tile_pool(name="keep", bufs=1))
         reused = ctx.enter_context(tc.tile_pool(name="reused", bufs=1))
-        links = ctx.enter_context(tc.tile_pool(name="links", bufs=1))
-        psum = ctx.enter_context(tc.psum_pool(name="psum", bufs=8))
+        psum = ctx.enter_context(tc.psum_pool(name="psum", bufs=1))
+        psum_u = ctx.enter_context(tc.psum_pool(name="psum_u", bufs=2))
 
         W_rows = W.rearrange("(p t) c -> p t c", t=PACK)
         dz_rows = dz.rearrange("(p t) c -> p t c", t=PACK)
 
-        dz_raw = keep.tile([P, PACK, X], F32)
-        w_raw_0 = keep.tile([P, PACK, P], F32)
-        w_raw_rest = keep.tile([P, PACK, D - P], F32)
+        dz_raw = [keep.tile([P, PACK, X // 2], F32, name="dz_raw%d" % h) for h in range(2)]
+        w_raw_01 = keep.tile([P, PACK, 2 * P], F32)
+        w_raw_23 = keep.tile([P, PACK, 2 * P], F32)
         bag_list = keep.tile([P, C // 16], U16)
         idx_list = keep.tile([P, C // 16], U16)
-        wc_again = links.tile([P, PIECE], F32, offset=4 * T + WEIGHTS_AT * SLOT)
-        wc_sb = keep.tile([P, C], F32)
+        wc_sb = [keep.tile([P, PIECE], F32, name="wc%d" % q) for q in range(4)]
         table = [keep.tile([P, T], F32, name="table%d" % j) for j in range(D_TILES)]
 
-        nc.sync.dma_start(out=w_raw_0[:], in_=W_rows[:, :, :P])
-        nc.sync.dma_start(out=dz_raw[:], in_=dz_rows)
-        nc.sync.dma_start(idx_list[:], offs)
-        nc.sync.dma_start(out=table[0][:], in_=eT[:P, :])
-        nc.sync.dma_start(bag_list[:], bagoffs)
-        nc.sync.dma_start(out=w_raw_rest[:], in_=W_rows[:, :, P:])
-        nc.sync.dma_start(out=table[1][:], in_=eT[P : 2 * P, :])
-        nc.sync.dma_start(out=table[2][:], in_=eT[2 * P : 3 * P, :])
-        nc.sync.dma_start(out=wc_sb[:], in_=wc)
-        nc.sync.dma_start(out=table[3][:], in_=eT[3 * P :, :])
-        nc.sync.dma_start(out=wc_again[:], in_=wc[:, HALF:EARLY])
+        def load_weights(q):
+            nc.sync.dma_start(out=wc_sb[q][:], in_=wc[:, q * PIECE : (q + 1) * PIECE])
 
-        windows = [keep.tile([P, T], F32, name="window%d" % h, tag="window%d" % h) for h in range(2)]
+        nc.sync.dma_start(out=w_raw_01[:], in_=W_rows[:, :, : 2 * P])
+        for h in range(2):
+            nc.sync.dma_start(out=dz_raw[h][:], in_=dz_rows[:, :, h * X // 2 : (h + 1) * X // 2])
+        nc.sync.dma_start(bag_list[:], bagoffs)
+        nc.sync.dma_start(idx_list[:], offs)
+        load_weights(0)
+        nc.sync.dma_start(out=w_raw_23[:], in_=W_rows[:, :, 2 * P :])
+        load_weights(1)
+        for j in range(D_TILES):
+            nc.sync.dma_start(out=table[j][:], in_=eT[j * P : (j + 1) * P, :])
+            if j == 0:
+                load_weights(2)
+                load_weights(3)
+
+        windows = [keep.tile([P, T], F32, name="window%d" % j) for j in range(2)]
         for window in windows:
             nc.vector.memset(window[:], 0.0)
         ident = keep.tile([P, P], F32)
         make_identity(nc, ident[:])
-        dw_cols_early = keep.tile([P, P], F32)
-        dw_cols_late = keep.tile([P, P], F32, align_bytes=64)
-        nc.gpsimd.memset(dw_cols_early[:], 0.0)
-        nc.gpsimd.memset(dw_cols_late[:], 0.0)
+        dw_cols = keep.tile([P, BLOCKS * SQUARE], F32, align_bytes=64)
+        nc.gpsimd.memset(dw_cols[:], 0.0)
 
-        dz_codes = keep.tile([P, X], U32, align_bytes=64)
+        dz_codes = reused.tile([P, X], U32, align_bytes=64, offset=0)
         dz_scales = keep.tile([P, X], U8, align_bytes=64)
-        w_codes = keep.tile([P, D], U32, align_bytes=64)
+        w_codes = reused.tile([P, D], U32, align_bytes=64, offset=4 * T)
         w_scales = keep.tile([P, D], U8, align_bytes=64)
-        w_bf_0 = reused.tile([P, P, PACK], BF16, align_bytes=64, offset=ROUNDED_AT)
-        w_bf_rest = links.tile([P, D - P, PACK], BF16, align_bytes=64, offset=ROUNDED_AT)
+        w_bf_01 = keep.tile([P, 2 * P, PACK], BF16, align_bytes=64)
+        dz_bf = [keep.tile([P, X // 2, PACK], BF16, align_bytes=64, name="dz_bf%d" % h) for h in range(2)]
+        gathered = keep.tile([P, 8 * PIECE], F32, align_bytes=64)
+        u = [keep.tile([P, X], F32, name="u%d" % j) for j in range(D_TILES)]
 
         def cast(engine_copy, grouped, raw, lo, hi):
             dst, src = interleave_views(grouped, raw, lo, hi)
@@ -102,169 +97,171 @@ def tile_attend_gebag_kernel(tc, eT, W, dz, wc, offs, bagoffs, out_0, out_1):
         def scalar_cast(out, in_):
             nc.scalar.activation(out=out, in_=in_, func=COPY)
 
-        def gpsimd_cast(out, in_):
-            nc.gpsimd.tensor_scalar(out=out, in0=in_, scalar1=1.0, scalar2=0.0, op0=MULT, op1=ADD)
-
-        def u_start(j):
-            return (D_TILES - 1 - j) * X
-
-        def multiply(j):
-            acc = psum.tile([P, X], F32, tag="bank")
+        def multiply(j, acc, lo, hi):
             nc.tensor.matmul_mx(
-                out=acc[:],
+                out=acc,
                 lhsT=w_codes[:, j * P : (j + 1) * P].bitcast(E4M3),
                 lhsT_scale=w_scales[:, j * P : (j + 1) * P],
-                rhs=dz_codes[:].bitcast(E5M2),
-                rhs_scale=dz_scales[:],
+                rhs=dz_codes[:, lo:hi].bitcast(E5M2),
+                rhs_scale=dz_scales[:, lo:hi],
                 start=True,
                 stop=True,
             )
-            nc.scalar.copy(out=u_all[:, u_start(j) : u_start(j) + X], in_=acc[:])
 
-        cast(scalar_cast, w_bf_0, w_raw_0, 0, P)
-        quantize(nc, w_bf_0[:], w_codes[:, :P], w_scales[:, :P], E4M3)
-        dz_bf = reused.tile([P, X, PACK], BF16, align_bytes=64, offset=ROUNDED_AT)
-        cast(nc.vector.tensor_copy, dz_bf, dz_raw, 0, DZ_VECTOR_SHARE)
-        cast(scalar_cast, dz_bf, dz_raw, DZ_VECTOR_SHARE, X)
-        quantize(nc, dz_bf[:], dz_codes[:], dz_scales[:], E5M2)
-        u_all = reused.tile([P, (D_TILES - 1) * X + U_WINDOW], F32, align_bytes=64, offset=4 * T)
-        nc.gpsimd.memset(u_all[:, D_TILES * X :], 0.0)
-        windows.append(reused.tile([P, T], F32, name="window2", align_bytes=64, offset=0))
-        nc.gpsimd.memset(windows[2][:], 0.0)
-        multiply(0)
+        def make_u(j):
+            acc = psum_u.tile([P, X], F32, name="acc")
+            multiply(j, acc[:], 0, X)
+            nc.scalar.copy(out=u[j][:], in_=acc[:])
 
-        def turn_and_add(j, values, lo, hi):
-            for b in range(lo // P, hi // P):
-                nc.tensor.matmul(
-                    sums[b][:, :P],
-                    lhsT=values[:, b * P - lo : (b + 1) * P - lo],
-                    rhs=ident[:],
-                    is_transpose=True,
-                    start=(j == 0),
-                    stop=(j == D_TILES - 1),
-                )
+        def gpsimd_cast(out, in_):
+            nc.gpsimd.tensor_scalar(out=out, in0=in_, scalar1=1.0, scalar2=0.0, op0=MULT, op1=ADD)
 
-        def sum_on_scalar(b, column):
-            nc.scalar.activation(out=spent[:, b, :], in_=sums[b][:, :P], func=COPY, accum_out=column)
+        cast(scalar_cast, w_bf_01, w_raw_01, 0, 2 * P)
+        quantize(nc, w_bf_01[:], w_codes[:, : 2 * P], w_scales[:, : 2 * P], E4M3)
+        first = [psum.tile([P, X // 2], F32, name="first%d" % h) for h in range(2)]
+        for h in range(2):
+            lo, hi = h * X // 2, (h + 1) * X // 2
+            cast(nc.vector.tensor_copy, dz_bf[h], dz_raw[h], 0, DZ_VECTOR_SHARE)
+            cast(scalar_cast, dz_bf[h], dz_raw[h], DZ_VECTOR_SHARE, X // 2)
+            quantize(nc, dz_bf[h][:], dz_codes[:, lo:hi], dz_scales[:, lo:hi], E5M2)
+            multiply(0, first[h][:], lo, hi)
+            nc.scalar.copy(out=u[0][:, lo:hi], in_=first[h][:])
 
-        def sum_on_vector(b, column):
-            nc.vector.tensor_reduce(out=column, in_=sums[b][:, :P], axis=mybir.AxisListType.X, op=ADD)
-
-        sums = []
+        made = keep.tile([P, 18 * PIECE], F32)
+        sums = [psum.tile([P, X], F32, name="sums%d" % b) for b in range(3)]
         spent = keep.tile([P, BLOCKS, P], F32)
-        picked, picked_at, ub = {}, {}, {}
 
-        def span(k):
-            j, h = divmod(k, CUTS)
-            return j, h * PIECE, (h + 1) * PIECE
+        def slot(j, q):
+            at = 4 * j + q if j < 2 else 4 * (q // 2) + 2 * (j - 2) + 1 + q % 2
+            return {0: 7, 8: 1}.get(at, at)
 
-        def listed(j, lo, hi):
-            return table[j][:].indirect(idx_list[:, lo // 16 : hi // 16])
+        def ub(j, q, lo=0, hi=PIECE):
+            at = slot(j, q) * PIECE
+            return gathered[:, at + lo : at + hi]
 
-        def bagged(j, lo, hi):
-            return u_all[:, u_start(j) : u_start(j) + U_WINDOW].indirect(bag_list[:, lo // 16 : hi // 16])
+        def offsets(listed, lo, hi):
+            return listed[:, lo // 16 : hi // 16]
 
-        def placed(name, slot, columns):
-            return links.tile([P, columns], F32, name=name, offset=4 * T + slot * SLOT)
+        def gather_u_on_vector(j, q):
+            nc.vector.tensor_copy(ub(j, q), u[j][:].indirect(offsets(bag_list, q * PIECE, (q + 1) * PIECE)))
 
-        def gather_table(k, slot):
-            picked_at[k] = slot
-            picked[k] = placed("picked%d" % k, slot, (4 if k == 0 else 3) * PIECE)[:, :PIECE]
-            nc.vector.tensor_copy(picked[k], listed(*span(k)))
+        def gather_u(j, q):
+            nc.scalar.activation(ub(j, q), u[j][:].indirect(offsets(bag_list, q * PIECE, (q + 1) * PIECE)), COPY)
 
-        def gather_u_whole(j, values):
-            for h in range(CUTS):
-                ub[j * CUTS + h] = values[:, h * PIECE : (h + 1) * PIECE]
-            nc.vector.tensor_copy(values[:], bagged(j, 0, C))
+        def weights(q):
+            return wc_sb[q][:]
 
-        def product(k, values):
-            j, lo, hi = span(k)
-            nc.gpsimd.tensor_tensor(values, ub[k], picked[k], MULT)
-            turn_and_add(j, values, lo, hi)
-
-        for k in range(CUTS):
-            gather_table(k, LANE * (k + 1))
-        cast(scalar_cast, w_bf_rest, w_raw_rest, 0, D - 2 * P)
-        cast(gpsimd_cast, w_bf_rest, w_raw_rest, D - 2 * P, D - P)
-        ub_0 = keep.tile([P, C], F32)
-        gather_u_whole(0, ub_0)
-        quantize(nc, w_bf_rest[:, :P, :], w_codes[:, P : 2 * P], w_scales[:, P : 2 * P], E4M3)
-        quantize(nc, w_bf_rest[:, P:, :], w_codes[:, 2 * P :], w_scales[:, 2 * P :], E4M3)
-        for j in range(1, D_TILES):
-            multiply(j)
-        for b in range(BLOCKS):
-            sums.append(psum.tile([P, X], F32, tag="bank", name="sums%d" % b))
-        for k in range(CUTS, 2 * CUTS):
-            gather_table(k, LANE * (k + 1))
-        gather_u_whole(1, keep.tile([P, C], F32, name="ub_1"))
-
-        late = (3 * CUTS - 1, PIECES - 1)
-        order = [0, 1, 4, 2, 5, 3, 6, 8, 7, 9, 12, 10, 13, 11, 14, 15]
-        to_gather = [(2 * order.index(k) - 3, bagged, k) for k in range(2 * CUTS, PIECES)]
-        to_gather += [(2 * order.index(k), listed, k) for k in range(2 * CUTS, PIECES) if k not in late]
-        to_gather.sort(key=lambda entry: entry[0])
-        windows.append(links.tile([P, T], F32, name="window3", offset=0))
-        nc.gpsimd.memset(windows[3][:], 0.0)
-
-        def weigh(k, values):
-            j, lo, hi = span(k)
-            weights = wc_again[:] if k == PIECES - 2 else wc_sb[:, lo:hi]
-            nc.gpsimd.tensor_tensor(values, ub[k], weights, MULT)
-
-        def scatter(j, lo, hi, values):
-            nc.vector.tensor_copy(windows[j][:].indirect(idx_list[:, lo // 16 : hi // 16]), values)
-            if hi == C:
+        def store(j, q):
+            if q == 3:
                 nc.sync.dma_start(out=out_0[j * P : (j + 1) * P, :], in_=windows[j][:])
 
-        first_two = placed("first_two", 0, 2 * PIECE)
-        nc.gpsimd.tensor_tensor(first_two[:], ub_0[:, : 2 * PIECE], wc_sb[:, : 2 * PIECE], MULT)
-        scatter(0, 0, 2 * PIECE, first_two[:])
-        for at in range(1, PIECES):
-            k, before = order[at], order[at - 1]
-            if at >= 2:
-                de = placed("de%d" % k, picked_at[0] + 1 if at == 2 else picked_at[order[at - 3]], PIECE)
-                weigh(k, de[:])
-                scatter(*span(k), de[:])
-            if before in picked:
-                product(before, placed("prod1", picked_at[0] + 3, PIECE)[:] if at == 2 else ub[before])
-            if at - 1 < len(to_gather):
-                source, later = to_gather[at - 1][1:]
-                slot = picked_at[before] + 2 if before in picked else WEIGHTS_AT
-                if source is listed:
-                    gather_table(later, slot)
-                else:
-                    ub[later] = placed("ub%d" % later, slot, PIECE)[:]
-                    nc.vector.tensor_copy(ub[later], bagged(*span(later)))
+        def vector_scatter(k):
+            j, q = 2 * (k // 4), k % 4
+            target = windows[j][:].indirect(offsets(idx_list, q * PIECE, (q + 1) * PIECE))
+            nc.vector.tensor_tensor(target, ub(j, q), weights(q), MULT)
+            store(j, q)
 
-        def fused_product(j, values, lo, hi):
-            at = (CUTS - 1) * PIECE
-            nc.vector.tensor_tensor(values, listed(j, lo, hi), ub[(j + 1) * CUTS - 1][:, lo - at : hi - at], MULT)
-            turn_and_add(j, values, lo, hi)
+        def weighted(k):
+            at = {0: 17 * PIECE, 6: 13 * PIECE + PIECE // 2, 7: 16 * PIECE}.get(k, 2 * k * PIECE)
+            return made[:, at : at + PIECE]
 
-        early_blocks = HALF // P
-        for b in range(early_blocks):
-            sum_on_scalar(b, dw_cols_early[:, b : b + 1])
-        turned = psum.tile([P, X], F32, tag="bank")
-        nc.tensor.transpose(turned[:, :P], dw_cols_early[:], ident[:])
-        dw_rows_early = keep.tile([early_blocks, P], F32)
-        nc.scalar.copy(out=dw_rows_early[:], in_=turned[:early_blocks, :P])
-        nc.scalar.dma_start(out=out_1[:, :HALF].rearrange("o (b p) -> (o b) p", p=P), in_=dw_rows_early[:])
+        def weigh(k):
+            j, q = 2 * (k // 4) + 1, k % 4
+            nc.vector.tensor_tensor(weighted(k), ub(j, q), weights(q), MULT)
 
-        prod_late = placed("prod_late", picked_at[PIECES - 2], 2 * (C - EARLY))
-        pieces = [(D_TILES - 2, EARLY, C), (D_TILES - 1, EARLY, LAST), (D_TILES - 1, LAST, C)]
-        filled = 0
-        for j, lo, hi in pieces:
-            fused_product(j, prod_late[:, filled : filled + hi - lo], lo, hi)
-            filled += hi - lo
-        for b in range(early_blocks, BLOCKS):
-            at = (b - early_blocks) * SQUARE
-            add_up = sum_on_vector if b == BLOCKS - 2 else sum_on_scalar
-            add_up(b, dw_cols_late[:, at : at + 1])
+        def scalar_scatter(k):
+            j, q = 2 * (k // 4) + 1, k % 4
+            target = windows[j][:].indirect(offsets(idx_list, q * PIECE, (q + 1) * PIECE))
+            nc.scalar.activation(target, weighted(k), COPY)
+            store(j, q)
 
-        late_blocks = BLOCKS - early_blocks
-        dw_rows_late = keep.tile([P, P], F32, align_bytes=64)
-        nc.vector.transpose(dw_rows_late[:], dw_cols_late[:])
+        def bank(b):
+            return (sums[0], b) if b < 4 else (sums[b // 2 - 1], b % 2)
+
+        def gather_table(g, lo=0, hi=HALF):
+            j, h = divmod(g, 2) if g < 4 else (2 + g % 2, (g - 4) // 2)
+            values = made[:, g * HALF + lo : g * HALF + hi]
+            q = 2 * h + lo // PIECE
+            at = lo % PIECE
+            looked_up = table[j][:].indirect(offsets(idx_list, h * HALF + lo, h * HALF + hi))
+            nc.vector.tensor_tensor(values, looked_up, ub(j, q, at, at + hi - lo), MULT)
+            for b in range((h * HALF + lo) // P, (h * HALF + hi) // P):
+                tile, place = bank(b)
+                nc.tensor.matmul(
+                    tile[:, place * P : (place + 1) * P],
+                    lhsT=made[:, g * HALF + b * P - h * HALF : g * HALF + (b + 1) * P - h * HALF],
+                    rhs=ident[:],
+                    is_transpose=True,
+                    start=(j == 0 and place == 0),
+                    stop=(j == D_TILES - 1 and b in (3, 5, 7)),
+                )
+
+        def column(b):
+            return dw_cols[:, b * SQUARE : b * SQUARE + 1]
+
+        def summed(b):
+            tile, place = bank(b)
+            return tile[:, place * P : (place + 1) * P]
+
+        def sum_on_scalar(b):
+            nc.scalar.activation(out=spent[:, b, :], in_=summed(b), func=COPY, accum_out=column(b))
+
+        def sum_on_vector(b):
+            columns = dw_cols[:, b * SQUARE : (b + 2) * SQUARE : SQUARE]
+            pair = bank(b)[0][:, : 2 * P].rearrange("p (b i) -> p b i", i=P)
+            nc.vector.tensor_reduce(out=columns, in_=pair, axis=mybir.AxisListType.X, op=ADD)
+
+        gather_u_on_vector(0, 0)
+        gather_u(0, 1)
+        vector_scatter(0)
+        make_u(1)
+        gather_u(1, 0)
+        weigh(0)
+        gather_u(1, 1)
+        gather_u(0, 2)
+        scalar_scatter(0)
+        rounded = {2: ub(1, 2), 3: ub(0, 3)}
+        for j in (2, 3):
+            rounded[j] = rounded[j].bitcast(BF16).rearrange("p (c t) -> p c t", t=PACK)
+            dst = rounded[j].rearrange("p (c i) t -> p c t i", i=PACK)
+            src = w_raw_23[:, :, (j - 2) * P : (j - 1) * P].rearrange("p t (c i) -> p c t i", i=PACK)
+            gpsimd_cast(dst, src)
+        for j in (2, 3):
+            quantize(nc, rounded[j], w_codes[:, j * P : (j + 1) * P], w_scales[:, j * P : (j + 1) * P], E4M3)
+        vector_scatter(1)
+        weigh(1)
+        gather_table(0, 0, PIECE)
+        gather_table(0, PIECE, HALF)
+        gather_u(1, 2)
+        gather_u(0, 3)
+        scalar_scatter(1)
+        make_u(2)
+        make_u(3)
+        for j in (2, 3):
+            windows.append(reused.tile([P, T], F32, name="window%d" % j, align_bytes=64, offset=(j - 2) * 4 * T))
+            nc.gpsimd.memset(windows[j][:], 0.0)
+        for k in range(2, 8):
+            vector_scatter(k)
+            if k > 2:
+                gather_table(k - 2)
+            weigh(k)
+            if k + 1 < 8:
+                gather_u(2 * ((k + 1) // 4) + 1, (k + 1) % 4)
+            if k + 2 < 8:
+                gather_u(2 * ((k + 2) // 4), (k + 2) % 4)
+            scalar_scatter(k)
+        for b in range(4):
+            sum_on_scalar(b)
+        gather_table(6)
+        gather_table(7, 0, PIECE)
+        sum_on_scalar(4)
+        sum_on_scalar(5)
+        gather_table(7, PIECE, HALF)
+        sum_on_vector(6)
+
+        dw_rows = keep.tile([P, BLOCKS * SQUARE], F32, align_bytes=64)
+        nc.vector.transpose(dw_rows[:], dw_cols[:])
         nc.sync.dma_start(
-            out=out_1[:, HALF:].rearrange("o (b q i) -> (o q) b i", q=P // SQUARE, i=SQUARE),
-            in_=dw_rows_late[0:P:SQUARE, : late_blocks * SQUARE].rearrange("q (b i) -> q b i", i=SQUARE),
+            out=out_1.rearrange("o (b q i) -> (o q) b i", q=P // SQUARE, i=SQUARE),
+            in_=dw_rows[0:P:SQUARE, :].rearrange("q (b i) -> q b i", i=SQUARE),
         )

@@ -25,6 +25,8 @@ BLOCKS = C // P
 HALF = C // 2
 PIECE = C // 4
 DZ_VECTOR_SHARE = 160
+WIDE = 384
+VECTOR_TILE = 1
 
 
 def interleave_views(grouped, raw, lo, hi):
@@ -41,7 +43,6 @@ def tile_attend_gebag_kernel(tc, eT, W, dz, wc, offs, bagoffs, out_0, out_1):
     nc = tc.nc
     with ExitStack() as ctx:
         keep = ctx.enter_context(tc.tile_pool(name="keep", bufs=1))
-        reused = ctx.enter_context(tc.tile_pool(name="reused", bufs=1))
         psum = ctx.enter_context(tc.psum_pool(name="psum", bufs=1))
         psum_u = ctx.enter_context(tc.psum_pool(name="psum_u", bufs=2))
 
@@ -53,41 +54,36 @@ def tile_attend_gebag_kernel(tc, eT, W, dz, wc, offs, bagoffs, out_0, out_1):
         w_raw_23 = keep.tile([P, PACK, 2 * P], F32)
         bag_list = keep.tile([P, C // 16], U16)
         idx_list = keep.tile([P, C // 16], U16)
-        wc_sb = [keep.tile([P, PIECE], F32, name="wc%d" % q) for q in range(4)]
+        wc_sb = keep.tile([P, C], F32)
         table = [keep.tile([P, T], F32, name="table%d" % j) for j in range(D_TILES)]
-
-        def load_weights(q):
-            nc.sync.dma_start(out=wc_sb[q][:], in_=wc[:, q * PIECE : (q + 1) * PIECE])
 
         nc.sync.dma_start(out=w_raw_01[:], in_=W_rows[:, :, : 2 * P])
         for h in range(2):
             nc.sync.dma_start(out=dz_raw[h][:], in_=dz_rows[:, :, h * X // 2 : (h + 1) * X // 2])
         nc.sync.dma_start(bag_list[:], bagoffs)
-        nc.sync.dma_start(idx_list[:], offs)
-        load_weights(0)
         nc.sync.dma_start(out=w_raw_23[:], in_=W_rows[:, :, 2 * P :])
-        load_weights(1)
+        nc.sync.dma_start(idx_list[:], offs)
+        nc.sync.dma_start(out=wc_sb[:, :PIECE], in_=wc[:, :PIECE])
+        nc.sync.dma_start(out=wc_sb[:, PIECE:], in_=wc[:, PIECE:])
         for j in range(D_TILES):
             nc.sync.dma_start(out=table[j][:], in_=eT[j * P : (j + 1) * P, :])
-            if j == 0:
-                load_weights(2)
-                load_weights(3)
 
-        windows = [keep.tile([P, T], F32, name="window%d" % j) for j in range(2)]
-        for window in windows:
-            nc.vector.memset(window[:], 0.0)
+        windows = [keep.tile([P, T], F32, name="window%d" % j) for j in range(D_TILES)]
+        for j in (0, 2, 1, 3):
+            nc.vector.memset(windows[j][:], 0.0)
         ident = keep.tile([P, P], F32)
         make_identity(nc, ident[:])
         dw_cols = keep.tile([P, BLOCKS * SQUARE], F32, align_bytes=64)
         nc.gpsimd.memset(dw_cols[:], 0.0)
 
-        dz_codes = reused.tile([P, X], U32, align_bytes=64, offset=0)
+        dz_codes = keep.tile([P, X], U32, align_bytes=64)
         dz_scales = keep.tile([P, X], U8, align_bytes=64)
-        w_codes = reused.tile([P, D], U32, align_bytes=64, offset=4 * T)
+        w_codes = keep.tile([P, D], U32, align_bytes=64)
         w_scales = keep.tile([P, D], U8, align_bytes=64)
         w_bf_01 = keep.tile([P, 2 * P, PACK], BF16, align_bytes=64)
         dz_bf = [keep.tile([P, X // 2, PACK], BF16, align_bytes=64, name="dz_bf%d" % h) for h in range(2)]
-        gathered = keep.tile([P, 8 * PIECE], F32, align_bytes=64)
+        w_bf_23 = keep.tile([P, 2 * P, PACK], BF16, align_bytes=64)
+        ub = [keep.tile([P, C], F32, name="ub%d" % j) for j in range(D_TILES)]
         u = [keep.tile([P, X], F32, name="u%d" % j) for j in range(D_TILES)]
 
         def cast(engine_copy, grouped, raw, lo, hi):
@@ -113,9 +109,6 @@ def tile_attend_gebag_kernel(tc, eT, W, dz, wc, offs, bagoffs, out_0, out_1):
             multiply(j, acc[:], 0, X)
             nc.scalar.copy(out=u[j][:], in_=acc[:])
 
-        def gpsimd_cast(out, in_):
-            nc.gpsimd.tensor_scalar(out=out, in0=in_, scalar1=1.0, scalar2=0.0, op0=MULT, op1=ADD)
-
         cast(scalar_cast, w_bf_01, w_raw_01, 0, 2 * P)
         quantize(nc, w_bf_01[:], w_codes[:, : 2 * P], w_scales[:, : 2 * P], E4M3)
         first = [psum.tile([P, X // 2], F32, name="first%d" % h) for h in range(2)]
@@ -127,53 +120,29 @@ def tile_attend_gebag_kernel(tc, eT, W, dz, wc, offs, bagoffs, out_0, out_1):
             multiply(0, first[h][:], lo, hi)
             nc.scalar.copy(out=u[0][:, lo:hi], in_=first[h][:])
 
-        made = keep.tile([P, 18 * PIECE], F32)
+        made = keep.tile([P, 6 * C], F32)
         sums = [psum.tile([P, X], F32, name="sums%d" % b) for b in range(3)]
         spent = keep.tile([P, BLOCKS, P], F32)
-
-        def slot(j, q):
-            at = 4 * j + q if j < 2 else 4 * (q // 2) + 2 * (j - 2) + 1 + q % 2
-            return {0: 7, 8: 1}.get(at, at)
-
-        def ub(j, q, lo=0, hi=PIECE):
-            at = slot(j, q) * PIECE
-            return gathered[:, at + lo : at + hi]
 
         def offsets(listed, lo, hi):
             return listed[:, lo // 16 : hi // 16]
 
-        def gather_u_on_vector(j, q):
-            nc.vector.tensor_copy(ub(j, q), u[j][:].indirect(offsets(bag_list, q * PIECE, (q + 1) * PIECE)))
+        def bagged(j, lo, hi):
+            return u[j][:].indirect(offsets(bag_list, lo, hi))
 
-        def gather_u(j, q):
-            nc.scalar.activation(ub(j, q), u[j][:].indirect(offsets(bag_list, q * PIECE, (q + 1) * PIECE)), COPY)
+        def gather_u(j, lo, hi):
+            nc.vector.tensor_copy(ub[j][:, lo:hi], bagged(j, lo, hi))
 
-        def weights(q):
-            return wc_sb[q][:]
-
-        def store(j, q):
-            if q == 3:
+        def weigh_and_scatter(j, lo, hi, at):
+            values = made[:, at : at + hi - lo]
+            nc.gpsimd.tensor_tensor(values, ub[j][:, lo:hi], wc_sb[:, lo:hi], MULT)
+            target = windows[j][:].indirect(offsets(idx_list, lo, hi))
+            if j == VECTOR_TILE:
+                nc.vector.tensor_copy(target, values)
+            else:
+                nc.scalar.activation(target, values, COPY)
+            if hi == C:
                 nc.sync.dma_start(out=out_0[j * P : (j + 1) * P, :], in_=windows[j][:])
-
-        def vector_scatter(k):
-            j, q = 2 * (k // 4), k % 4
-            target = windows[j][:].indirect(offsets(idx_list, q * PIECE, (q + 1) * PIECE))
-            nc.vector.tensor_tensor(target, ub(j, q), weights(q), MULT)
-            store(j, q)
-
-        def weighted(k):
-            at = {0: 17 * PIECE, 6: 13 * PIECE + PIECE // 2, 7: 16 * PIECE}.get(k, 2 * k * PIECE)
-            return made[:, at : at + PIECE]
-
-        def weigh(k):
-            j, q = 2 * (k // 4) + 1, k % 4
-            nc.vector.tensor_tensor(weighted(k), ub(j, q), weights(q), MULT)
-
-        def scalar_scatter(k):
-            j, q = 2 * (k // 4) + 1, k % 4
-            target = windows[j][:].indirect(offsets(idx_list, q * PIECE, (q + 1) * PIECE))
-            nc.scalar.activation(target, weighted(k), COPY)
-            store(j, q)
 
         def bank(b):
             return (sums[0], b) if b < 4 else (sums[b // 2 - 1], b % 2)
@@ -181,10 +150,8 @@ def tile_attend_gebag_kernel(tc, eT, W, dz, wc, offs, bagoffs, out_0, out_1):
         def gather_table(g, lo=0, hi=HALF):
             j, h = divmod(g, 2) if g < 4 else (2 + g % 2, (g - 4) // 2)
             values = made[:, g * HALF + lo : g * HALF + hi]
-            q = 2 * h + lo // PIECE
-            at = lo % PIECE
             looked_up = table[j][:].indirect(offsets(idx_list, h * HALF + lo, h * HALF + hi))
-            nc.vector.tensor_tensor(values, looked_up, ub(j, q, at, at + hi - lo), MULT)
+            nc.vector.tensor_tensor(values, looked_up, ub[j][:, h * HALF + lo : h * HALF + hi], MULT)
             for b in range((h * HALF + lo) // P, (h * HALF + hi) // P):
                 tile, place = bank(b)
                 nc.tensor.matmul(
@@ -211,45 +178,38 @@ def tile_attend_gebag_kernel(tc, eT, W, dz, wc, offs, bagoffs, out_0, out_1):
             pair = bank(b)[0][:, : 2 * P].rearrange("p (b i) -> p b i", i=P)
             nc.vector.tensor_reduce(out=columns, in_=pair, axis=mybir.AxisListType.X, op=ADD)
 
-        gather_u_on_vector(0, 0)
-        gather_u(0, 1)
-        vector_scatter(0)
+        cuts = [(0, PIECE), (PIECE, PIECE + WIDE), (PIECE + WIDE, C)]
+        quarters = [(q * PIECE, (q + 1) * PIECE) for q in range(4)]
+        apart = 4 * C
+
+        cast(nc.vector.tensor_copy, w_bf_23, w_raw_23, 0, 2 * P)
+        gather_u(0, *cuts[0])
+        quantize(nc, w_bf_23[:], w_codes[:, 2 * P :], w_scales[:, 2 * P :], E4M3)
         make_u(1)
-        gather_u(1, 0)
-        weigh(0)
-        gather_u(1, 1)
-        gather_u(0, 2)
-        scalar_scatter(0)
-        rounded = {2: ub(1, 2), 3: ub(0, 3)}
-        for j in (2, 3):
-            rounded[j] = rounded[j].bitcast(BF16).rearrange("p (c t) -> p c t", t=PACK)
-            dst = rounded[j].rearrange("p (c i) t -> p c t i", i=PACK)
-            src = w_raw_23[:, :, (j - 2) * P : (j - 1) * P].rearrange("p t (c i) -> p c t i", i=PACK)
-            gpsimd_cast(dst, src)
-        for j in (2, 3):
-            quantize(nc, rounded[j], w_codes[:, j * P : (j + 1) * P], w_scales[:, j * P : (j + 1) * P], E4M3)
-        vector_scatter(1)
-        weigh(1)
-        gather_table(0, 0, PIECE)
-        gather_table(0, PIECE, HALF)
-        gather_u(1, 2)
-        gather_u(0, 3)
-        scalar_scatter(1)
+        nc.scalar.activation(ub[1][:, :WIDE], bagged(1, 0, WIDE), COPY)
+        weigh_and_scatter(0, *cuts[0], apart)
         make_u(2)
         make_u(3)
-        for j in (2, 3):
-            windows.append(reused.tile([P, T], F32, name="window%d" % j, align_bytes=64, offset=(j - 2) * 4 * T))
-            nc.gpsimd.memset(windows[j][:], 0.0)
-        for k in range(2, 8):
-            vector_scatter(k)
-            if k > 2:
-                gather_table(k - 2)
-            weigh(k)
-            if k + 1 < 8:
-                gather_u(2 * ((k + 1) // 4) + 1, (k + 1) % 4)
-            if k + 2 < 8:
-                gather_u(2 * ((k + 2) // 4), (k + 2) % 4)
-            scalar_scatter(k)
+        gather_u(0, *cuts[1])
+        gather_u(0, *cuts[2])
+        gather_u(1, WIDE, WIDE + PIECE)
+        gather_u(2, *cuts[0])
+        gather_u(1, WIDE + PIECE, C)
+        gather_u(3, *cuts[0])
+        for cut in cuts[1:]:
+            gather_u(2, *cut)
+            gather_u(3, *cut)
+        weigh_and_scatter(0, *cuts[1], apart + PIECE)
+        turns = [(2, 0, 0), (0, 2, HALF), (3, 0, 2 * HALF), (2, 1, 4 * HALF - WIDE // 2)]
+        for q, (j, cut, at) in enumerate(turns):
+            weigh_and_scatter(VECTOR_TILE, *quarters[q], apart + C + q * PIECE)
+            weigh_and_scatter(j, *cuts[cut], at)
+            gather_table(q)
+        gather_table(4)
+        weigh_and_scatter(3, *cuts[1], 6 * HALF - WIDE // 2)
+        gather_table(5)
+        weigh_and_scatter(2, *cuts[2], 7 * HALF + PIECE - WIDE // 2)
+        weigh_and_scatter(3, *cuts[2], apart + PIECE + WIDE)
         for b in range(4):
             sum_on_scalar(b)
         gather_table(6)

@@ -69,8 +69,9 @@ def tile_attend_gebag_kernel(tc, eT, W, dz, wc, offs, bagoffs, out_0, out_1):
             nc.sync.dma_start(out=table[j][:], in_=eT[j * P : (j + 1) * P, :])
 
         windows = [keep.tile([P, T], F32, name="window%d" % j) for j in range(D_TILES)]
-        for j in (0, 2, 1, 3):
+        for j in (0, 2):
             nc.vector.memset(windows[j][:], 0.0)
+            nc.gpsimd.memset(windows[j + 1][:], 0.0)
         ident = keep.tile([P, P], F32)
         make_identity(nc, ident[:])
         dw_cols = keep.tile([P, BLOCKS * SQUARE], F32, align_bytes=64)

@@ -26,7 +26,6 @@ HALF = C // 2
 PIECE = C // 4
 DZ_VECTOR_SHARE = 160
 WIDE = 384
-VECTOR_TILE = 1
 
 
 def interleave_views(grouped, raw, lo, hi):
@@ -63,15 +62,13 @@ def tile_attend_gebag_kernel(tc, eT, W, dz, wc, offs, bagoffs, out_0, out_1):
         nc.sync.dma_start(bag_list[:], bagoffs)
         nc.sync.dma_start(out=w_raw_23[:], in_=W_rows[:, :, 2 * P :])
         nc.sync.dma_start(idx_list[:], offs)
-        nc.sync.dma_start(out=wc_sb[:, :PIECE], in_=wc[:, :PIECE])
-        nc.sync.dma_start(out=wc_sb[:, PIECE:], in_=wc[:, PIECE:])
+        nc.sync.dma_start(out=wc_sb[:], in_=wc)
         for j in range(D_TILES):
             nc.sync.dma_start(out=table[j][:], in_=eT[j * P : (j + 1) * P, :])
 
         windows = [keep.tile([P, T], F32, name="window%d" % j) for j in range(D_TILES)]
-        for j in (0, 2):
+        for j in (0, 2, 1, 3):
             nc.vector.memset(windows[j][:], 0.0)
-            nc.gpsimd.memset(windows[j + 1][:], 0.0)
         ident = keep.tile([P, P], F32)
         make_identity(nc, ident[:])
         dw_cols = keep.tile([P, BLOCKS * SQUARE], F32, align_bytes=64)
@@ -84,7 +81,9 @@ def tile_attend_gebag_kernel(tc, eT, W, dz, wc, offs, bagoffs, out_0, out_1):
         w_bf_01 = keep.tile([P, 2 * P, PACK], BF16, align_bytes=64)
         dz_bf = [keep.tile([P, X // 2, PACK], BF16, align_bytes=64, name="dz_bf%d" % h) for h in range(2)]
         w_bf_23 = keep.tile([P, 2 * P, PACK], BF16, align_bytes=64)
-        ub = [keep.tile([P, C], F32, name="ub%d" % j) for j in range(D_TILES)]
+        bagged_03 = keep.tile([P, C + P], F32)
+        bagged_12 = keep.tile([P, 2 * C], F32)
+        ub = [bagged_03[:, P:], bagged_12[:, :C], bagged_12[:, C:], bagged_03[:, :C]]
         u = [keep.tile([P, X], F32, name="u%d" % j) for j in range(D_TILES)]
 
         def cast(engine_copy, grouped, raw, lo, hi):
@@ -121,7 +120,8 @@ def tile_attend_gebag_kernel(tc, eT, W, dz, wc, offs, bagoffs, out_0, out_1):
             multiply(0, first[h][:], lo, hi)
             nc.scalar.copy(out=u[0][:, lo:hi], in_=first[h][:])
 
-        made = keep.tile([P, 6 * C], F32)
+        made = keep.tile([P, D_TILES * C], F32)
+        weighted = {j: keep.tile([P, C], F32, name="weighted%d" % j) for j in (0, 2, 3)}
         sums = [psum.tile([P, X], F32, name="sums%d" % b) for b in range(3)]
         spent = keep.tile([P, BLOCKS, P], F32)
 
@@ -134,16 +134,31 @@ def tile_attend_gebag_kernel(tc, eT, W, dz, wc, offs, bagoffs, out_0, out_1):
         def gather_u(j, lo, hi):
             nc.vector.tensor_copy(ub[j][:, lo:hi], bagged(j, lo, hi))
 
-        def weigh_and_scatter(j, lo, hi, at):
-            values = made[:, at : at + hi - lo]
-            nc.gpsimd.tensor_tensor(values, ub[j][:, lo:hi], wc_sb[:, lo:hi], MULT)
-            target = windows[j][:].indirect(offsets(idx_list, lo, hi))
-            if j == VECTOR_TILE:
-                nc.vector.tensor_copy(target, values)
-            else:
-                nc.scalar.activation(target, values, COPY)
+        def gather_u_on_scalar(j, lo, hi):
+            nc.scalar.activation(ub[j][:, lo:hi], bagged(j, lo, hi), COPY)
+
+        def listed(j, lo, hi):
+            return windows[j][:].indirect(offsets(idx_list, lo, hi))
+
+        def store(j, hi):
             if hi == C:
                 nc.sync.dma_start(out=out_0[j * P : (j + 1) * P, :], in_=windows[j][:])
+
+        def weigh(j, lo, hi):
+            nc.vector.tensor_tensor(weighted[j][:, lo:hi], ub[j][:, lo:hi], wc_sb[:, lo:hi], MULT)
+
+        def scatter(j, lo, hi):
+            nc.scalar.activation(listed(j, lo, hi), weighted[j][:, lo:hi], COPY)
+            store(j, hi)
+
+        def weigh_for_scalar(j, cut):
+            weigh(j, *cut)
+            scatter(j, *cut)
+
+        def scatter_on_vector(q):
+            lo, hi = q * PIECE, (q + 1) * PIECE
+            nc.vector.tensor_tensor(listed(1, lo, hi), ub[1][:, lo:hi], wc_sb[:, lo:hi], MULT)
+            store(1, hi)
 
         def bank(b):
             return (sums[0], b) if b < 4 else (sums[b // 2 - 1], b % 2)
@@ -179,38 +194,46 @@ def tile_attend_gebag_kernel(tc, eT, W, dz, wc, offs, bagoffs, out_0, out_1):
             pair = bank(b)[0][:, : 2 * P].rearrange("p (b i) -> p b i", i=P)
             nc.vector.tensor_reduce(out=columns, in_=pair, axis=mybir.AxisListType.X, op=ADD)
 
-        cuts = [(0, PIECE), (PIECE, PIECE + WIDE), (PIECE + WIDE, C)]
-        quarters = [(q * PIECE, (q + 1) * PIECE) for q in range(4)]
-        apart = 4 * C
+        first_cut, second_cut, third_cut = (0, PIECE), (PIECE, PIECE + WIDE), (PIECE + WIDE, C)
+        middle = (WIDE + C) // 2
 
         cast(nc.vector.tensor_copy, w_bf_23, w_raw_23, 0, 2 * P)
-        gather_u(0, *cuts[0])
+        gather_u(0, *first_cut)
         quantize(nc, w_bf_23[:], w_codes[:, 2 * P :], w_scales[:, 2 * P :], E4M3)
         make_u(1)
-        nc.scalar.activation(ub[1][:, :WIDE], bagged(1, 0, WIDE), COPY)
-        weigh_and_scatter(0, *cuts[0], apart)
+        gather_u_on_scalar(1, 0, WIDE)
+        weigh(0, *first_cut)
+        scatter(0, *first_cut)
         make_u(2)
         make_u(3)
-        gather_u(0, *cuts[1])
-        gather_u(0, *cuts[2])
-        gather_u(1, WIDE, WIDE + PIECE)
-        gather_u(2, *cuts[0])
-        gather_u(1, WIDE + PIECE, C)
-        gather_u(3, *cuts[0])
-        for cut in cuts[1:]:
-            gather_u(2, *cut)
-            gather_u(3, *cut)
-        weigh_and_scatter(0, *cuts[1], apart + PIECE)
-        turns = [(2, 0, 0), (0, 2, HALF), (3, 0, 2 * HALF), (2, 1, 4 * HALF - WIDE // 2)]
-        for q, (j, cut, at) in enumerate(turns):
-            weigh_and_scatter(VECTOR_TILE, *quarters[q], apart + C + q * PIECE)
-            weigh_and_scatter(j, *cuts[cut], at)
-            gather_table(q)
-        gather_table(4)
-        weigh_and_scatter(3, *cuts[1], 6 * HALF - WIDE // 2)
-        gather_table(5)
-        weigh_and_scatter(2, *cuts[2], 7 * HALF + PIECE - WIDE // 2)
-        weigh_and_scatter(3, *cuts[2], apart + PIECE + WIDE)
+        gather_u(0, *second_cut)
+        gather_u(0, *third_cut)
+        weigh(0, *second_cut)
+        scatter(0, *second_cut)
+        gather_u(2, *first_cut)
+        gather_u(1, WIDE, middle)
+        weigh_for_scalar(2, first_cut)
+        scatter_on_vector(0)
+        gather_table(0)
+        gather_u_on_scalar(3, *second_cut)
+        weigh_for_scalar(0, third_cut)
+        scatter_on_vector(1)
+        gather_table(1)
+        gather_u_on_scalar(3, *third_cut)
+        gather_u(3, *first_cut)
+        gather_u(2, *second_cut)
+        weigh_for_scalar(3, first_cut)
+        weigh_for_scalar(2, second_cut)
+        gather_u(1, middle, C)
+        weigh_for_scalar(3, second_cut)
+        scatter_on_vector(2)
+        gather_u(2, *third_cut)
+        scatter_on_vector(3)
+        weigh_for_scalar(2, third_cut)
+        gather_table(2)
+        weigh_for_scalar(3, third_cut)
+        for g in (3, 4, 5):
+            gather_table(g)
         for b in range(4):
             sum_on_scalar(b)
         gather_table(6)

@@ -26,6 +26,10 @@ HALF = C // 2
 PIECE = C // 4
 DZ_VECTOR_SHARE = 160
 WIDE = 384
+GAP = 192
+LATE = 160
+UB3_AT = 64
+UB2_AT = 1312
 
 
 def interleave_views(grouped, raw, lo, hi):
@@ -81,9 +85,6 @@ def tile_attend_gebag_kernel(tc, eT, W, dz, wc, offs, bagoffs, out_0, out_1):
         w_bf_01 = keep.tile([P, 2 * P, PACK], BF16, align_bytes=64)
         dz_bf = [keep.tile([P, X // 2, PACK], BF16, align_bytes=64, name="dz_bf%d" % h) for h in range(2)]
         w_bf_23 = keep.tile([P, 2 * P, PACK], BF16, align_bytes=64)
-        bagged_03 = keep.tile([P, C + P], F32)
-        bagged_12 = keep.tile([P, 2 * C], F32)
-        ub = [bagged_03[:, P:], bagged_12[:, :C], bagged_12[:, C:], bagged_03[:, :C]]
         u = [keep.tile([P, X], F32, name="u%d" % j) for j in range(D_TILES)]
 
         def cast(engine_copy, grouped, raw, lo, hi):
@@ -121,9 +122,21 @@ def tile_attend_gebag_kernel(tc, eT, W, dz, wc, offs, bagoffs, out_0, out_1):
             nc.scalar.copy(out=u[0][:, lo:hi], in_=first[h][:])
 
         made = keep.tile([P, D_TILES * C], F32)
-        weighted = {j: keep.tile([P, C], F32, name="weighted%d" % j) for j in (0, 2, 3)}
         sums = [psum.tile([P, X], F32, name="sums%d" % b) for b in range(3)]
         spent = keep.tile([P, BLOCKS, P], F32)
+        ub0 = keep.tile([P, C], F32)
+        ub1 = keep.tile([P, C], F32)
+        ub2_head = keep.tile([P, HALF], F32)
+        de01 = keep.tile([P, 2 * C], F32)
+        de2 = keep.tile([P, C], F32)
+        de = [de01[:, :C], de01[:, C:], de2[:]]
+
+        def ub(j, lo, hi):
+            if j == 3:
+                return de01[:, UB3_AT + lo : UB3_AT + hi]
+            if j == 2 and lo >= HALF:
+                return de01[:, UB2_AT + lo - HALF : UB2_AT + hi - HALF]
+            return (ub0, ub1, ub2_head)[j][:, lo:hi]
 
         def offsets(listed, lo, hi):
             return listed[:, lo // 16 : hi // 16]
@@ -132,10 +145,10 @@ def tile_attend_gebag_kernel(tc, eT, W, dz, wc, offs, bagoffs, out_0, out_1):
             return u[j][:].indirect(offsets(bag_list, lo, hi))
 
         def gather_u(j, lo, hi):
-            nc.vector.tensor_copy(ub[j][:, lo:hi], bagged(j, lo, hi))
+            nc.vector.tensor_copy(ub(j, lo, hi), bagged(j, lo, hi))
 
         def gather_u_on_scalar(j, lo, hi):
-            nc.scalar.activation(ub[j][:, lo:hi], bagged(j, lo, hi), COPY)
+            nc.scalar.activation(ub(j, lo, hi), bagged(j, lo, hi), COPY)
 
         def listed(j, lo, hi):
             return windows[j][:].indirect(offsets(idx_list, lo, hi))
@@ -145,34 +158,28 @@ def tile_attend_gebag_kernel(tc, eT, W, dz, wc, offs, bagoffs, out_0, out_1):
                 nc.sync.dma_start(out=out_0[j * P : (j + 1) * P, :], in_=windows[j][:])
 
         def weigh(j, lo, hi):
-            nc.vector.tensor_tensor(weighted[j][:, lo:hi], ub[j][:, lo:hi], wc_sb[:, lo:hi], MULT)
+            nc.vector.tensor_tensor(de[j][:, lo:hi], ub(j, lo, hi), wc_sb[:, lo:hi], MULT)
 
         def scatter(j, lo, hi):
-            nc.scalar.activation(listed(j, lo, hi), weighted[j][:, lo:hi], COPY)
+            nc.scalar.activation(listed(j, lo, hi), de[j][:, lo:hi], COPY)
             store(j, hi)
-
-        def weigh_for_scalar(j, cut):
-            weigh(j, *cut)
-            scatter(j, *cut)
 
         def scatter_on_vector(q):
             lo, hi = q * PIECE, (q + 1) * PIECE
-            nc.vector.tensor_tensor(listed(1, lo, hi), ub[1][:, lo:hi], wc_sb[:, lo:hi], MULT)
-            store(1, hi)
+            nc.vector.tensor_tensor(listed(3, lo, hi), ub(3, lo, hi), wc_sb[:, lo:hi], MULT)
+            store(3, hi)
 
         def bank(b):
             return (sums[0], b) if b < 4 else (sums[b // 2 - 1], b % 2)
 
-        def gather_table(g, lo=0, hi=HALF):
-            j, h = divmod(g, 2) if g < 4 else (2 + g % 2, (g - 4) // 2)
-            values = made[:, g * HALF + lo : g * HALF + hi]
-            looked_up = table[j][:].indirect(offsets(idx_list, h * HALF + lo, h * HALF + hi))
-            nc.vector.tensor_tensor(values, looked_up, ub[j][:, h * HALF + lo : h * HALF + hi], MULT)
-            for b in range((h * HALF + lo) // P, (h * HALF + hi) // P):
+        def gather_table(j, lo, hi):
+            looked_up = table[j][:].indirect(offsets(idx_list, lo, hi))
+            nc.vector.tensor_tensor(made[:, j * C + lo : j * C + hi], looked_up, ub(j, lo, hi), MULT)
+            for b in range(lo // P, hi // P):
                 tile, place = bank(b)
                 nc.tensor.matmul(
                     tile[:, place * P : (place + 1) * P],
-                    lhsT=made[:, g * HALF + b * P - h * HALF : g * HALF + (b + 1) * P - h * HALF],
+                    lhsT=made[:, j * C + b * P : j * C + (b + 1) * P],
                     rhs=ident[:],
                     is_transpose=True,
                     start=(j == 0 and place == 0),
@@ -194,53 +201,58 @@ def tile_attend_gebag_kernel(tc, eT, W, dz, wc, offs, bagoffs, out_0, out_1):
             pair = bank(b)[0][:, : 2 * P].rearrange("p (b i) -> p b i", i=P)
             nc.vector.tensor_reduce(out=columns, in_=pair, axis=mybir.AxisListType.X, op=ADD)
 
-        first_cut, second_cut, third_cut = (0, PIECE), (PIECE, PIECE + WIDE), (PIECE + WIDE, C)
-        middle = (WIDE + C) // 2
+        def piece(q):
+            return q * PIECE, (q + 1) * PIECE
 
         cast(nc.vector.tensor_copy, w_bf_23, w_raw_23, 0, 2 * P)
-        gather_u(0, *first_cut)
-        quantize(nc, w_bf_23[:], w_codes[:, 2 * P :], w_scales[:, 2 * P :], E4M3)
+        nc.vector.tensor_tensor(de[0][:, :PIECE], bagged(0, 0, PIECE), wc_sb[:, :PIECE], MULT)
         make_u(1)
-        gather_u_on_scalar(1, 0, WIDE)
-        weigh(0, *first_cut)
-        scatter(0, *first_cut)
+        scatter(0, *piece(0))
+        gather_u_on_scalar(1, 0, GAP)
+        quantize(nc, w_bf_23[:], w_codes[:, 2 * P :], w_scales[:, 2 * P :], E4M3)
         make_u(2)
         make_u(3)
-        gather_u(0, *second_cut)
-        gather_u(0, *third_cut)
-        weigh(0, *second_cut)
-        scatter(0, *second_cut)
-        gather_u(2, *first_cut)
-        gather_u(1, WIDE, middle)
-        weigh_for_scalar(2, first_cut)
-        scatter_on_vector(0)
-        gather_table(0)
-        gather_u_on_scalar(3, *second_cut)
-        weigh_for_scalar(0, third_cut)
-        scatter_on_vector(1)
-        gather_table(1)
-        gather_u_on_scalar(3, *third_cut)
-        gather_u(3, *first_cut)
-        gather_u(2, *second_cut)
-        weigh_for_scalar(3, first_cut)
-        weigh_for_scalar(2, second_cut)
+        gather_u(0, PIECE, PIECE + WIDE)
+        gather_u(0, PIECE + WIDE, C)
+        weigh(0, PIECE, PIECE + WIDE)
+        gather_u(0, 0, PIECE)
+        weigh(0, PIECE + WIDE, C)
+        middle = (GAP + C) // 2
+        gather_u(1, GAP, middle)
         gather_u(1, middle, C)
-        weigh_for_scalar(3, second_cut)
+        weigh(1, 0, middle)
+        weigh(1, middle, C)
+        for k in range(1, 6):
+            scatter(k // 4, *piece(k % 4))
+            gather_u_on_scalar(3, (k - 1) * GAP, k * GAP if k < 5 else C)
+        gather_table(0, 0, HALF)
+        for q in range(2):
+            scatter_on_vector(q)
+            gather_u(2, *piece(q))
+            gather_table(q, (1 - q) * HALF, (2 - q) * HALF)
+            weigh(2, *piece(q))
+        scatter(1, *piece(2))
+        gather_u_on_scalar(2, HALF, HALF + LATE)
+        scatter(1, *piece(3))
+        gather_u_on_scalar(2, HALF + LATE, HALF + 2 * LATE)
+        scatter(2, *piece(0))
+        gather_u_on_scalar(2, HALF + 2 * LATE, C)
         scatter_on_vector(2)
-        gather_u(2, *third_cut)
+        gather_table(1, HALF, C)
+        weigh(2, HALF, HALF + LATE)
+        scatter(2, PIECE, PIECE + WIDE)
         scatter_on_vector(3)
-        weigh_for_scalar(2, third_cut)
-        gather_table(2)
-        weigh_for_scalar(3, third_cut)
-        for g in (3, 4, 5):
-            gather_table(g)
+        gather_table(2, 0, HALF)
+        weigh(2, HALF + LATE, C)
+        scatter(2, PIECE + WIDE, C)
+        gather_table(3, 0, HALF)
         for b in range(4):
             sum_on_scalar(b)
-        gather_table(6)
-        gather_table(7, 0, PIECE)
+        gather_table(2, HALF, C)
+        gather_table(3, HALF, HALF + PIECE)
         sum_on_scalar(4)
         sum_on_scalar(5)
-        gather_table(7, PIECE, HALF)
+        gather_table(3, HALF + PIECE, C)
         sum_on_vector(6)
 
         dw_rows = keep.tile([P, BLOCKS * SQUARE], F32, align_bytes=64)

@@ -26,10 +26,6 @@ HALF = C // 2
 PIECE = C // 4
 DZ_VECTOR_SHARE = 160
 WIDE = 384
-GAP = 192
-LATE = 160
-UB3_AT = 64
-UB2_AT = 1312
 
 
 def interleave_views(grouped, raw, lo, hi):
@@ -67,7 +63,7 @@ def tile_attend_gebag_kernel(tc, eT, W, dz, wc, offs, bagoffs, out_0, out_1):
         nc.sync.dma_start(out=w_raw_23[:], in_=W_rows[:, :, 2 * P :])
         nc.sync.dma_start(idx_list[:], offs)
         nc.sync.dma_start(out=wc_sb[:], in_=wc)
-        for j in range(D_TILES):
+        for j in (0, 1, 3, 2):
             nc.sync.dma_start(out=table[j][:], in_=eT[j * P : (j + 1) * P, :])
 
         windows = [keep.tile([P, T], F32, name="window%d" % j) for j in range(D_TILES)]
@@ -123,20 +119,14 @@ def tile_attend_gebag_kernel(tc, eT, W, dz, wc, offs, bagoffs, out_0, out_1):
 
         made = keep.tile([P, D_TILES * C], F32)
         sums = [psum.tile([P, X], F32, name="sums%d" % b) for b in range(3)]
-        spent = keep.tile([P, BLOCKS, P], F32)
         ub0 = keep.tile([P, C], F32)
         ub1 = keep.tile([P, C], F32)
-        ub2_head = keep.tile([P, HALF], F32)
         de01 = keep.tile([P, 2 * C], F32)
         de2 = keep.tile([P, C], F32)
         de = [de01[:, :C], de01[:, C:], de2[:]]
 
         def ub(j, lo, hi):
-            if j == 3:
-                return de01[:, UB3_AT + lo : UB3_AT + hi]
-            if j == 2 and lo >= HALF:
-                return de01[:, UB2_AT + lo - HALF : UB2_AT + hi - HALF]
-            return (ub0, ub1, ub2_head)[j][:, lo:hi]
+            return (ub0[:], ub1[:], de[1], de[0])[j][:, lo:hi]
 
         def offsets(listed, lo, hi):
             return listed[:, lo // 16 : hi // 16]
@@ -183,7 +173,7 @@ def tile_attend_gebag_kernel(tc, eT, W, dz, wc, offs, bagoffs, out_0, out_1):
                     rhs=ident[:],
                     is_transpose=True,
                     start=(j == 0 and place == 0),
-                    stop=(j == D_TILES - 1 and b in (3, 5, 7)),
+                    stop=(j == 2 and b in (3, 5, 7)),
                 )
 
         def column(b):
@@ -194,7 +184,7 @@ def tile_attend_gebag_kernel(tc, eT, W, dz, wc, offs, bagoffs, out_0, out_1):
             return tile[:, place * P : (place + 1) * P]
 
         def sum_on_scalar(b):
-            nc.scalar.activation(out=spent[:, b, :], in_=summed(b), func=COPY, accum_out=column(b))
+            nc.scalar.activation(out=de2[:, C - (b + 1) * P : C - b * P], in_=summed(b), func=COPY, accum_out=column(b))
 
         def sum_on_vector(b):
             columns = dw_cols[:, b * SQUARE : (b + 2) * SQUARE : SQUARE]
@@ -208,7 +198,7 @@ def tile_attend_gebag_kernel(tc, eT, W, dz, wc, offs, bagoffs, out_0, out_1):
         nc.vector.tensor_tensor(de[0][:, :PIECE], bagged(0, 0, PIECE), wc_sb[:, :PIECE], MULT)
         make_u(1)
         scatter(0, *piece(0))
-        gather_u_on_scalar(1, 0, GAP)
+        gather_u_on_scalar(1, *piece(0))
         quantize(nc, w_bf_23[:], w_codes[:, 2 * P :], w_scales[:, 2 * P :], E4M3)
         make_u(2)
         make_u(3)
@@ -217,42 +207,33 @@ def tile_attend_gebag_kernel(tc, eT, W, dz, wc, offs, bagoffs, out_0, out_1):
         weigh(0, PIECE, PIECE + WIDE)
         gather_u(0, 0, PIECE)
         weigh(0, PIECE + WIDE, C)
-        middle = (GAP + C) // 2
-        gather_u(1, GAP, middle)
-        gather_u(1, middle, C)
-        weigh(1, 0, middle)
-        weigh(1, middle, C)
-        for k in range(1, 6):
+        gather_u(1, PIECE, PIECE + WIDE)
+        gather_u(1, PIECE + WIDE, C)
+        weigh(1, 0, PIECE + WIDE)
+        weigh(1, PIECE + WIDE, C)
+        for k in range(1, 8):
             scatter(k // 4, *piece(k % 4))
-            gather_u_on_scalar(3, (k - 1) * GAP, k * GAP if k < 5 else C)
-        gather_table(0, 0, HALF)
-        for q in range(2):
+            gather_u_on_scalar(3 - k // 5, *piece((k - 1) % 4))
+        for q in range(4):
+            gather_table(q // 2, q % 2 * HALF, (q % 2 + 1) * HALF)
+            if q == 3:
+                weigh(2, 0, WIDE)
             scatter_on_vector(q)
-            gather_u(2, *piece(q))
-            gather_table(q, (1 - q) * HALF, (2 - q) * HALF)
-            weigh(2, *piece(q))
-        scatter(1, *piece(2))
-        gather_u_on_scalar(2, HALF, HALF + LATE)
-        scatter(1, *piece(3))
-        gather_u_on_scalar(2, HALF + LATE, HALF + 2 * LATE)
-        scatter(2, *piece(0))
-        gather_u_on_scalar(2, HALF + 2 * LATE, C)
-        scatter_on_vector(2)
-        gather_table(1, HALF, C)
-        weigh(2, HALF, HALF + LATE)
-        scatter(2, PIECE, PIECE + WIDE)
-        scatter_on_vector(3)
-        gather_table(2, 0, HALF)
-        weigh(2, HALF + LATE, C)
-        scatter(2, PIECE + WIDE, C)
+        scatter(2, 0, WIDE)
+        gather_u_on_scalar(2, *piece(3))
         gather_table(3, 0, HALF)
+        weigh(2, WIDE, 2 * WIDE)
+        scatter(2, WIDE, 2 * WIDE)
+        gather_table(2, 0, HALF)
+        weigh(2, 2 * WIDE, C)
+        scatter(2, 2 * WIDE, C)
         for b in range(4):
             sum_on_scalar(b)
-        gather_table(2, HALF, C)
-        gather_table(3, HALF, HALF + PIECE)
+        gather_table(3, HALF, C)
+        gather_table(2, HALF, HALF + PIECE)
         sum_on_scalar(4)
         sum_on_scalar(5)
-        gather_table(3, HALF + PIECE, C)
+        gather_table(2, HALF + PIECE, C)
         sum_on_vector(6)
 
         dw_rows = keep.tile([P, BLOCKS * SQUARE], F32, align_bytes=64)

@@ -61,9 +61,10 @@ def tile_attend_gebag_kernel(tc, eT, W, dz, wc, offs, bagoffs, out_0, out_1):
             nc.sync.dma_start(out=dz_raw[h][:], in_=dz_rows[:, :, h * X // 2 : (h + 1) * X // 2])
         nc.sync.dma_start(bag_list[:], bagoffs)
         nc.sync.dma_start(out=w_raw_23[:], in_=W_rows[:, :, 2 * P :])
+        nc.sync.dma_start(out=wc_sb[:, :PIECE], in_=wc[:, :PIECE])
         nc.sync.dma_start(idx_list[:], offs)
-        nc.sync.dma_start(out=wc_sb[:], in_=wc)
-        for j in (0, 1, 3, 2):
+        nc.sync.dma_start(out=wc_sb[:, PIECE:], in_=wc[:, PIECE:])
+        for j in (3, 0, 1, 2):
             nc.sync.dma_start(out=table[j][:], in_=eT[j * P : (j + 1) * P, :])
 
         windows = [keep.tile([P, T], F32, name="window%d" % j) for j in range(D_TILES)]
@@ -122,11 +123,17 @@ def tile_attend_gebag_kernel(tc, eT, W, dz, wc, offs, bagoffs, out_0, out_1):
         ub0 = keep.tile([P, C], F32)
         ub1 = keep.tile([P, C], F32)
         de01 = keep.tile([P, 2 * C], F32)
-        de2 = keep.tile([P, C], F32)
-        de = [de01[:, :C], de01[:, C:], de2[:]]
 
         def ub(j, lo, hi):
-            return (ub0[:], ub1[:], de[1], de[0])[j][:, lo:hi]
+            if j == 2:
+                at = C + (lo + PIECE) % C
+                return de01[:, at : at + hi - lo]
+            return (ub0, ub1, None, de01)[j][:, lo:hi]
+
+        def de(j, lo, hi):
+            if j < 2:
+                return de01[:, j * C + lo : j * C + hi]
+            return (de01[:, :PIECE], ub0[:, :PIECE], ub1[:, :PIECE])[lo // PIECE]
 
         def offsets(listed, lo, hi):
             return listed[:, lo // 16 : hi // 16]
@@ -143,21 +150,17 @@ def tile_attend_gebag_kernel(tc, eT, W, dz, wc, offs, bagoffs, out_0, out_1):
         def listed(j, lo, hi):
             return windows[j][:].indirect(offsets(idx_list, lo, hi))
 
-        def store(j, hi):
-            if hi == C:
-                nc.sync.dma_start(out=out_0[j * P : (j + 1) * P, :], in_=windows[j][:])
+        def store(j):
+            nc.sync.dma_start(out=out_0[j * P : (j + 1) * P, :], in_=windows[j][:])
 
         def weigh(j, lo, hi):
-            nc.vector.tensor_tensor(de[j][:, lo:hi], ub(j, lo, hi), wc_sb[:, lo:hi], MULT)
+            nc.vector.tensor_tensor(de(j, lo, hi), ub(j, lo, hi), wc_sb[:, lo:hi], MULT)
 
         def scatter(j, lo, hi):
-            nc.scalar.activation(listed(j, lo, hi), de[j][:, lo:hi], COPY)
-            store(j, hi)
+            nc.scalar.activation(listed(j, lo, hi), de(j, lo, hi), COPY)
 
-        def scatter_on_vector(q):
-            lo, hi = q * PIECE, (q + 1) * PIECE
-            nc.vector.tensor_tensor(listed(3, lo, hi), ub(3, lo, hi), wc_sb[:, lo:hi], MULT)
-            store(3, hi)
+        def scatter_on_vector(j, lo, hi):
+            nc.vector.tensor_tensor(listed(j, lo, hi), ub(j, lo, hi), wc_sb[:, lo:hi], MULT)
 
         def bank(b):
             return (sums[0], b) if b < 4 else (sums[b // 2 - 1], b % 2)
@@ -172,30 +175,20 @@ def tile_attend_gebag_kernel(tc, eT, W, dz, wc, offs, bagoffs, out_0, out_1):
                     lhsT=made[:, j * C + b * P : j * C + (b + 1) * P],
                     rhs=ident[:],
                     is_transpose=True,
-                    start=(j == 0 and place == 0),
+                    start=(j == 3 and place == 0),
                     stop=(j == 2 and b in (3, 5, 7)),
                 )
 
-        def column(b):
-            return dw_cols[:, b * SQUARE : b * SQUARE + 1]
-
-        def summed(b):
-            tile, place = bank(b)
-            return tile[:, place * P : (place + 1) * P]
-
-        def sum_on_scalar(b):
-            nc.scalar.activation(out=de2[:, C - (b + 1) * P : C - b * P], in_=summed(b), func=COPY, accum_out=column(b))
-
-        def sum_on_vector(b):
-            columns = dw_cols[:, b * SQUARE : (b + 2) * SQUARE : SQUARE]
-            pair = bank(b)[0][:, : 2 * P].rearrange("p (b i) -> p b i", i=P)
-            nc.vector.tensor_reduce(out=columns, in_=pair, axis=mybir.AxisListType.X, op=ADD)
+        def sum_on_vector(b, count):
+            columns = dw_cols[:, b * SQUARE : (b + count) * SQUARE : SQUARE]
+            blocks = bank(b)[0][:, : count * P].rearrange("p (b i) -> p b i", i=P)
+            nc.vector.tensor_reduce(out=columns, in_=blocks, axis=mybir.AxisListType.X, op=ADD)
 
         def piece(q):
             return q * PIECE, (q + 1) * PIECE
 
         cast(nc.vector.tensor_copy, w_bf_23, w_raw_23, 0, 2 * P)
-        nc.vector.tensor_tensor(de[0][:, :PIECE], bagged(0, 0, PIECE), wc_sb[:, :PIECE], MULT)
+        nc.vector.tensor_tensor(de(0, *piece(0)), bagged(0, *piece(0)), wc_sb[:, :PIECE], MULT)
         make_u(1)
         scatter(0, *piece(0))
         gather_u_on_scalar(1, *piece(0))
@@ -205,7 +198,7 @@ def tile_attend_gebag_kernel(tc, eT, W, dz, wc, offs, bagoffs, out_0, out_1):
         gather_u(0, PIECE, PIECE + WIDE)
         gather_u(0, PIECE + WIDE, C)
         weigh(0, PIECE, PIECE + WIDE)
-        gather_u(0, 0, PIECE)
+        gather_u(0, *piece(0))
         weigh(0, PIECE + WIDE, C)
         gather_u(1, PIECE, PIECE + WIDE)
         gather_u(1, PIECE + WIDE, C)
@@ -213,28 +206,35 @@ def tile_attend_gebag_kernel(tc, eT, W, dz, wc, offs, bagoffs, out_0, out_1):
         weigh(1, PIECE + WIDE, C)
         for k in range(1, 8):
             scatter(k // 4, *piece(k % 4))
-            gather_u_on_scalar(3 - k // 5, *piece((k - 1) % 4))
+            if k % 4 == 3:
+                store(k // 4)
+            if k < 5:
+                gather_u_on_scalar(3, *piece(k - 1))
+            else:
+                gather_u_on_scalar(2, *piece((k - 6) % 4))
         for q in range(4):
-            gather_table(q // 2, q % 2 * HALF, (q % 2 + 1) * HALF)
-            if q == 3:
-                weigh(2, 0, WIDE)
-            scatter_on_vector(q)
-        scatter(2, 0, WIDE)
-        gather_u_on_scalar(2, *piece(3))
-        gather_table(3, 0, HALF)
-        weigh(2, WIDE, 2 * WIDE)
-        scatter(2, WIDE, 2 * WIDE)
+            scatter_on_vector(3, *piece(q))
+            gather_table(3, *piece(q))
+        store(3)
+        scatter_on_vector(2, *piece(3))
+        gather_table(0, *piece(0))
+        weigh(2, *piece(0))
+        scatter(2, *piece(0))
+        gather_u_on_scalar(2, *piece(2))
+        gather_table(0, PIECE, C)
+        weigh(2, *piece(1))
+        scatter(2, *piece(1))
+        gather_table(1, 0, HALF)
         gather_table(2, 0, HALF)
-        weigh(2, 2 * WIDE, C)
-        scatter(2, 2 * WIDE, C)
-        for b in range(4):
-            sum_on_scalar(b)
-        gather_table(3, HALF, C)
-        gather_table(2, HALF, HALF + PIECE)
-        sum_on_scalar(4)
-        sum_on_scalar(5)
-        gather_table(2, HALF + PIECE, C)
-        sum_on_vector(6)
+        weigh(2, *piece(2))
+        scatter(2, *piece(2))
+        store(2)
+        gather_table(1, HALF, C)
+        sum_on_vector(0, 4)
+        gather_table(2, *piece(2))
+        gather_table(2, *piece(3))
+        sum_on_vector(4, 2)
+        sum_on_vector(6, 2)
 
         dw_rows = keep.tile([P, BLOCKS * SQUARE], F32, align_bytes=64)
         nc.vector.transpose(dw_rows[:], dw_cols[:])

@@ -225,14 +225,15 @@ def tile_attend_gebag_kernel(tc, eT, W, dz, wc, offs, bagoffs, out_0, out_1):
         weigh(2, *piece(1))
         scatter(2, *piece(1))
         gather_table(1, 0, HALF)
-        gather_table(2, 0, HALF)
+        gather_table(1, *piece(2))
         weigh(2, *piece(2))
         scatter(2, *piece(2))
         store(2)
-        gather_table(1, HALF, C)
-        sum_on_vector(0, 4)
+        gather_table(1, *piece(3))
+        gather_table(2, 0, HALF)
         gather_table(2, *piece(2))
         gather_table(2, *piece(3))
+        sum_on_vector(0, 4)
         sum_on_vector(4, 2)
         sum_on_vector(6, 2)
 

from contextlib import ExitStack

import concourse.mybir as mybir
from concourse.masks import make_identity

M, D, X, C, T = 512, 512, 512, 1024, 2048
FLOPS = 2 * M * D * X

F32 = mybir.dt.float32
BF16 = mybir.dt.bfloat16
U32 = mybir.dt.uint32
U16 = mybir.dt.uint16
U8 = mybir.dt.uint8
E4M3 = mybir.dt.float8_e4m3fn_x4
E5M2 = mybir.dt.float8_e5m2_x4
MULT = mybir.AluOpType.mult
ADD = mybir.AluOpType.add
COPY = mybir.ActivationFunctionType.Copy

P = 128
PACK = 4
SQUARE = 32
D_TILES = D // P
BLOCKS = C // P
HALF = C // 2
PIECE = C // 4
DZ_VECTOR_SHARE = 160
WIDE = 384


def interleave_views(grouped, raw, lo, hi):
    dst = grouped[:, lo:hi, :].rearrange("p (c i) t -> p c t i", i=PACK)
    src = raw[:, :, lo:hi].rearrange("p t (c i) -> p c t i", i=PACK)
    return dst, src


def quantize(nc, grouped, codes, scales, fmt):
    nc.vector.quantize_mx(out=codes.bitcast(fmt), scales=scales, in_=grouped.rearrange("p c t -> p (c t)"))


def tile_attend_gebag_kernel(tc, eT, W, dz, wc, offs, bagoffs, out_0, out_1):
    nc = tc.nc
    with ExitStack() as ctx:
        keep = ctx.enter_context(tc.tile_pool(name="keep", bufs=1))
        psum = ctx.enter_context(tc.psum_pool(name="psum", bufs=1))
        psum_u = ctx.enter_context(tc.psum_pool(name="psum_u", bufs=2))

        W_rows = W.rearrange("(p t) c -> p t c", t=PACK)
        dz_rows = dz.rearrange("(p t) c -> p t c", t=PACK)

        dz_raw = [keep.tile([P, PACK, X // 2], F32, name="dz_raw%d" % h) for h in range(2)]
        w_raw_01 = keep.tile([P, PACK, 2 * P], F32)
        w_raw_23 = keep.tile([P, PACK, 2 * P], F32)
        bag_list = keep.tile([P, C // 16], U16)
        idx_list = keep.tile([P, C // 16], U16)
        wc_sb = keep.tile([P, C], F32)
        table = [keep.tile([P, T], F32, name="table%d" % j) for j in range(D_TILES)]

        nc.sync.dma_start(out=w_raw_01[:], in_=W_rows[:, :, : 2 * P])
        for h in range(2):
            nc.sync.dma_start(out=dz_raw[h][:], in_=dz_rows[:, :, h * X // 2 : (h + 1) * X // 2])
        nc.sync.dma_start(bag_list[:], bagoffs)
        nc.sync.dma_start(out=w_raw_23[:], in_=W_rows[:, :, 2 * P :])
        nc.sync.dma_start(out=wc_sb[:, :PIECE], in_=wc[:, :PIECE])
        nc.sync.dma_start(idx_list[:], offs)
        nc.sync.dma_start(out=wc_sb[:, PIECE:], in_=wc[:, PIECE:])
        for j in (3, 0, 1, 2):
            nc.sync.dma_start(out=table[j][:], in_=eT[j * P : (j + 1) * P, :])

        windows = [keep.tile([P, T], F32, name="window%d" % j) for j in range(D_TILES)]
        for j in (0, 2, 1, 3):
            nc.vector.memset(windows[j][:], 0.0)
        ident = keep.tile([P, P], F32)
        make_identity(nc, ident[:])
        dw_cols = keep.tile([P, BLOCKS * SQUARE], F32, align_bytes=64)
        nc.gpsimd.memset(dw_cols[:], 0.0)

        dz_codes = keep.tile([P, X], U32, align_bytes=64)
        dz_scales = keep.tile([P, X], U8, align_bytes=64)
        w_codes = keep.tile([P, D], U32, align_bytes=64)
        w_scales = keep.tile([P, D], U8, align_bytes=64)
        w_bf_01 = keep.tile([P, 2 * P, PACK], BF16, align_bytes=64)
        dz_bf = [keep.tile([P, X // 2, PACK], BF16, align_bytes=64, name="dz_bf%d" % h) for h in range(2)]
        w_bf_23 = keep.tile([P, 2 * P, PACK], BF16, align_bytes=64)
        u = [keep.tile([P, X], F32, name="u%d" % j) for j in range(D_TILES)]

        def cast(engine_copy, grouped, raw, lo, hi):
            dst, src = interleave_views(grouped, raw, lo, hi)
            engine_copy(out=dst, in_=src)

        def scalar_cast(out, in_):
            nc.scalar.activation(out=out, in_=in_, func=COPY)

        def multiply(j, acc, lo, hi):
            nc.tensor.matmul_mx(
                out=acc,
                lhsT=w_codes[:, j * P : (j + 1) * P].bitcast(E4M3),
                lhsT_scale=w_scales[:, j * P : (j + 1) * P],
                rhs=dz_codes[:, lo:hi].bitcast(E5M2),
                rhs_scale=dz_scales[:, lo:hi],
                start=True,
                stop=True,
            )

        def make_u(j):
            acc = psum_u.tile([P, X], F32, name="acc")
            multiply(j, acc[:], 0, X)
            nc.scalar.copy(out=u[j][:], in_=acc[:])

        cast(scalar_cast, w_bf_01, w_raw_01, 0, 2 * P)
        quantize(nc, w_bf_01[:], w_codes[:, : 2 * P], w_scales[:, : 2 * P], E4M3)
        first = [psum.tile([P, X // 2], F32, name="first%d" % h) for h in range(2)]
        for h in range(2):
            lo, hi = h * X // 2, (h + 1) * X // 2
            cast(nc.vector.tensor_copy, dz_bf[h], dz_raw[h], 0, DZ_VECTOR_SHARE)
            cast(scalar_cast, dz_bf[h], dz_raw[h], DZ_VECTOR_SHARE, X // 2)
            quantize(nc, dz_bf[h][:], dz_codes[:, lo:hi], dz_scales[:, lo:hi], E5M2)
            multiply(0, first[h][:], lo, hi)
            nc.scalar.copy(out=u[0][:, lo:hi], in_=first[h][:])

        made = keep.tile([P, D_TILES * C], F32)
        sums = [psum.tile([P, X], F32, name="sums%d" % b) for b in range(3)]
        ub0 = keep.tile([P, C], F32)
        ub1 = keep.tile([P, C], F32)
        de01 = keep.tile([P, 2 * C], F32)

        def ub(j, lo, hi):
            if j == 2:
                at = C + (lo + PIECE) % C
                return de01[:, at : at + hi - lo]
            return (ub0, ub1, None, de01)[j][:, lo:hi]

        def de(j, lo, hi):
            if j < 2:
                return de01[:, j * C + lo : j * C + hi]
            return (de01[:, :PIECE], ub0[:, :PIECE], ub1[:, :PIECE])[lo // PIECE]

        def offsets(listed, lo, hi):
            return listed[:, lo // 16 : hi // 16]

        def bagged(j, lo, hi):
            return u[j][:].indirect(offsets(bag_list, lo, hi))

        def gather_u(j, lo, hi):
            nc.vector.tensor_copy(ub(j, lo, hi), bagged(j, lo, hi))

        def gather_u_on_scalar(j, lo, hi):
            nc.scalar.activation(ub(j, lo, hi), bagged(j, lo, hi), COPY)

        def listed(j, lo, hi):
            return windows[j][:].indirect(offsets(idx_list, lo, hi))

        def store(j):
            nc.sync.dma_start(out=out_0[j * P : (j + 1) * P, :], in_=windows[j][:])

        def weigh(j, lo, hi):
            nc.vector.tensor_tensor(de(j, lo, hi), ub(j, lo, hi), wc_sb[:, lo:hi], MULT)

        def scatter(j, lo, hi):
            nc.scalar.activation(listed(j, lo, hi), de(j, lo, hi), COPY)

        def scatter_on_vector(j, lo, hi):
            nc.vector.tensor_tensor(listed(j, lo, hi), ub(j, lo, hi), wc_sb[:, lo:hi], MULT)

        def bank(b):
            return (sums[0], b) if b < 4 else (sums[b // 2 - 1], b % 2)

        def gather_table(j, lo, hi):
            looked_up = table[j][:].indirect(offsets(idx_list, lo, hi))
            nc.vector.tensor_tensor(made[:, j * C + lo : j * C + hi], looked_up, ub(j, lo, hi), MULT)
            for b in range(lo // P, hi // P):
                tile, place = bank(b)
                nc.tensor.matmul(
                    tile[:, place * P : (place + 1) * P],
                    lhsT=made[:, j * C + b * P : j * C + (b + 1) * P],
                    rhs=ident[:],
                    is_transpose=True,
                    start=(j == 3 and place == 0),
                    stop=(j == 2 and b in (3, 5, 7)),
                )

        def sum_on_vector(b, count):
            columns = dw_cols[:, b * SQUARE : (b + count) * SQUARE : SQUARE]
            blocks = bank(b)[0][:, : count * P].rearrange("p (b i) -> p b i", i=P)
            nc.vector.tensor_reduce(out=columns, in_=blocks, axis=mybir.AxisListType.X, op=ADD)

        def piece(q):
            return q * PIECE, (q + 1) * PIECE

        cast(nc.vector.tensor_copy, w_bf_23, w_raw_23, 0, 2 * P)
        nc.vector.tensor_tensor(de(0, *piece(0)), bagged(0, *piece(0)), wc_sb[:, :PIECE], MULT)
        make_u(1)
        scatter(0, *piece(0))
        gather_u_on_scalar(1, *piece(0))
        quantize(nc, w_bf_23[:], w_codes[:, 2 * P :], w_scales[:, 2 * P :], E4M3)
        make_u(2)
        make_u(3)
        gather_u(0, PIECE, PIECE + WIDE)
        gather_u(0, PIECE + WIDE, C)
        weigh(0, PIECE, PIECE + WIDE)
        gather_u(0, *piece(0))
        weigh(0, PIECE + WIDE, C)
        gather_u(1, PIECE, PIECE + WIDE)
        gather_u(1, PIECE + WIDE, C)
        weigh(1, 0, PIECE + WIDE)
        weigh(1, PIECE + WIDE, C)
        for k in range(1, 8):
            scatter(k // 4, *piece(k % 4))
            if k % 4 == 3:
                store(k // 4)
            if k < 5:
                gather_u_on_scalar(3, *piece(k - 1))
            else:
                gather_u_on_scalar(2, *piece((k - 6) % 4))
        for q in range(4):
            scatter_on_vector(3, *piece(q))
            gather_table(3, *piece(q))
        store(3)
        scatter_on_vector(2, *piece(3))
        gather_table(0, *piece(0))
        weigh(2, *piece(0))
        scatter(2, *piece(0))
        gather_u_on_scalar(2, *piece(2))
        gather_table(0, PIECE, C)
        weigh(2, *piece(1))
        scatter(2, *piece(1))
        gather_table(1, 0, HALF)
        gather_table(1, *piece(2))
        weigh(2, *piece(2))
        scatter(2, *piece(2))
        store(2)
        gather_table(1, *piece(3))
        gather_table(2, 0, HALF)
        gather_table(2, *piece(2))
        gather_table(2, *piece(3))
        sum_on_vector(0, 4)
        sum_on_vector(4, 2)
        sum_on_vector(6, 2)

        dw_rows = keep.tile([P, BLOCKS * SQUARE], F32, align_bytes=64)
        nc.vector.transpose(dw_rows[:], dw_cols[:])
        nc.sync.dma_start(
            out=out_1.rearrange("o (b q i) -> (o q) b i", q=P // SQUARE, i=SQUARE),
            in_=dw_rows[0:P:SQUARE, :].rearrange("q (b i) -> q b i", i=SQUARE),
        )
